import numpy as np, ml_dtypes
CORES = [5,29,101,125,133,157,229,253]
N = 8
BF = ml_dtypes.bfloat16
def gentries(a):
    return np.ascontiguousarray(a.reshape(8, 16, -1).transpose(0, 2, 1)).reshape(8, -1)
def gtable(e):
    e = np.asarray(e); return np.ascontiguousarray(e.reshape(8, -1, 16).transpose(0, 2, 1)).reshape(128, -1).astype(np.int32)
V, H, Q, ST = 3072, 512, 3, 2
MOST, SAME = 2 ** (Q + 1) - 1, 3
def sizes(w):
    return 1 + np.minimum((w * (V - 1 - H)) // np.add.reduce(w, axis=-1, keepdims=True), MOST - 1)
def usual(rng):
    return sizes((1000 * rng.standard_exponential((N, 8, H))).astype(np.int64) + 1)
def forest(rng, n, stale, last):
    pool = rng.permutation(V - 1) + 1; r = np.zeros((Q + 1, H), np.int64)
    if last: pool = np.concatenate([pool[pool == V - 1], pool[pool != V - 1]])
    c = rng.integers(0, V, (Q, V)) if stale else np.zeros((Q, V), np.int64)
    high = pool[:0]; at = 0
    for o in range(Q, -1, -1):
        hs = np.nonzero((n >> o) & 1)[0]
        a = pool[at:at + hs.size]; at += hs.size; r[o, hs] = a
        k = pool[at:at + high.size]; at += high.size
        if o < Q: c[o, high] = k
        high = np.concatenate([high, a, k])
    return r, c
def forests(rng, n, stale=False, last=False):
    p = [[forest(rng, n[q, g], stale, last) for g in range(8)] for q in range(N)]
    return np.array([[x[0] for x in a] for a in p]), np.array([[x[1] for x in a] for a in p])
def records(rng):
    v = rng.integers(0, 256, (N, 8, 16, V))
    lev = np.clip(rng.integers(0, 256, (N, 8, 1, V)) + rng.integers(-40, 41, (N, 8, 16, V)), 0, 255)
    return np.where(rng.random((N, 8, 1, V)) < 0.5, v, lev)
def pack(v, r, c):
    return {"rec": np.ascontiguousarray(v.reshape(N, 128, V)).astype(np.float32).astype(BF), "rt": np.stack([gtable(a.reshape(8, -1)) for a in r]),
            "ch": np.ascontiguousarray(c.reshape(N, 8, Q * V)).astype(np.int32)}
def setup_inputs(rng):
    r, c = forests(rng, usual(rng)); return pack(records(rng), r, c)
def setup_inputs_alike(rng):
    n = usual(rng); n[:, 0] = 1; n[:, 2] = SAME
    for q in range(N):
        n[q, 4] = rng.permutation(2 ** (np.arange(H) % (Q + 1)))
        room = MOST - n[q, 6]; before = np.add.accumulate(room) - room
        n[q, 6] = n[q, 6] + np.clip(V - 1 - np.add.reduce(n[q, 6]) - before, 0, room)
        for g in (5, 7):
            more = 2 ** (1 + (q + g // 2) % Q) - 1; many = min(H, (V - 1 - H) // more)
            n[q, g] = rng.permutation(1 + more * (np.arange(H) < many).astype(np.int64))
    r, c = forests(rng, n, last=True); v = records(rng)
    for q in range(N):
        for g in (1, 3): v[q, g] = v[q, g][:, rng.integers(0, 8, V)]
    return pack(v, r, c)
def setup_inputs_ties(rng):
    r, c = forests(rng, usual(rng))
    base = np.array([1, 128, 254, 128, 1, 254, 128, 128])[rng.permutation(8)].reshape(1, 8, 1, 1)
    k = rng.choice(np.array([0, 7, 8, 9, 16]), (N, 8, 1, V)); low = rng.integers(0, 2, (N, 8, 1, V))
    up = np.argsort(rng.random((N, 8, 16, V), dtype=np.float32), axis=2) < k
    return pack(base + np.where(up, 1, -low), r, c)
def setup_inputs_tall(rng):
    n = np.ones((N, 8, H), np.int64)
    run = [np.full((V - 1 - H) // (MOST - 1), MOST), 2 ** Q + 1 - (np.arange(2 * ((V - 1 - H) // MOST)) & 1)]
    st = np.stack([rng.integers(1, H - run[g & 1].size + 1, N) for g in range(8)], axis=1)
    for q in range(N):
        for g in range(8): n[q, g, st[q, g]:st[q, g] + run[g & 1].size] = run[g & 1]
    r, c = forests(rng, n); v = rng.integers(100, 256, (N, 8, 16, V))
    for q in range(N):
        for g in range(8):
            k = np.arange(run[g & 1].size); h = st[q, g] + k
            o = np.where((k + (0 if g & 1 else int(rng.integers(0, 2)))) & 1 == 1, Q, 0)
            v[q, g][:, r[q, g, o, h]] = rng.integers(0, 100, (16, k.size))
            v[q, g][:, r[q, g, 0, 0]] = (np.arange(16) == rng.integers(0, 16)).astype(np.int64)
    return pack(v, r, c)
def setup_inputs_stale(rng):
    n = usual(rng); n[:, :, 0] = 1
    r, c = forests(rng, n, True); v = records(rng); v[..., 0] = 0
    for q in range(N):
        for g in range(8):
            t = (0, 1, H - 1, H, 4080, H // 2)[(q + g) % 6]
            v[q, g][:, r[q, g, 0, 0]] = rng.permutation(np.clip(t - 255 * np.arange(16), 0, 255))
    return pack(v, r, c)
def setup_inputs_spread(rng):
    r, c = forests(rng, sizes(np.exp2(12 * rng.random((N, 8, H))).astype(np.int64)))
    v = (np.exp2(8 * rng.random((N, 8, 1, V))) * rng.random((N, 8, 16, V))).astype(np.int64); u = rng.random((N, 8, 1, V))
    return pack(np.where(u < 0.0625, 0, np.where(u > 0.9375, 255, np.minimum(v, 255))), r, c)
def check_inputs(d):
    bad = []
    x = np.asarray(d["rec"]).astype(np.float32)
    if not np.all((x >= 0) & (x <= 255) & (x == np.floor(x))): bad.append("whole numbers from 0 to 255 in rec")
    for k in ("rt", "ch"):
        if np.min(d[k]) < 0 or np.max(d[k]) > V - 1: bad.append("range of " + k)
    if "range of rt" in bad or "range of ch" in bad: return bad
    empty, lack, twice = False, False, False
    for q in range(N):
        rr = gentries(d["rt"][q]).reshape(8, Q + 1, H); cc = np.asarray(d["ch"][q]).reshape(8, Q, V)
        for g in range(8):
            if not np.all(np.max(rr[g], axis=0) > 0): empty = True
            high = np.zeros(0, np.int64)
            for o in range(Q, -1, -1):
                a = rr[g, o][rr[g, o] > 0].astype(np.int64); k = cc[g, o][high].astype(np.int64) if o < Q else high
                if np.any(k == 0): lack = True
                high = np.concatenate([high, a, k])
            if np.unique(high).size != high.size: twice = True
    if empty: bad.append("every heap has a root")
    if lack: bad.append("every child that counts is a node")
    if twice: bad.append("no node stands twice")
    return bad
def pick(v, ix):
    return np.take_along_axis(v, ix[:, :, None, :], 3)
def beats(x, y):
    return np.add.reduce((x < y).astype(np.int64), axis=2) >= 9
def reference(rec, rt, ch):
    v = rec.astype(np.float32).astype(np.int64).reshape(N, 8, 16, V); kid = ch.astype(np.int64).reshape(N, 8, Q, V)
    root = np.stack([gentries(a) for a in rt]).astype(np.int64).reshape(N, 8, Q + 1, H)
    for step in range(ST):
        m = root[:, :, 0].copy(); order = np.zeros_like(m)
        for o in range(1, Q + 1):
            a = root[:, :, o]; w = (a > 0) & ((m == 0) | beats(pick(v, a), pick(v, m)))
            m = np.where(w, a, m); order = np.where(w, o, order)
        for o in range(Q + 1): root[:, :, o] = np.where(order == o, 0, root[:, :, o])
        z = pick(v, m); got = np.roll(z, 1, axis=0)
        s = np.add.reduce(got[:, :, :, 0], axis=2) & (H - 1)
        np.put_along_axis(v, m[:, :, None, :], (z + got) >> 1, 3)
        j = (np.arange(H) + s[:, :, None]) & (H - 1)
        mj = np.take_along_axis(m, j, 2); oj = np.take_along_axis(order, j, 2)
        c = m
        for o in range(Q):
            a = root[:, :, o].copy(); b = np.where(o < oj, np.take_along_axis(kid[:, :, o], mj, 2), 0)
            n = (a > 0).astype(np.int64) + (b > 0) + (c > 0); link = n >= 2
            x = np.where((n == 2) & (a > 0), a, b); y = np.where(c > 0, c, b)
            win = beats(pick(v, y), pick(v, x)); wn = np.where(win, y, x); ls = np.where(win, x, y)
            rl = pick(v, ls); new = rl + np.clip(pick(v, wn) - rl, -1, 1)
            i = np.nonzero(link)
            v[i[0], i[1], :, ls[i]] = new.transpose(0, 1, 3, 2)[i]
            kid[i[0], i[1], o, wn[i]] = ls[i]
            root[:, :, o] = np.where(n == 1, a + b + c, np.where(n == 3, a, 0))
            c = np.where(link, wn, 0)
        root[:, :, Q] = np.where(root[:, :, Q] > 0, root[:, :, Q], c)
    return {"yrec": v.reshape(N, 128, V).astype(np.float32).astype(BF), "yrt": np.stack([gtable(a.reshape(8, -1)) for a in root]).astype(np.float32)}

@@ -1,0 +1,651 @@
+from concourse.bass import DstId, RemoteDMATransfer
+from concourse.mybir import AluOpType as ALU, ActivationFunctionType as ACT
+
+V, H = 3072, 512
+OFF = 34816.0
+MAGIC = 12582912.0
+F, B, I, U, HF = "float32", "bfloat16", "int32", "uint16", "float16"
+
+
+def _sb(n, d):
+    return ("sbuf", [128, n], d)
+
+
+SCRATCH = {
+    "pool": _sb(V + H, B), "chw": _sb(V, I), "rti": _sb(128, I), "sv": _sb(2, B),
+    "rw": _sb(4 * H, B), "xs": _sb(3 * H, B), "cmpa": _sb(H, B), "cmpb": _sb(H, B),
+    "e1": _sb(H, B), "e2": _sb(H, B), "mb": _sb(H, B), "sg": _sb(3 * H, B), "lc": _sb(2 * H, B),
+    "xyn": _sb(2 * H, B), "ln2": _sb(H, B), "kg": _sb(H, HF), "cq": _sb(H, B),
+    "z0": _sb(H, B), "z1": _sb(H, B), "w0": _sb(H, B), "w1": _sb(H, B),
+    "eo": _sb(64, B), "ei": _sb(64, B), "fo": _sb(16, B), "fi": _sb(16, B),
+    "he": _sb(32, B), "hf": _sb(16, B), "h0": _sb(H // 2, B), "h1": _sb(H // 2, B),
+    "pc": _sb(4, I), "pf": _sb(8, F), "t1": _sb(144, F), "bc": _sb(144, B), "bo": _sb(3 * 144, HF), "rm": _sb(4, F),
+    "id1": _sb(128, B), "idn": _sb(128, B), "id2": _sb(128, B), "idm": _sb(128, B), "idh": _sb(128, B), "id4": _sb(128, B),
+    "idf": _sb(128, F), "idg": _sb(128, F), "idk": _sb(128, F), "id16": _sb(128, HF), "c15": _sb(32, HF), "cb": _sb(32, B),
+    "blk": _sb(128, B), "blkn": _sb(128, B), "blki": _sb(128, B), "m2": _sb(256, B), "pp": _sb(256, HF),
+    "ali": _sb(128, F), "al": _sb(128, F), "dmi": _sb(96, F), "dm": _sb(96, F), "h2i": _sb(32, F), "h2": _sb(32, F),
+    "uci": _sb(4, F), "uc": _sb(4, F),
+    "r0": _sb(128, F), "r1": _sb(128, F), "r2": _sb(128, F), "r16": _sb(128, U), "e16": _sb(4, U),
+    "ml": _sb(32, F), "mt": _sb(32, F), "ml16": _sb(32, U), "m16": _sb(32, U),
+    "ne": _sb(128, F), "ge": _sb(96, F), "a": _sb(128, F), "ea": _sb(128, B), "eb": _sb(96, B),
+    "lk": _sb(96, F), "nl": _sb(128, F), "thr": _sb(96, F), "dnl": _sb(96, F), "odd": _sb(96, F), "fx": _sb(96, F),
+    "wl": _sb(96, F), "ao": _sb(96, F), "x16": _sb(96, U), "ta": _sb(96, F), "tb": _sb(96, F),
+    "y0": _sb(128, F), "y1": _sb(128, F), "y16": _sb(64, U), "q": _sb(32, F), "wn": _sb(32, F), "u": _sb(96, F),
+    "ls": _sb(96, F), "l16": _sb(96, U), "td": _sb(32, F), "o16": _sb(32, U),
+    "kw": _sb(96, F), "g16": _sb(144, HF), "si": _sb(4, I), "sj": _sb(4, I), "s16": _sb(4, U), "sf": _sb(2, F),
+    "lt": _sb(8, B), "tx": _sb(4, F), "ty": _sb(16, F), "tz": _sb(16, F),
+}
+for _k in range(8):
+    SCRATCH["b%d" % _k] = ("psum", [128, 512], F)
+SEMAPHORES = ["cv", "cs", "cp", "cg", "lrec", "lrt", "lsv", "lch", "sto", "stp", "ae", "a0", "af", "a1", "le", "l0", "lf", "l1"]
+MSG = (("e", "eo", "he", "ei", 32), ("0", "z0", "h0", "w0", H // 2), ("f", "fo", "hf", "fi", 16), ("1", "z1", "h1", "w1", H // 2))
+
+
+def helpers(src, dst, topo):
+    ok = [c for c in topo.cores_of(src) if c != src and topo.may_write(c, dst)]
+    near = [c for c in ok if topo.die(c) == topo.die(src)]
+    far = [c for c in ok if topo.die(c) != topo.die(src)]
+    return [near[0], far[0]]
+
+
+def bits(engs):
+    return sum(1 << e for e in engs)
+
+
+def hand_on(g, core, T, topo, src, dst, k):
+    rid, pid = topo.addr(dst, core)
+    n_in = len(topo.engines(src, core)) // 2
+    engs = topo.engines(core, dst)
+    for tag, _, mid, land, wd in MSG:
+        if tag == "f" and k == 1:
+            continue
+        g.wait_ge(T.sem["a" + tag], n_in)
+        g.remote_dma(T[land][:, k * wd:(k + 1) * wd], T[mid][:], T.sem["a" + tag], T.sem["l" + tag], pid, rid, bits(engs))
+    for tag, _, mid, land, wd in MSG:
+        if not (tag == "f" and k == 1):
+            g.wait_ge(T.sem["l" + tag], len(engs))
+
+
+def rank_program(g, core, T, topo):
+    cores = list(T.cores)
+    nr = len(cores)
+    rank = T.rank_of(core)
+    if rank is None:
+        for r in range(nr):
+            hs = helpers(cores[r], cores[(r + 1) % nr], topo)
+            if core in hs:
+                hand_on(g, core, T, topo, cores[r], cores[(r + 1) % nr], hs.index(core))
+        return
+    nxt, prv = cores[(rank + 1) % nr], cores[(rank - 1) % nr]
+    hs = helpers(core, nxt, topo)
+    n_arr = [len(topo.engines(c, core)) for c in helpers(prv, core, topo)]
+    Q = {"v": g.vector, "s": g.scalar, "p": g.tensor, "g": g, "y": g.sync}
+    ops = []
+
+    def A(name, a=0, b=None, step=None):
+        if b is None:
+            b = SCRATCH[name][1][1]
+        ap = T[name][:, a:b] if step is None else T[name][:, a:b:step]
+        return (ap, [(name, a, b)])
+
+    def X(name, a, b, off, c, d):
+        return (T[name][:, a:b].indirect(T[off][:, c:d]), [(name, a, b)], [(off, c, d)])
+
+    def op(q, fn, rd, wr, sem=None, cnt=0):
+        r, w = [], []
+        for o in rd:
+            if isinstance(o, tuple):
+                r += o[1]
+                if len(o) > 2:
+                    r += o[2]
+        for o in wr:
+            w += o[1]
+            if len(o) > 2:
+                r += o[2]
+        ops.append((q, fn, r, w, sem, cnt))
+
+    def val(o):
+        return o[0] if isinstance(o, tuple) else o
+
+    def tt(out, a, b, alu):
+        op("v", lambda: g.vector.tensor_tensor(out[0], a[0], b[0], alu), [a, b], [out])
+
+    def ts(out, a, s1, o1, s2=None, o2=None):
+        if o2 is None:
+            op("v", lambda: g.vector.tensor_scalar(out[0], a[0], val(s1), None, o1), [a, s1], [out])
+        else:
+            op("v", lambda: g.vector.tensor_scalar(out[0], a[0], val(s1), val(s2), o1, o2), [a, s1, s2], [out])
+
+    def cp(out, a):
+        op("v", lambda: g.vector.tensor_copy(out[0], a[0]), [a], [out])
+
+    def ms(out, c):
+        op("v", lambda: g.vector.memset(out[0], c), [], [out])
+
+    def act(out, a, f=ACT.Copy, bias=None, scale=None):
+        kw = {}
+        if bias is not None:
+            kw["bias"] = val(bias)
+        if scale is not None:
+            kw["scale"] = val(scale)
+        op("s", lambda: g.scalar.activation(out[0], a[0], f, **kw), [a, bias, scale], [out])
+
+    def mm(out, l, r, st=True, sp=True):
+        op("p", lambda: g.tensor.matmul(out[0], l[0], r[0], st, sp), [l, r], [out])
+
+    def lin(out, terms, st=True, sp=True):
+        for k, (l, r) in enumerate(terms):
+            mm(out, A(l), r, st and k == 0, sp and k == len(terms) - 1)
+
+    def iota(out, pat, base, cm):
+        if SCRATCH[out[1][0][0]][2] == I:
+            op("g", lambda: g.iota(out[0], pat, base, cm), [], [out])
+        else:
+            op("g", lambda: g.iota(out[0], pat, base, cm, allow_small_or_imprecise_dtypes=True), [], [out])
+
+    def dma(q, pairs, rd, wr, sem):
+        def fn():
+            for o, i in pairs:
+                Q[q].dma_start(o, i).then_inc(T.sem[sem], 16)
+        op(q, fn, rd, wr, sem, 16 * len(pairs))
+
+    def send(k):
+        tag, src, mid, _, wd = MSG[k]
+        tr, tot = [], 0
+        for j, c in enumerate(hs[:1] if tag == "f" else hs):
+            e = topo.engines(core, c)
+            e = e[j * len(e) // 2:(j + 1) * len(e) // 2]
+            rid, pid = topo.addr(c, core)
+            tr.append(RemoteDMATransfer(dst_ids=[DstId(rid=rid, pnc=pid)], dma_engine_mask=bits(e), remote_sem=T.sem["a" + tag],
+                                        src=T[src][:, j * wd:(j + 1) * wd], dst=T[mid][:]))
+            tot += len(e)
+        op("g", lambda: g.remote_dma_fused(tr, local_sem=T.sem["l" + tag]), [A(src)], [], "l" + tag, tot)
+        op("x", None, [], [A(MSG[k][3])], "a" + tag, n_arr[0] if tag == "f" else sum(n_arr))
+
+    def count(bank, cmp, signs=False):
+        if signs:
+            mm(A(bank, 0, 32), A("id1"), A("cb"), True, False)
+        for i in range(16):
+            mm(A(bank, 0, 32), A("bc", 15 - i, 143 - i), A(cmp, i, H, 16), i == 0 and not signs, i == 15)
+
+    def blk(name, o, n=1):
+        return A(name, 32 * o, 32 * (o + n))
+
+    def big(name, o, a=0, b=H):
+        return A(name, H * o + a, H * o + b)
+
+    def roots(o, eng, half=None):
+        a, b = (0, 32) if half is None else (16 * half, 16 * half + 16)
+        f = cp if eng == "v" else act
+        f(big("rw", o, 16 * a, 16 * b), X("pool", 0, V, "r16", 32 * o + a, 32 * o + b))
+
+    def duel(o, cmp):
+        if o == 1:
+            tt(A(cmp), X("pool", 0, V, "r16", 32, 64), big("rw", 0), ALU.is_lt)
+        else:
+            tt(A(cmp), X("rw", 0, H * o, "ml16", 0, 32), big("rw", o), ALU.is_gt)
+        count("b7", cmp)
+
+    def crown(o):
+        tt(A("mt"), A("b7", 0, 32), blk("al", o), ALU.min)
+        tt(A("ml"), A("mt"), blk("al", 0) if o == 1 else A("ml"), ALU.max)
+        ts(A("ml16"), A("ml"), OFF, ALU.subtract)
+
+    def follow(o):
+        w = blk("ge", 2) if o == 3 else A("wn")
+        tt(w, A("ml"), blk("al", o), ALU.is_ge)
+        tt(A("q"), w, A("td"), ALU.mult)
+        tt(blk("y0", 0), A("q"), blk("r0", 0) if o == 1 else blk("y0", 0), ALU.add)
+        if o < 3:
+            tt(A("td"), blk("r0", o + 1), blk("y0", 0), ALU.subtract)
+
+    def children():
+        ts(A("kg"), X("chw", 0, V, "m16", 0, 32), 1536.0, ALU.subtract)
+
+    def wrap_children(rest):
+        for o in range(3):
+            bank = rest if o else "b4"
+            mm(blk(bank, o), A("id16"), A("c15"), True, False)
+            for i in range(16):
+                mm(blk(bank, o), A("bo", 144 * o + 15 - i, 144 * o + 143 - i), A("kg", i, H, 16), False, i == 15)
+
+    def halve_open(t):
+        lin(A("b1"), [("id1", A("cq")), ("idh", A("z%d" % t))], True, False)
+        mm(A("b2"), A("idh"), A("z%d" % t), True, False)
+
+    def halve_p(t):
+        mm(A("b2"), A("idh"), A("w%d" % t), False, True)
+        mm(A("b1"), A("idh"), A("w%d" % t), False, True)
+
+    def halve():
+        ts(A("mb"), A("b1"), MAGIC, ALU.add, MAGIC, ALU.subtract)
+
+    def shift_a(s):
+        ts(A("si"), A("uc"), s, ALU.add)
+        ts(A("sj", 0, 3), A("si", 0, 3), 4, ALU.logical_shift_right, 31, ALU.bitwise_and)
+        ts(A("sj", 3, 4), A("si", 3, 4), 15, ALU.bitwise_and)
+        cp(A("s16", 0, 3), A("sj", 0, 3))
+        cp(A("sf", 0, 1), A("sj", 3, 4))
+        ts(A("pp"), A("m2"), A("sf", 0, 1), ALU.add, A("pf", 3, 4), ALU.is_equal)
+
+    def shift_v(orders):
+        for o in orders:
+            ts(A("g16", 48 * o, 48 * o + 48), X("kw", 32 * o, 32 * o + 32, "s16", 0, 3), 1536.0, ALU.subtract)
+
+    def shift_p(orders, less):
+        for o in orders:
+            bank = ("b3" if o else "b0") if less else "b5"
+            mm(blk(bank, o), A("id16"), A("c15"), True, False)
+            if less:
+                mm(blk(bank, o), A("idg"), blk("a", o), False, False)
+            mm(blk(bank, o), A("pp", 0, 128), A("g16", 48 * o, 48 * o + 32), False, False)
+            mm(blk(bank, o), A("pp", 128, 256), A("g16", 48 * o + 1, 48 * o + 33), False, True)
+
+    def structure(t):
+        def sums():
+            for o in range(3):
+                lin(blk("b7", o), [("id%d" % (1 << j), blk(e, j)) for j in range(o + 1) for e in ("ea", "eb")])
+        if t:
+            act(A("eb"), blk("b5", 0, 3), ACT.Sign)
+            tt(blk("tb", 0), blk("eb", 0), blk("b0", 0), ALU.mult)
+            lin(blk("b6", 0), [("idf", blk("a", 0)), ("idf", blk("tb", 0))])
+            sums()
+            halve_p(t)
+            cp(blk("x16", 0), blk("b6", 0))
+            act(big("xs", 0), X("pool", 0, V, "x16", 0, 32))
+        else:
+            ts(blk("eb", 1, 2), blk("b5", 1, 2), 0.0, ALU.is_gt)
+            sums()
+            shift_p((1, 2), True)
+            lin(blk("b6", 0), [("idf", blk("a", 0)), ("idf", blk("tb", 0))])
+        for o in range(3):
+            ts(blk("lk", o), blk("b7", o), float((2 << o) - 1), ALU.is_ge)
+        tt(blk("ta", 1, 2), blk("eb", 1, 2), blk("lk", 0, 2), ALU.mult)
+        tt(blk("tb", 1, 2), blk("ta", 1, 2), blk("b3", 1, 2), ALU.mult)
+        lin(blk("b6", 1, 2), [("idf", blk("a", 1, 2)), ("idf", blk("tb", 1, 2))])
+        if t:
+            halve()
+        else:
+            halve_p(t)
+            kept()
+        lin(blk("b7", 0, 3), [("idf", A("dm")), ("idk", A("lk"))])
+        act(blk("nl", 0, 3), A("lk"), ACT.Identity, 1.0, -1.0)
+        act(A("thr"), A("lk"), ACT.Identity, 1048576.0 + 36864.0, -1048576.0)
+        cp(blk("x16", 1, 2), blk("b6", 1, 2))
+        act(big("xs", 1), X("pool", 0, V, "x16", 32, 64))
+        act(big("xs", 2), X("pool", 0, V, "x16", 64, 96))
+        act(blk("nl", 3), blk("ea", 3), ACT.Identity, 1.0, -1.0)
+        act(A("dnl"), blk("b7", 0, 3))
+
+    def carries(t):
+        tt(A("ta"), A("lk"), blk("b6", 0, 3), ALU.mult)
+        tt(blk("tb", 0, 2), blk("nl", 0, 2), blk("b5", 1, 2), ALU.mult)
+        tt(A("q"), blk("y%d" % t, 0), blk("b6", 0), ALU.subtract)
+        lin(blk("b6", 3, 2), [("idf", blk("ta", 0, 2)), ("idf", blk("tb", 0, 2))])
+        mm(blk("b6", 5), A("idf"), blk("ta", 2))
+
+    def kept():
+        tt(blk("odd", 1, 2), blk("eb", 1, 2), blk("lk", 0, 2), ALU.is_equal)
+        tt(blk("ao", 0), blk("eb", 0), blk("a", 0), ALU.mult)
+        tt(blk("ao", 1, 2), blk("odd", 1, 2), blk("a", 1, 2), ALU.mult)
+
+    def root(t, o, n=1):
+        r = "r%d" % (t + 1)
+        tt(blk("ne", o, n), blk("nl", o, n), blk("y%d" % t, o, n), ALU.mult)
+        tt(blk(r, o, n), blk("ne", o, n), blk("ao", o, n) if o < 3 else blk("a", 3), ALU.add)
+        if t == 0:
+            cp(blk("r16", o, n), blk(r, o, n))
+
+    def pick():
+        tt(A("td"), A("wn"), A("h2"), ALU.add)
+        cp(A("o16"), A("td"))
+
+    def link(t, o):
+        y = "y%d" % t
+        tt(A("wn"), A("b0", 0, 32), blk("thr", o), ALU.is_ge)
+        if o == 2 and t == 1:
+            pick()
+            act(A("ln2"), X("xyn", 0, 2 * H, "o16", 0, 32))
+        tt(blk("u", o), A("wn"), A("q"), ALU.mult)
+        if o < 2 or t == 0:
+            tt(blk(y, o + 1), blk("u", o), blk("b6", 3 + o), ALU.add)
+        if o < 2:
+            cp(blk("y16", o), blk(y, o + 1))
+
+    def gap(t, o):
+        tt(A("q"), blk("y%d" % t, o), blk("b6", o), ALU.subtract)
+
+    def loser_p(t, o, n, bank):
+        lin(blk(bank, 8 + o, n), [("idf", blk("y%d" % t, o, n)), ("idg", blk("u", o, n))])
+
+    def loser(o, n, bank):
+        tt(blk("ls", o, n), blk("dnl", o, n), blk(bank, 8 + o, n), ALU.max)
+        cp(blk("l16", o, n), blk("ls", o, n))
+
+    def differ(o, early):
+        e = "e%d" % o
+        tt(A(e), X("pool", 0, V, "y16", 32 * (o - 1), 32 * o), big("xs", o), ALU.subtract)
+        ts(A("cmpa"), A(e), 0.0, ALU.is_lt)
+        if early:
+            moved_p(o - 1, True)
+        count("b0", "cmpa")
+
+    def moved_p(o, last):
+        x0, x1, x2, e1, e2 = big("xs", 0), big("xs", 1), big("xs", 2), A("e1"), A("e2")
+        d, l = (A("b2"), A("b3")) if o == 0 else (A("b1"), A("b4"))
+        if last:
+            mm(d, A("id2"), e2 if o else e1, False, True)
+            mm(l, A("idn"), e2 if o else e1, False, True)
+        elif o == 0:
+            lin(d, [("idn", x0), ("idn", A("mb")), ("id2", x1)], True, False)
+            lin(l, [("id1", x0), ("id1", A("mb")), ("idn", x1)], True, False)
+        else:
+            lin(d, [("idm", x1), ("idn", e1), ("id2", x2)], True, False)
+            lin(l, [("id2", x1), ("id1", e1), ("idn", x2)], True, False)
+
+    def moved_s(o):
+        act(big("sg", o), A("b1" if o else "b2"), ACT.Sign)
+        act(big("lc", o), A("b4" if o else "b3"))
+
+    def both_p(by, bx):
+        lin(A(by), [("id1", big("xs", 2)), ("id1", A("e2")), ("idn", big("sg", 2))])
+        lin(A(bx), [("id1", big("xs", 2)), ("id1", big("sg", 2))])
+
+    def both_s(by, bx):
+        act(A("xyn", 0, 2 * H, 2), A(by))
+        act(A("xyn", 1, 2 * H, 2), A(bx))
+
+    def put(o, a=0, b=32):
+        dst = X("pool", 0, V + H, "l16", 32 * o + a, 32 * o + b)
+        if o < 2:
+            tt(dst, big("lc", o, 16 * a, 16 * b), big("sg", o, 16 * a, 16 * b), ALU.add)
+        else:
+            cp(dst, A("ln2", 16 * a, 16 * b))
+
+    def meld_start(t):
+        tt(A("cmpa"), big("xs", 0), A("b2"), ALU.is_gt)
+        count("b0", "cmpa")
+        carries(t)
+        if t == 0:
+            halve()
+        link(t, 0)
+
+    dma("y", [(T.pool[:, 0:V], T.rec[:])], [], [A("pool", 0, V)], "lrec")
+    dma("s", [(T.rti[:], T.rt[:])], [], [A("rti")], "lrt")
+    dma("s", [(T.sv[:], T.rec[:, 0:2])], [], [A("sv")], "lsv")
+    iota(A("pc", 0, 1), [[0, 1]], 0, 1)
+    iota(A("t1"), [[1, 144]], 0, 0)
+    iota(A("ali"), [[16, 128]], int(OFF), 0)
+    iota(A("blki"), [[1, 8], [0, 16]], 0, 0)
+    iota(A("dmi"), [[0, 3], [16, 32]], V, 0)
+    iota(A("h2i"), [[32, 32]], 0, 0)
+    iota(A("uci"), [[256, 4]], 0, 0)
+    iota(A("m2"), [[-16, 2], [32, 8], [1, 16]], 0, 0)
+    iota(A("chw", 2048, V), [[0, 1024]], 0, 0)
+    ms(A("chw", 0, 1024), 0)
+    ts(A("pc", 1, 2), A("pc", 0, 1), 15, ALU.bitwise_and)
+    ts(A("pc", 2, 3), A("pc", 0, 1), 4, ALU.logical_shift_right)
+    cp(A("pf", 0, 3), A("pc", 0, 3))
+    ts(A("pf", 4, 5), A("pf", 2, 3), 16.0, ALU.mult, 15.0, ALU.add)
+    ts(A("pf", 3, 4), A("pf", 2, 3), 32.0, ALU.mult, A("pf", 1, 2), ALU.add)
+    ts(A("id1"), A("t1", 0, 128), A("pf", 0, 1), ALU.is_equal)
+    ts(A("bc"), A("t1"), A("pf", 4, 5), ALU.is_equal, 4096.0, ALU.mult)
+    ts(A("blk"), A("blki"), A("pf", 2, 3), ALU.is_equal)
+    act(A("al"), A("ali"), ACT.Identity, A("pf", 1, 2))
+    act(A("pf", 5, 6), A("pf", 1, 2), ACT.Copy, None, 2.0)
+    act(A("pf", 6, 7), A("pf", 1, 2), ACT.Copy, None, 16.0)
+    for name, c in (("idf", 1.0), ("idg", -1.0), ("idh", 0.5), ("idn", -1.0), ("id2", 2.0), ("idm", -2.0), ("id4", 4.0),
+                    ("idk", -8192.0)):
+        act(A(name), A("id1"), ACT.Copy, None, c)
+    act(A("blkn"), A("blk"), ACT.Copy, None, -1.0)
+    act(A("dm"), A("dmi"), ACT.Identity, A("pf", 1, 2))
+    act(A("h2"), A("h2i"), ACT.Identity, A("pf", 5, 6))
+    act(A("uc", 0, 3), A("uci", 0, 3), ACT.Identity, A("pf", 6, 7))
+    act(A("uc", 3, 4), A("uci", 0, 1))
+    act(A("cb"), A("h2i"), ACT.Identity, 30720.0, 0.0)
+    ms(A("chw", 1024, 2048), 0)
+    cp(A("r16"), A("rti"))
+    cp(A("e16"), A("rti", 0, 128, 32))
+    cp(A("r0"), A("rti"))
+    dma("y", [(T.chw[16 * k:16 * k + 3, :], T.ch[k]) for k in range(8)], [], [A("chw")], "lch")
+    ts(A("rm", 0, 3), A("t1", 0, 3), A("pf", 1, 2), ALU.is_equal)
+    for o in range(3):
+        ts(A("bo", 144 * o, 144 * o + 144), A("t1"), A("pf", 4, 5), ALU.is_equal, A("rm", o, o + 1), ALU.mult)
+    tt(A("td"), blk("r0", 1), blk("r0", 0), ALU.subtract)
+    ms(A("pool", 0, 1), 256.0)
+
+    act(A("eo"), X("pool", 0, V, "e16", 0, 4))
+    send(0)
+    roots(0, "v", 0)
+    roots(0, "s", 1)
+    duel(1, "cmpa")
+    roots(2, "s")
+    roots(1, "s")
+    roots(3, "s")
+    ms(A("cq"), -0.25)
+    cp(A("id16"), A("id1"))
+    ts(A("c15"), A("t1", 0, 32), 0.0, ALU.mult, 1536.0, ALU.add)
+    crown(1)
+    duel(2, "cmpb")
+    follow(1)
+    crown(2)
+    duel(3, "cmpa")
+    follow(2)
+    crown(3)
+    cp(A("z0", 0, 256), X("rw", 0, 4 * H, "ml16", 0, 16))
+    act(A("z0", 256, H), X("rw", 0, 4 * H, "ml16", 16, 32))
+    send(1)
+    act(A("tx"), A("ei", 0, 64, 16), ACT.Identity, -0.5)
+    act(A("lt", 0, 3), A("ei", 16, 64, 16), ACT.Sign, A("tx", 0, 1), -1.0)
+    act(A("lt", 3, 5), A("ei", 32, 64, 16), ACT.Sign, A("tx", 1, 2), -1.0)
+    act(A("lt", 5, 6), A("ei", 48, 49), ACT.Sign, A("tx", 2, 3), -1.0)
+    follow(3)
+    cp(A("m16"), blk("y0", 0))
+    children()
+    for o in range(2):
+        tt(blk("ge", o), A("ml"), blk("al", o + 1), ALU.is_ge)
+    for o in range(1, 4):
+        tt(blk("ne", o), A("ml"), blk("al", o), ALU.not_equal)
+    tt(blk("a", 0), blk("r0", 0), blk("ge", 0), ALU.mult)
+    tt(blk("a", 1, 3), blk("r0", 1, 3), blk("ne", 1, 3), ALU.mult)
+    mm(A("b3", 0, 3), A("blk"), A("lt", 0, 3))
+    mm(A("b3", 3, 4), A("blk"), A("ei", 0, 1))
+    lin(A("b3", 4, 6), [("blk", A("lt", 3, 5)), ("blkn", A("lt", 1, 3))])
+    lin(A("b3", 6, 7), [("blk", A("ei", 16, 17)), ("blkn", A("ei", 0, 1))])
+    mm(A("b3", 7, 8), A("blk"), A("lt", 5, 6))
+    mm(A("b3", 8, 10), A("blk"), A("ei", 32, 64, 16))
+    halve_open(0)
+    wrap_children("b7")
+
+    def col(n, k):
+        return A(n, k, k + 1)
+
+    def wins(out, a):
+        act(col("tz", 15), a, ACT.Sign, -1.0)
+        act(out, col("tz", 15), ACT.Relu)
+
+    def choose(out, w, yes, no):
+        act(col("tz", 14), no, ACT.Identity, yes, -1.0)
+        act(out, col("tz", 14), ACT.Identity, no, w)
+
+    act(A("ty", 0, 10), A("b3", 0, 10))
+    wins(col("tz", 0), col("ty", 0))
+    for k in range(3):
+        act(col("tz", 1 + k), col("ty", 4 + k), ACT.Identity, col("ty", 1 + k), col("tz", 0))
+    wins(col("tz", 4), col("tz", 1))
+    choose(col("tz", 5), col("tz", 4), col("ty", 7), col("tz", 2))
+    wins(col("tz", 7), col("tz", 5))
+    choose(col("tz", 6), col("tz", 4), col("ty", 8), col("tz", 3))
+    choose(col("tz", 8), col("tz", 7), col("ty", 9), col("tz", 6))
+    act(A("ea"), A("a"), ACT.Sign)
+    tt(blk("kw", 0), blk("b4", 0), blk("ge", 0), ALU.mult)
+    shift_a(col("tz", 8))
+    shift_v((0,))
+    shift_p((0,), False)
+    shift_p((0,), True)
+    tt(blk("kw", 1, 2), blk("b7", 1, 2), blk("ge", 1, 2), ALU.mult)
+    shift_v((1, 2))
+    ts(blk("eb", 0), blk("b5", 0), 0.0, ALU.is_gt)
+    shift_p((1, 2), False)
+    tt(blk("tb", 0), blk("eb", 0), blk("b0", 0), ALU.mult)
+    tt(A("td"), blk("tb", 0), blk("a", 0), ALU.add)
+    cp(blk("x16", 0), A("td"))
+    act(big("xs", 0), X("pool", 0, V, "x16", 0, 32))
+    structure(0)
+
+    meld_start(0)
+    root(0, 0, 2)
+    cp(X("pool", 0, V + H, "m16", 0, 32), A("mb"))
+    moved_p(0, False)
+    roots(0, "s")
+    roots(1, "s")
+    differ(1, False)
+    gap(0, 1)
+    lin(A("b1"), [("id1", big("rw", 0)), ("idn", big("rw", 1))])
+    act(A("cmpb"), A("b1"), ACT.Sign, -0.5)
+    moved_p(0, True)
+    count("b7", "cmpb", True)
+    link(0, 1)
+    root(0, 2)
+    roots(2, "s")
+    moved_s(0)
+    differ(2, False)
+    gap(0, 2)
+    crown(1)
+    moved_p(1, False)
+    duel(2, "cmpb")
+    link(0, 2)
+    root(0, 3)
+    roots(3, "s", 1)
+    roots(3, "v", 0)
+    act(big("sg", 2), A("e2"), ACT.Sign)
+    moved_p(1, True)
+    moved_s(1)
+    loser_p(0, 0, 3, "b0")
+    lin(blk("b0", 11, 3), [("idf", blk("y0", 1, 3)), ("idk", blk("nl", 0, 3))])
+    crown(2)
+    duel(3, "cmpa")
+    lin(blk("b6", 6), [("idf", blk("r1", o)) for o in range(4)], True, False)
+    pick()
+    loser(0, 3, "b0")
+    act(A("wl"), blk("b0", 11, 3))
+    crown(3)
+    cp(A("fo"), X("rw", 0, 4 * H, "ml16", 0, 1))
+    send(2)
+    act(A("z1"), X("rw", 0, 4 * H, "ml16", 0, 32))
+    send(3)
+
+    for o in range(4):
+        mm(blk("b7", o), A("idf"), A("ml"))
+    both_p("b2", "b3")
+    both_s("b2", "b3")
+    act(A("ln2"), X("xyn", 0, 2 * H, "o16", 0, 32))
+    put(0, 0, 16)
+    tt(A("ne"), A("al"), blk("b7", 0, 4), ALU.not_equal)
+    tt(A("a"), A("r1"), A("ne"), ALU.mult)
+    lin(blk("b6", 6), [("idg", blk("a", o)) for o in range(4)], False, True)
+    tt(A("ge"), blk("al", 1, 3), blk("b7", 0, 3), ALU.is_le)
+    put(0, 16, 32)
+    cp(A("m16"), blk("b6", 6))
+    children()
+    for o in range(3):
+        tt(blk("fx", o), blk("wl", o), blk("b6", 6), ALU.is_equal)
+    act(blk("y1", 0), blk("b6", 6))
+    wrap_children("b4")
+    put(1)
+    tt(A("ta"), blk("b4", 0, 3), A("ge"), ALU.mult)
+    lin(blk("b7", 0, 3), [("idf", A("ls")), ("idg", A("ta"))])
+    mm(A("b0", 0, 1), A("blk"), A("fi", 0, 1))
+    shift_a(A("b0", 0, 1))
+    tt(A("tb"), A("fx"), blk("b7", 0, 3), ALU.mult)
+    lin(blk("b7", 0, 3), [("idf", A("ta")), ("idf", A("tb"))])
+    act(A("kw"), blk("b7", 0, 3))
+    act(A("ea"), A("a"), ACT.Sign)
+    halve_open(1)
+    put(2, 0, 16)
+    shift_v((0, 1, 2))
+    shift_p((0, 1, 2), False)
+    shift_p((0, 1, 2), True)
+    put(2, 16, 32)
+    structure(1)
+    meld_start(1)
+    loser_p(1, 0, 1, "b6")
+    cp(X("pool", 0, V + H, "m16", 0, 32), A("mb"))
+    moved_p(0, False)
+    differ(1, True)
+    moved_s(0)
+    moved_p(1, False)
+    gap(1, 1)
+    loser(0, 1, "b6")
+    kept()
+    link(1, 1)
+    loser_p(1, 1, 1, "b6")
+    differ(2, True)
+    act(A("pool", 0, 1), A("sv", 0, 1))
+    act(big("sg", 2), A("e2"), ACT.Sign)
+    both_p("b5", "b7")
+    moved_s(1)
+    both_s("b5", "b7")
+    gap(1, 2)
+    loser(1, 1, "b6")
+    put(0)
+    link(1, 2)
+    loser_p(1, 2, 1, "b6")
+    put(1)
+    loser(2, 1, "b6")
+    put(2)
+    dma("y", [(T.yrec[:], T.pool[:, 0:V])], [A("pool", 0, V)], [], "sto")
+    tt(blk("y1", 3), blk("u", 2), blk("b6", 5), ALU.add)
+    root(1, 0, 3)
+    root(1, 3)
+    dma("s", [(T.yrt[:], T.r2[:])], [A("r2")], [], "stp")
+
+    seen = {}
+    clock = {q: {} for q in Q}
+    done, waits, need = [], [], set()
+    for k, (q, fn, rd, wr, sem, cnt) in enumerate(ops):
+        dep = {}
+        for regs, w in ((rd, False), (wr, True)):
+            for name, a, b in regs:
+                ps = SCRATCH[name][0] == "psum"
+                for a2, b2, j, w2 in seen.get(name, []):
+                    if ps:
+                        hit = ops[j][0] != q
+                    else:
+                        hit = a < b2 and a2 < b and (w or w2)
+                    if hit:
+                        key = ops[j][4] or ops[j][0]
+                        dep[key] = max(dep.get(key, -1), j)
+        wl = []
+        if q != "x":
+            for key, j in sorted(dep.items(), key=lambda e: -e[1]):
+                if clock[q].get(key, -1) < j:
+                    wl.append(j)
+                    need.add(j)
+                    for k2, j2 in done[j].items():
+                        clock[q][k2] = max(clock[q].get(k2, -1), j2)
+        waits.append(wl)
+        d = dict(clock[q]) if q != "x" else {}
+        d[sem or q] = k
+        done.append(d)
+        for name, a, b in rd:
+            seen.setdefault(name, []).append((a, b, k, False))
+        for name, a, b in wr:
+            seen.setdefault(name, []).append((a, b, k, True))
+    tick, n = {}, {}
+    for k, (q, fn, rd, wr, sem, cnt) in enumerate(ops):
+        if sem is not None:
+            tick[k] = (sem, cnt)
+        elif k in need:
+            n[q] = n.get(q, 0) + 1
+            tick[k] = ("c" + q, n[q])
+    for k, (q, fn, rd, wr, sem, cnt) in enumerate(ops):
+        for j in waits[k]:
+            Q[q].wait_ge(T.sem[tick[j][0]], tick[j][1])
+        if fn is not None:
+            ins = fn()
+            if sem is None and k in need:
+                ins.then_inc(T.sem["c" + q], 1)
+    for k, (q, fn, rd, wr, sem, cnt) in enumerate(ops):
+        if sem is not None and k not in need:
+            g.wait_ge(T.sem[sem], cnt)

@@ -2,9 +2,28 @@ from concourse.bass import DstId, RemoteDMATransfer
 from concourse.mybir import AluOpType as ALU, ActivationFunctionType as ACT
 
 V, H = 3072, 512
-OFF = 34816.0
+P0 = 32 + 7 * H + 16
+UB = (P0 + V + 2 * H, 0)
+LOS = (P0 - 16 - H, P0 + V, P0 + V + H)
+MID = (1520.0, 2048.0, 2048.0)
+C = 2048.0
+K = 16384.0
 MAGIC = 12582912.0
 F, B, I, U, HF = "float32", "bfloat16", "int32", "uint16", "float16"
+OPT = {"cmp0": "vv", "c12": "vv", "duel1": "vv", "pieces": (4, 2, 2, 2, 2, 2, 2, 1), "sc": 3.0, "ga": 1.4, "lat": (7.3, 5.7, 4.8, 5.5),
+       "zs": (16, 16), "lt": "vs", "fo": "s", "cut": (((0, 1), (1, 2)), ((0, 1), (1, 2))),
+       "wake": 0.11, "turns": 2, "rounds": 8, "damp": 0.3, "fill": False, "xs": (16, 0), "cy": 0.92, "waw": True,
+       "wb": (("b6", "b4", "b5"), ("b6", "b1", "b3"))}
+ORDER = []
+
+
+EYE = (("id1", 1.0), ("idn", -1.0), ("idh", 0.5), ("idi", -0.5), ("idm", -2.0), ("idq", -4.0), ("idk", K / 2), ("idb", 33 / 128),
+       ("idl", -K), ("idj", C / 2), ("idu", -C / 2))
+EYF = (("idf", 1.0), ("idg", -1.0))
+ALIAS = {"z0": ("pool", LOS[1], H), "cmpb": ("pool", LOS[2], H)}
+ALIAS.update({"lo%d" % o: ("pool", LOS[o], H) for o in range(3)})
+ALIAS.update({e[0]: ("eye", 128 * k, 128) for k, e in enumerate(EYE)})
+ALIAS.update({e[0]: ("eyf", 128 * k, 128) for k, e in enumerate(EYF)})
 
 
 def _sb(n, d):
@@ -12,33 +31,36 @@ def _sb(n, d):
 
 
 SCRATCH = {
-    "pool": _sb(V + H, B), "chw": _sb(V, I), "rti": _sb(128, I), "sv": _sb(2, B),
-    "rw": _sb(4 * H, B), "xs": _sb(3 * H, B), "cmpa": _sb(H, B), "cmpb": _sb(H, B),
-    "e1": _sb(H, B), "e2": _sb(H, B), "mb": _sb(H, B), "sg": _sb(3 * H, B), "lc": _sb(2 * H, B),
-    "xyn": _sb(2 * H, B), "ln2": _sb(H, B), "kg": _sb(H, HF), "cq": _sb(H, B),
-    "z0": _sb(H, B), "z1": _sb(H, B), "w0": _sb(H, B), "w1": _sb(H, B),
-    "eo": _sb(64, B), "ei": _sb(64, B), "fo": _sb(16, B), "fi": _sb(16, B),
-    "he": _sb(32, B), "hf": _sb(16, B), "h0": _sb(H // 2, B), "h1": _sb(H // 2, B),
-    "pc": _sb(4, I), "pf": _sb(8, F), "t1": _sb(144, F), "bc": _sb(144, B), "bo": _sb(3 * 144, HF), "rm": _sb(4, F),
-    "id1": _sb(128, B), "idn": _sb(128, B), "id2": _sb(128, B), "idm": _sb(128, B), "idh": _sb(128, B), "id4": _sb(128, B),
-    "idf": _sb(128, F), "idg": _sb(128, F), "idk": _sb(128, F), "id16": _sb(128, HF), "c15": _sb(32, HF), "cb": _sb(32, B),
-    "blk": _sb(128, B), "blkn": _sb(128, B), "blki": _sb(128, B), "m2": _sb(256, B), "pp": _sb(256, HF),
-    "ali": _sb(128, F), "al": _sb(128, F), "dmi": _sb(96, F), "dm": _sb(96, F), "h2i": _sb(32, F), "h2": _sb(32, F),
-    "uci": _sb(4, F), "uc": _sb(4, F),
-    "r0": _sb(128, F), "r1": _sb(128, F), "r2": _sb(128, F), "r16": _sb(128, U), "e16": _sb(4, U),
-    "ml": _sb(32, F), "mt": _sb(32, F), "ml16": _sb(32, U), "m16": _sb(32, U),
-    "ne": _sb(128, F), "ge": _sb(96, F), "a": _sb(128, F), "ea": _sb(128, B), "eb": _sb(96, B),
-    "lk": _sb(96, F), "nl": _sb(128, F), "thr": _sb(96, F), "dnl": _sb(96, F), "odd": _sb(96, F), "fx": _sb(96, F),
-    "wl": _sb(96, F), "ao": _sb(96, F), "x16": _sb(96, U), "ta": _sb(96, F), "tb": _sb(96, F),
-    "y0": _sb(128, F), "y1": _sb(128, F), "y16": _sb(64, U), "q": _sb(32, F), "wn": _sb(32, F), "u": _sb(96, F),
-    "ls": _sb(96, F), "l16": _sb(96, U), "td": _sb(32, F), "o16": _sb(32, U),
-    "kw": _sb(96, F), "g16": _sb(144, HF), "si": _sb(4, I), "sj": _sb(4, I), "s16": _sb(4, U), "sf": _sb(2, F),
-    "lt": _sb(8, B), "tx": _sb(4, F), "ty": _sb(16, F), "tz": _sb(16, F),
+    "pool": _sb(UB[0] + 32 + 12 * H, B), "outp": _sb(V + H, B), "v1": _sb(6 * H, B), "chw": _sb(V, I), "rti": _sb(128, I),
+    "y3": _sb(H, B), "kx": _sb(96, F), "gx": _sb(144, HF), "alp": _sb(96, F), "lp": _sb(96, F), "cm": _sb(96, B), "cp5": _sb(96, HF),
+    "cf": _sb(96, B), "qs": _sb(64, B), "vq": _sb(64, HF), "dmi": _sb(96, F), "ri": _sb(128, F), "te": _sb(96, B),
+    "uq": _sb(32, B), "er": _sb(128, B),
+    "cmpa": _sb(H, B), "sg": _sb(2 * H, B), "lc": _sb(2 * H, B),
+    "dw": _sb(2 * H, B), "ln": _sb(H, B), "kg": _sb(H, HF), "idw": _sb(128, HF),
+    "z1": _sb(H, B), "w0": _sb(H, B), "w1": _sb(H, B),
+    "eo": _sb(64, B), "ei": _sb(64, B), "fo": _sb(64, B), "fi": _sb(64, B),
+    "he": _sb(32, B), "hf": _sb(32, B), "h0": _sb(H // 2, B), "h1": _sb(H // 2, B),
+    "pc": _sb(4, I), "pf": _sb(8, F), "t1": _sb(144, F), "bc": _sb(144, B), "bd": _sb(144, B), "bo": _sb(3 * 144, HF),
+    "rm": _sb(4, F), "eye": _sb(128 * len(EYE), B), "eyf": _sb(128 * len(EYF), F),
+    "th": _sb(128, F), "wb": _sb(128, HF), "jc": _sb(32, F), "hi": _sb(128, F), "f16": _sb(4, U),
+    "cl": _sb(128, B), "one": _sb(96, B), "c15": _sb(96, HF), "j2": _sb(32, HF), "csh": _sb(16, HF),
+    "blk": _sb(128, B), "blki": _sb(128, B), "m2": _sb(256, B), "pp": _sb(256, HF),
+    "ali": _sb(128, F), "al": _sb(128, F), "xp": _sb(96, F), "cvi": _sb(12, F), "lui": _sb(64, F), "lut": _sb(64, F),
+    "r2": _sb(128, F), "rz": _sb(128, F), "r16": _sb(128, U), "e16": _sb(4, U), "ml16": _sb(96, U), "m16": _sb(64, U),
+    "sd": _sb(96, B), "sm": _sb(96, B), "ng": _sb(96, B), "nh": _sb(32, B), "ce": _sb(96, HF), "u3": _sb(32, F),
+    "ad": _sb(224, F), "ea": _sb(128, B), "eb": _sb(96, B), "bz": _sb(96, F), "nk0": _sb(128, B), "nk1": _sb(128, B),
+    "mm": _sb(192, HF), "ic": _sb(128, B), "fp": _sb(128, F), "xi": _sb(96, HF), "ao": _sb(128, HF),
+    "y0": _sb(64, F), "y1": _sb(64, F), "u0": _sb(96, F), "u1": _sb(96, F), "cc": _sb(128, HF),
+    "xt": _sb(96, F), "x16": _sb(96, U), "y16": _sb(96, U), "rv": _sb(32, F),
+    "p16": _sb(128, U), "l16": _sb(192, U), "fx": _sb(96, B), "alt": _sb(96, F),
+    "kw": _sb(96, F), "g16": _sb(144, HF), "sa": _sb(16, F), "s16": _sb(16, U), "si": _sb(16, I), "sj": _sb(16, I),
+    "lt": _sb(8, B), "lu": _sb(8, B), "lf": _sb(24, F), "t16": _sb(2, U), "q16": _sb(16, U),
 }
 for _k in range(8):
     SCRATCH["b%d" % _k] = ("psum", [128, 512], F)
-SEMAPHORES = ["cv", "cs", "cp", "cg", "lrec", "lrt", "lsv", "lch", "sto", "stp", "ae", "a0", "af", "a1", "le", "l0", "lf", "l1"]
-MSG = (("e", "eo", "he", "ei", 32), ("0", "z0", "h0", "w0", H // 2), ("f", "fo", "hf", "fi", 16), ("1", "z1", "h1", "w1", H // 2))
+SEMAPHORES = ["cv", "cs", "cp", "cg", "lrec", "lrt", "lch", "lout", "sto", "stp", "ae", "a0", "af", "a1", "le", "l0", "lf", "l1"]
+MSG = (("e", "eo", "he", "ei", 32), ("0", "z0", "h0", "w0", H // 2), ("f", "fo", "hf", "fi", 32), ("1", "z1", "h1", "w1", H // 2))
+WIDTH = {F: 4, I: 4, B: 2, U: 2, HF: 2}
 
 
 def helpers(src, dst, topo):
@@ -57,13 +79,10 @@ def hand_on(g, core, T, topo, src, dst, k):
     n_in = len(topo.engines(src, core)) // 2
     engs = topo.engines(core, dst)
     for tag, _, mid, land, wd in MSG:
-        if tag == "f" and k == 1:
-            continue
         g.wait_ge(T.sem["a" + tag], n_in)
         g.remote_dma(T[land][:, k * wd:(k + 1) * wd], T[mid][:], T.sem["a" + tag], T.sem["l" + tag], pid, rid, bits(engs))
     for tag, _, mid, land, wd in MSG:
-        if not (tag == "f" and k == 1):
-            g.wait_ge(T.sem["l" + tag], len(engs))
+        g.wait_ge(T.sem["l" + tag], len(engs))
 
 
 def rank_program(g, core, T, topo):
@@ -81,46 +100,61 @@ def rank_program(g, core, T, topo):
     n_arr = [len(topo.engines(c, core)) for c in helpers(prv, core, topo)]
     Q = {"v": g.vector, "s": g.scalar, "p": g.tensor, "g": g, "y": g.sync}
     ops = []
+    last = {}
 
     def A(name, a=0, b=None, step=None):
+        if name in ALIAS:
+            name, a, b = ALIAS[name][0], ALIAS[name][1] + a, ALIAS[name][1] + (ALIAS[name][2] if b is None else b)
         if b is None:
             b = SCRATCH[name][1][1]
         ap = T[name][:, a:b] if step is None else T[name][:, a:b:step]
-        return (ap, [(name, a, b)])
+        return (ap, [(name, a, b, step)], len(range(a, b, step or 1)), None)
 
     def X(name, a, b, off, c, d):
-        return (T[name][:, a:b].indirect(T[off][:, c:d]), [(name, a, b)], [(off, c, d)])
+        return (T[name][:, a:b].indirect(T[off][:, c:d]), [(name, a, b, None)], 16 * (d - c), [(off, c, d, None)])
 
-    def op(q, fn, rd, wr, sem=None, cnt=0):
+    def op(q, fn, rd, wr, busy, sem=None, cnt=0, done=None, after=()):
         r, w = [], []
         for o in rd:
             if isinstance(o, tuple):
-                r += o[1]
-                if len(o) > 2:
-                    r += o[2]
+                r += o[1] + (o[3] or [])
         for o in wr:
             w += o[1]
-            if len(o) > 2:
-                r += o[2]
-        ops.append((q, fn, r, w, sem, cnt))
+            r += o[3] or []
+        ops.append((q, fn, r, w, sem, cnt, busy, busy if done is None else done, list(after)))
 
     def val(o):
         return o[0] if isinstance(o, tuple) else o
 
+    def kind(o):
+        return SCRATCH[o[1][0][0]]
+
+    def lasts(out, a, b=None, fix=0.03):
+        n = out[2]
+        if out[3]:
+            return 0.05 + OPT["sc"] * n / 1000
+        if a is not None and a[3]:
+            return 0.06 + OPT["ga"] * n / 1000
+        if b is not None:
+            n *= 2 if kind(a)[0] == kind(b)[0] else 1
+        elif fix < 0.05 and WIDTH[kind(out)[2]] == 2 and (a is None or WIDTH[kind(a)[2]] == 2):
+            n /= 2
+        return fix + max(64, n) * OPT["cy"] / 1000
+
     def tt(out, a, b, alu):
-        op("v", lambda: g.vector.tensor_tensor(out[0], a[0], b[0], alu), [a, b], [out])
+        op("v", lambda: g.vector.tensor_tensor(out[0], a[0], b[0], alu), [a, b], [out], lasts(out, a, b))
 
     def ts(out, a, s1, o1, s2=None, o2=None):
         if o2 is None:
-            op("v", lambda: g.vector.tensor_scalar(out[0], a[0], val(s1), None, o1), [a, s1], [out])
+            op("v", lambda: g.vector.tensor_scalar(out[0], a[0], val(s1), None, o1), [a, s1], [out], lasts(out, a))
         else:
-            op("v", lambda: g.vector.tensor_scalar(out[0], a[0], val(s1), val(s2), o1, o2), [a, s1, s2], [out])
+            op("v", lambda: g.vector.tensor_scalar(out[0], a[0], val(s1), val(s2), o1, o2), [a, s1, s2], [out], lasts(out, a))
 
     def cp(out, a):
-        op("v", lambda: g.vector.tensor_copy(out[0], a[0]), [a], [out])
+        op("v", lambda: g.vector.tensor_copy(out[0], a[0]), [a], [out], lasts(out, a))
 
     def ms(out, c):
-        op("v", lambda: g.vector.memset(out[0], c), [], [out])
+        op("v", lambda: g.vector.memset(out[0], c), [], [out], lasts(out, None))
 
     def act(out, a, f=ACT.Copy, bias=None, scale=None):
         kw = {}
@@ -128,524 +162,570 @@ def rank_program(g, core, T, topo):
             kw["bias"] = val(bias)
         if scale is not None:
             kw["scale"] = val(scale)
-        op("s", lambda: g.scalar.activation(out[0], a[0], f, **kw), [a, bias, scale], [out])
+        op("s", lambda: g.scalar.activation(out[0], a[0], f, **kw), [a, bias, scale], [out], lasts(out, a, None, 0.05))
+
+    def fill(out, c):
+        act(out, A("t1", 0, out[2]), ACT.Identity, c, 0.0)
+
+    def run(calls):
+        bank = calls[0][0][1][0][0]
+        t = sum(max(64, c[2][2]) * (4 if kind(c[1])[2] == F else 1) * OPT["cy"] / 2000 for c in calls)
+
+        def fn():
+            return [g.tensor.matmul(o[0], l[0], r[0], st, sp) for o, l, r, st, sp in calls][-1]
+        op("p", fn, [c[1] for c in calls] + [c[2] for c in calls], [c[0] for c in calls], t, after=[last[bank]] if bank in last else [])
+        last[bank] = len(ops) - 1
 
     def mm(out, l, r, st=True, sp=True):
-        op("p", lambda: g.tensor.matmul(out[0], l[0], r[0], st, sp), [l, r], [out])
+        run([(out, l, r, st, sp)])
 
     def lin(out, terms, st=True, sp=True):
-        for k, (l, r) in enumerate(terms):
-            mm(out, A(l), r, st and k == 0, sp and k == len(terms) - 1)
+        calls = [(out, A(l), r, st and k == 0, sp and k == len(terms) - 1) for k, (l, r) in enumerate(terms)]
+        if out[2] < H:
+            run(calls)
+        else:
+            for c in calls:
+                run([c])
+
+    def wrap(out, name, step, src):
+        run([(out, A(name, step + 15 - i, step + 143 - i), A(src, i, H, 16), False, i == 15) for i in range(16)])
 
     def iota(out, pat, base, cm):
-        if SCRATCH[out[1][0][0]][2] == I:
-            op("g", lambda: g.iota(out[0], pat, base, cm), [], [out])
+        t = 0.13 + out[2] / 500
+        if kind(out)[2] == I:
+            op("g", lambda: g.iota(out[0], pat, base, cm), [], [out], t)
         else:
-            op("g", lambda: g.iota(out[0], pat, base, cm, allow_small_or_imprecise_dtypes=True), [], [out])
+            op("g", lambda: g.iota(out[0], pat, base, cm, allow_small_or_imprecise_dtypes=True), [], [out], t)
 
-    def dma(q, pairs, rd, wr, sem):
+    def dma(q, pairs, rd, wr, sem, t):
         def fn():
             for o, i in pairs:
                 Q[q].dma_start(o, i).then_inc(T.sem[sem], 16)
-        op(q, fn, rd, wr, sem, 16 * len(pairs))
+        op(q, fn, rd, wr, 0.05 * len(pairs), sem, 16 * len(pairs), t)
 
     def send(k):
         tag, src, mid, _, wd = MSG[k]
         tr, tot = [], 0
-        for j, c in enumerate(hs[:1] if tag == "f" else hs):
+        for j, c in enumerate(hs):
             e = topo.engines(core, c)
             e = e[j * len(e) // 2:(j + 1) * len(e) // 2]
             rid, pid = topo.addr(c, core)
             tr.append(RemoteDMATransfer(dst_ids=[DstId(rid=rid, pnc=pid)], dma_engine_mask=bits(e), remote_sem=T.sem["a" + tag],
-                                        src=T[src][:, j * wd:(j + 1) * wd], dst=T[mid][:]))
+                                        src=A(src, j * wd, (j + 1) * wd)[0], dst=T[mid][:]))
             tot += len(e)
-        op("g", lambda: g.remote_dma_fused(tr, local_sem=T.sem["l" + tag]), [A(src)], [], "l" + tag, tot)
-        op("x", None, [], [A(MSG[k][3])], "a" + tag, n_arr[0] if tag == "f" else sum(n_arr))
-
-    def count(bank, cmp, signs=False):
-        if signs:
-            mm(A(bank, 0, 32), A("id1"), A("cb"), True, False)
-        for i in range(16):
-            mm(A(bank, 0, 32), A("bc", 15 - i, 143 - i), A(cmp, i, H, 16), i == 0 and not signs, i == 15)
+        op("g", lambda: g.remote_dma_fused(tr, local_sem=T.sem["l" + tag]), [A(src)], [], 0.3, "l" + tag, tot, 2.0)
+        op("x", None, [], [A(MSG[k][3])], 0.0, "a" + tag, sum(n_arr), OPT["lat"][k], [len(ops) - 1])
 
     def blk(name, o, n=1):
         return A(name, 32 * o, 32 * (o + n))
 
-    def big(name, o, a=0, b=H):
-        return A(name, H * o + a, H * o + b)
+    def big(name, o):
+        return A(name, H * o, H * o + H)
 
-    def roots(o, eng, half=None):
-        a, b = (0, 32) if half is None else (16 * half, 16 * half + 16)
-        f = cp if eng == "v" else act
-        f(big("rw", o, 16 * a, 16 * b), X("pool", 0, V, "r16", 32 * o + a, 32 * o + b))
+    def pair(t, k, side=None, a=0, b=H):
+        name, at = ("v1", 2 * H * (k - 3)) if t and k > 2 else ("pool", UB[t] + 32 + 2 * H * k)
+        return (name, at, at + 2 * H) if side is None else A(name, at + side + 2 * a, at + 2 * b, 2)
 
-    def duel(o, cmp):
-        if o == 1:
-            tt(A(cmp), X("pool", 0, V, "r16", 32, 64), big("rw", 0), ALU.is_lt)
+    def root(t, o, a=0, b=H):
+        return pair(t, max(o - 1, 0), min(o, 1), a, b)
+
+    def first(t, o, a=0, b=H):
+        return pair(t, 3 + o, 0, a, b)
+
+    def second(t, o, a=0, b=H):
+        return pair(t, 3 + o, 1, a, b)
+
+    def pick(t, k, off, c, d):
+        return X(*pair(t, k), off, c, d)
+
+    def kept(o, off, c, d):
+        return X("pool", UB[0], pair(0, 3 + max(o - 1, 0))[2], off, c, d)
+
+    def given(off, c, d):
+        return X("pool", P0 - 16, P0 + V, off, c, d)
+
+    def count(bank, cmp, signs, out16, flag, nk=None):
+        out, c = A(bank, 0, 32), (15 / 64 if nk is None else 63 / 128) + signs / 4
+        lin(out, [("id1", A("j2"))] + ([] if nk is None else [("idb", nk)]), True, False)
+        wrap(out, "bd" if signs else "bc", 0, cmp)
+        ts(out16, out, c, ALU.add)
+        tt(flag, out, blk("th", 2 * (nk is not None) + signs), ALU.is_ge)
+        return c
+
+    def signed(cmp, bank, terms, bias):
+        lin(A(bank), terms)
+        act(A(cmp), A(bank), ACT.Sign, bias)
+
+    def duel(t, o, cmp):
+        signs = o == 1 and OPT["duel1"][t] == "s"
+        if signs:
+            signed(cmp, "b3", [("id1", root(t, 0)), ("idn", root(t, 1))], -0.5)
+        elif o == 1:
+            tt(A(cmp), given("r16", 32, 64) if t == 0 else kept(1, "p16", 32, 64), root(t, 0), ALU.is_lt)
         else:
-            tt(A(cmp), X("rw", 0, H * o, "ml16", 0, 32), big("rw", o), ALU.is_gt)
-        count("b7", cmp)
+            act(pair(t, o - 1, 0), pick(t, o - 2, "ml16", 32 * o - 64, 32 * o - 32))
+            tt(A(cmp), pick(t, o - 2, "ml16", 32 * o - 64, 32 * o - 32), root(t, o), ALU.is_gt)
+        count("b1", cmp, signs, blk("ml16", o - 1), blk("sd", o - 1))
 
-    def crown(o):
-        tt(A("mt"), A("b7", 0, 32), blk("al", o), ALU.min)
-        tt(A("ml"), A("mt"), blk("al", 0) if o == 1 else A("ml"), ALU.max)
-        ts(A("ml16"), A("ml"), OFF, ALU.subtract)
+    def third(t):
+        (r, at), s1, s2, one = (("ad", 3), ("ao", 0))[t], blk("sd", 0), blk("sd", 1), blk("one", 0)
+        lin(blk("b6", 0), [("idn", s1), ("idn", s2)])
+        act(A("nh"), blk("b6", 0), ACT.Sign, 0.5)
+        lin(blk("b6", 10), [("idh", one), ("idh", A("nh"))])
+        lin(blk("b6", 11), [("idh", one), ("idn", s2), ("idi", A("nh"))])
+        mm(blk("b6", 12), A("id1"), s2)
+        tt(A("ce"), blk(r, at, 3), blk("b6", 10, 3), ALU.mult)
+        late = [[], []]
+        if t:
+            tt(A("cf"), blk("ic", 0, 3), blk("b6", 10, 3), ALU.mult)
+            lin(blk("b6", 14), [("id1", blk("ic", 3))] + [("idn", blk("cf", o)) for o in range(3)])
+            lin(blk("b6", 15), [("id1", blk("cf", o)) for o in range(3)])
+            act(A("qs"), blk("b6", 14, 2))
+            for k in range(2):
+                tt(blk("vq", k), blk("qs", k), blk("b7", 5), ALU.mult)
+                late[k] = [("id1", blk("vq", k))]
+        lin(blk("b6", 13), [(("idf", "id1")[t], blk(r, at + 3))] + [("idn", blk("ce", o)) for o in range(3)] + late[0])
+        lin(blk("b2", 0), [("id1", blk("ce", o)) for o in range(3)] + late[1], True, False)
+        if t:
+            for o in range(3):
+                lin(blk("b3", 10 + o), [("id1", blk("qs", 1)), ("idi", blk("nk0", o))] + [[("idm", one), ("idn", one)], [("idm", one)], [("idn", one)]][o]
+                    + [("id1", blk("sm", p)) for p in range(o + 1, 3)])
+            act(A("te"), blk("b3", 10, 3))
 
-    def follow(o):
-        w = blk("ge", 2) if o == 3 else A("wn")
-        tt(w, A("ml"), blk("al", o), ALU.is_ge)
-        tt(A("q"), w, A("td"), ALU.mult)
-        tt(blk("y0", 0), A("q"), blk("r0", 0) if o == 1 else blk("y0", 0), ALU.add)
-        if o < 3:
-            tt(A("td"), blk("r0", o + 1), blk("y0", 0), ALU.subtract)
-
-    def children():
-        ts(A("kg"), X("chw", 0, V, "m16", 0, 32), 1536.0, ALU.subtract)
-
-    def wrap_children(rest):
+    def crowned(t):
+        one = blk("one", 0)
+        tt(A("u3"), blk("sd", 2), blk("b6", 13), ALU.mult)
+        mm(blk("b2", 0), A("idf"), A("u3"), False, True)
+        ts(blk("m16", t), blk("b2", 0), C, ALU.add)
+        ts(A("kg"), X("chw", 0, V, "m16", 32 * t, 32 * t + 32), A("pf", 5, 6), ALU.subtract)
+        act(blk("y%d" % t, 0), blk("b2", 0))
         for o in range(3):
-            bank = rest if o else "b4"
-            mm(blk(bank, o), A("id16"), A("c15"), True, False)
-            for i in range(16):
-                mm(blk(bank, o), A("bo", 144 * o + 15 - i, 144 * o + 143 - i), A("kg", i, H, 16), False, i == 15)
+            lin(blk("b1", 1 + o), [("idn", blk("sd", j)) for j in range(o, 3)])
+        act(A("ng"), blk("b1", 1, 3), ACT.Sign, 0.5)
+        if t:
+            tt(A("uq"), blk("sd", 2), blk("b6", 14), ALU.mult)
+            for o in range(3):
+                lin(blk("b1", 12 + o), [("idk" if o else "idl", x) for x in (blk("te", o), A("uq")) * (1 + (o > 0))])
+            tt(blk("alp", 0), blk("b1", 12), blk("lp", 0), ALU.max)
+            tt(blk("alp", 1, 2), blk("b1", 13, 2), blk("lp", 1, 2), ALU.min)
+        lin(blk("b1", 4), [("idi", one), ("idi", blk("ng", 0)), ("id1", blk("er", 0))])
+        lin(blk("b1", 5, 2), [("idh", blk("ng", 0, 2)), ("idi", blk("ng", 1, 2)), ("id1", blk("er", 1, 2))])
+        lin(blk("b1", 7), [("idi", one), ("idh", blk("ng", 2)), ("id1", blk("er", 3))])
+        act(A("ea"), blk("b1", 4, 4), ACT.Relu)
+        for o in range(3):
+            out, w = blk(OPT["wb"][t][o], 8 + o), ("idk", "idl")[t]
+            lin(out, [(w, one), (w, blk("ng", o))], True, False)
+            wrap(out, "bo", 144 * o, "kg")
+            if t:
+                tt(blk("kw", o), out, blk("alp", o), ALU.max if o else ALU.min)
+            else:
+                act(blk("kw", o), out)
+        if t:
+            for o in range(3):
+                lin(blk("b1", 1 + o), [("id1", blk("te", o)), ("id1", A("uq")), ("idh", one)])
+            act(A("fx"), blk("b1", 1, 3), ACT.Relu)
+            lin(blk("b1", 4, 3), [("idg", A("u0")), ("idg", A("lp")), ("idn", A("cm"))], True, False)
+            run([(blk("b1", 4), A("idf"), blk("y0", 0), False, False), (blk("b1", 5, 2), A("idf"), blk("u0", 0, 2), False, False),
+                 (blk("b1", 5, 2), A("id1"), blk("xi", 0, 2), False, True)])
+            tt(A("alt"), A("fx"), blk("b1", 4, 3), ALU.mult)
+            lin(blk("b1", 12, 3), [("idf", A("kw")), ("idf", A("alt"))])
+            act(A("kx"), blk("b1", 12, 3))
 
-    def halve_open(t):
-        lin(A("b1"), [("id1", A("cq")), ("idh", A("z%d" % t))], True, False)
-        mm(A("b2"), A("idh"), A("z%d" % t), True, False)
+    def sendz(t):
+        n = OPT["zs"][t]
+        cp(A("z%d" % t, 0, 16 * n), pick(t, 2, "ml16", 64, 64 + n))
+        act(A("z%d" % t, 16 * n, H), pick(t, 2, "ml16", 64 + n, 96))
+        send(1 + 2 * t)
 
-    def halve_p(t):
-        mm(A("b2"), A("idh"), A("w%d" % t), False, True)
-        mm(A("b1"), A("idh"), A("w%d" % t), False, True)
-
-    def halve():
-        ts(A("mb"), A("b1"), MAGIC, ALU.add, MAGIC, ALU.subtract)
-
-    def shift_a(s):
-        ts(A("si"), A("uc"), s, ALU.add)
-        ts(A("sj", 0, 3), A("si", 0, 3), 4, ALU.logical_shift_right, 31, ALU.bitwise_and)
-        ts(A("sj", 3, 4), A("si", 3, 4), 15, ALU.bitwise_and)
-        cp(A("s16", 0, 3), A("sj", 0, 3))
-        cp(A("sf", 0, 1), A("sj", 3, 4))
-        ts(A("pp"), A("m2"), A("sf", 0, 1), ALU.add, A("pf", 3, 4), ALU.is_equal)
-
-    def shift_v(orders):
-        for o in orders:
-            ts(A("g16", 48 * o, 48 * o + 48), X("kw", 32 * o, 32 * o + 32, "s16", 0, 3), 1536.0, ALU.subtract)
-
-    def shift_p(orders, less):
-        for o in orders:
-            bank = ("b3" if o else "b0") if less else "b5"
-            mm(blk(bank, o), A("id16"), A("c15"), True, False)
-            if less:
-                mm(blk(bank, o), A("idg"), blk("a", o), False, False)
-            mm(blk(bank, o), A("pp", 0, 128), A("g16", 48 * o, 48 * o + 32), False, False)
-            mm(blk(bank, o), A("pp", 128, 256), A("g16", 48 * o + 1, 48 * o + 33), False, True)
+    def shift(t):
+        ei = ("ei", "fi")[t]
+        for p, a in ((0, 0), (1, 3), (2, 5)):
+            if OPT["lt"][t] == "v":
+                ts(A("lt", a, a + 3 - p), A(ei, 16 * p + 16, 64, 16), A(ei, 16 * p, 16 * p + 1), ALU.is_lt)
+            else:
+                act(A("lu", a, a + 3 - p), A(ei, 16 * p + 16, 64, 16), ACT.Sign, A(ei, 16 * p, 16 * p + 1), -1.0)
+        if OPT["lt"][t] == "s":
+            act(A("lt", 0, 6), A("lu", 0, 6), ACT.Relu)
+        mm(A("b3", 16, 32), A("id1"), A("csh"), True, False)
+        run([(A("b3", 16 + 4 * k, 20 + 4 * k), A("blk"), A(ei, 0, 64, 16), False, k == 3) for k in range(4)])
+        mm(A("b3", 0, 6), A("blk"), A("lt", 0, 6))
+        ts(A("lf", 0, 6), A("b3", 0, 6), 8.5, ALU.is_ge)
+        op("v", lambda: g.vector.tensor_tensor_scan(T.lf[:, 8:14], T.lf[:, 16:22], T.lf[:, 0:6], 0.0, ALU.mult, ALU.add),
+           [A("lf", 16, 24), A("lf", 0, 6)], [A("lf", 8, 14)], 0.1)
+        cp(A("t16", 0, 1), A("lf", 13, 14))
+        cp(A("q16"), X("lut", 0, 64, "t16", 0, 1))
+        cp(A("si"), A("b3", 16, 32))
+        ts(A("sj", 0, 12), A("si", 0, 12), 4, ALU.logical_shift_right, 31, ALU.bitwise_and)
+        ts(A("sj", 12, 16), A("si", 12, 16), 15, ALU.bitwise_and)
+        cp(A("s16"), X("sj", 0, 16, "q16", 0, 1))
+        cp(A("sa"), X("sj", 0, 16, "q16", 0, 1))
+        ts(A("pp"), A("m2"), A("sa", 3, 4), ALU.add, A("pf", 3, 4), ALU.is_equal)
+        for kw, g16, c, at in ((("kw", "g16", "cp5", 1), ("kx", "gx", "c15", 4)) if t else (("kw", "g16", "c15", 4),)):
+            for o in range(3):
+                cp(A(g16, 48 * o, 48 * o + 48), X(kw, 32 * o, 32 * o + 32, "s16", 0, 3))
+                run([(blk("b6", at + o), A("id1"), blk(c, o), True, False)]
+                    + [(blk("b6", at + o), A("pp", 128 * k, 128 * k + 128), A(g16, 48 * o + k, 48 * o + k + 32), False, k == 1) for k in range(2)])
 
     def structure(t):
-        def sums():
-            for o in range(3):
-                lin(blk("b7", o), [("id%d" % (1 << j), blk(e, j)) for j in range(o + 1) for e in ("ea", "eb")])
-        if t:
-            act(A("eb"), blk("b5", 0, 3), ACT.Sign)
-            tt(blk("tb", 0), blk("eb", 0), blk("b0", 0), ALU.mult)
-            lin(blk("b6", 0), [("idf", blk("a", 0)), ("idf", blk("tb", 0))])
-            sums()
-            halve_p(t)
-            cp(blk("x16", 0), blk("b6", 0))
-            act(big("xs", 0), X("pool", 0, V, "x16", 0, 32))
-        else:
-            ts(blk("eb", 1, 2), blk("b5", 1, 2), 0.0, ALU.is_gt)
-            sums()
-            shift_p((1, 2), True)
-            lin(blk("b6", 0), [("idf", blk("a", 0)), ("idf", blk("tb", 0))])
+        nk, one = "nk%d" % t, A("one")
+        for o, n in OPT["cut"][t]:
+            if t:
+                tt(blk("xt", o, n), blk("b6", 1 + o, n), blk("al", o, n), ALU.max)
+            else:
+                tt(blk("xt", o, n), blk("b6", 4 + o, n), blk("xp", o, n), ALU.min)
+            cp(blk("x16", o, n), blk("xt", o, n))
         for o in range(3):
-            ts(blk("lk", o), blk("b7", o), float((2 << o) - 1), ALU.is_ge)
-        tt(blk("ta", 1, 2), blk("eb", 1, 2), blk("lk", 0, 2), ALU.mult)
-        tt(blk("tb", 1, 2), blk("ta", 1, 2), blk("b3", 1, 2), ALU.mult)
-        lin(blk("b6", 1, 2), [("idf", blk("a", 1, 2)), ("idf", blk("tb", 1, 2))])
+            lo, hi = (0, P0 + V + H * o) if t else (P0, pair(0, 1)[2])
+            n = OPT["xs"][t] if o == 0 else 0
+            if n:
+                cp(first(t, o, 0, 16 * n), X("pool", lo, hi, "x16", 32 * o, 32 * o + n))
+            act(first(t, o, 16 * n, H), X("pool", lo, hi, "x16", 32 * o + n, 32 * o + 32))
         if t:
-            halve()
+            act(A("eb"), blk("b6", 1, 3), ACT.Sign)
+            act(A("bz"), blk("b6", 4, 3), ACT.Relu)
         else:
-            halve_p(t)
-            kept()
-        lin(blk("b7", 0, 3), [("idf", A("dm")), ("idk", A("lk"))])
-        act(blk("nl", 0, 3), A("lk"), ACT.Identity, 1.0, -1.0)
-        act(A("thr"), A("lk"), ACT.Identity, 1048576.0 + 36864.0, -1048576.0)
-        cp(blk("x16", 1, 2), blk("b6", 1, 2))
-        act(big("xs", 1), X("pool", 0, V, "x16", 32, 64))
-        act(big("xs", 2), X("pool", 0, V, "x16", 64, 96))
-        act(blk("nl", 3), blk("ea", 3), ACT.Identity, 1.0, -1.0)
-        act(A("dnl"), blk("b7", 0, 3))
-
-    def carries(t):
-        tt(A("ta"), A("lk"), blk("b6", 0, 3), ALU.mult)
-        tt(blk("tb", 0, 2), blk("nl", 0, 2), blk("b5", 1, 2), ALU.mult)
-        tt(A("q"), blk("y%d" % t, 0), blk("b6", 0), ALU.subtract)
-        lin(blk("b6", 3, 2), [("idf", blk("ta", 0, 2)), ("idf", blk("tb", 0, 2))])
-        mm(blk("b6", 5), A("idf"), blk("ta", 2))
-
-    def kept():
-        tt(blk("odd", 1, 2), blk("eb", 1, 2), blk("lk", 0, 2), ALU.is_equal)
-        tt(blk("ao", 0), blk("eb", 0), blk("a", 0), ALU.mult)
-        tt(blk("ao", 1, 2), blk("odd", 1, 2), blk("a", 1, 2), ALU.mult)
-
-    def root(t, o, n=1):
-        r = "r%d" % (t + 1)
-        tt(blk("ne", o, n), blk("nl", o, n), blk("y%d" % t, o, n), ALU.mult)
-        tt(blk(r, o, n), blk("ne", o, n), blk("ao", o, n) if o < 3 else blk("a", 3), ALU.add)
+            act(A("eb"), blk("b6", 4, 3), ACT.Sign, K / 4, -1.0)
+            act(A("bz"), blk("b6", 4, 3), ACT.Relu, K / 4, -1.0)
+        mm(blk("b0", 1, 4), A("id1"), A("cl"), True, False)
+        mm(blk("b0", 4), A("idk"), blk("ea", 3), False, False)
+        for e, w in (("ea", ("idn", "idm", "idq")), ("eb", ("idi", "idn", "idm"))):
+            run([(blk("b0", 1 + o), A(w[j]), blk(e, j), False, e == "eb" and o == 3 and j == 2)
+                 for o in range(4) for j in range(min(o, 2) + 1)])
+        act(A(nk), blk("b0", 1, 4), ACT.Sign)
+        bk = ("b6", "b1")[t]
+        lin(blk(bk, 8), [("idh", blk("one", 0)), ("idh", blk(nk, 0))])
+        lin(blk(bk, 9, 2), [("idh", blk(nk, 1, 2)), ("idi", blk(nk, 0, 2))])
+        lin(blk(bk, 11), [("idh", blk("one", 0)), ("idi", blk(nk, 3))])
+        act(A("ic"), blk(bk, 8, 4))
+        lin(blk(bk, 12, 3), [("idh", blk(nk, 0, 3)), ("idh", A("eb")), ("id1", blk("ea", 0, 3))])
+        mm(blk(bk, 15), A("id1"), blk("ea", 3))
         if t == 0:
-            cp(blk("r16", o, n), blk(r, o, n))
+            tt(A("fp"), A("al"), blk(bk, 12, 4), ALU.mult)
+            lin(blk(bk, 8, 4), [("idk", A("ic")), ("idn", A("wb"))])
+            tt(A("hi"), A("fp"), blk(bk, 8, 4), ALU.add)
+        lin(blk("b7", 0, 3), [("idh", one), ("idh", blk(nk, 0, 3))])
+        lin(blk("b7", 3, 3), [("idi", blk(nk, 0, 3)), ("idi", A("eb"))])
+        tt(A("mm"), blk("ad", 0, 6), blk("b7", 0, 6), ALU.mult)
+        w = ("idj", "idu")[t]
+        lin(blk("b7", 0, 3), [(("idg", "idf")[t], A("bz")), (w, one), (w, A("eb"))], True, False)
+        lin(blk("b7", 0, 3), [("id1", blk("mm", 0, 3)), ("id1", blk("mm", 3, 3))], False, True)
+        cp(A("xi"), blk("b7", 0, 3))
+        tt(A("ao"), blk("ad", 3, 4), blk(bk, 12, 4), ALU.mult)
+        lin(blk(bk, 8, 3), [("idh", blk(nk, 0, 3)), ("idh", A("eb")), ("id1", blk("ea", 0, 3)), ("id1", blk("ic", 0, 3))])
+        lin(blk(bk, 11), [("id1", blk("ea", 3)), ("id1", blk("ic", 3))])
+        act(A("er"), blk(bk, 8, 4))
 
-    def pick():
-        tt(A("td"), A("wn"), A("h2"), ALU.add)
-        cp(A("o16"), A("td"))
+    def halve(t):
+        z, w = A("z%d" % t), A("w%d" % t)
+        lin(A("b2"), [("idw", z), ("idw", w)])
+        ts(second(t, 0), A("b2"), MAGIC, ALU.add, MAGIC, ALU.subtract)
 
     def link(t, o):
-        y = "y%d" % t
-        tt(A("wn"), A("b0", 0, 32), blk("thr", o), ALU.is_ge)
-        if o == 2 and t == 1:
-            pick()
-            act(A("ln2"), X("xyn", 0, 2 * H, "o16", 0, 32))
-        tt(blk("u", o), A("wn"), A("q"), ALU.mult)
-        if o < 2 or t == 0:
-            tt(blk(y, o + 1), blk("u", o), blk("b6", 3 + o), ALU.add)
-        if o < 2:
-            cp(blk("y16", o), blk(y, o + 1))
-
-    def gap(t, o):
-        tt(A("q"), blk("y%d" % t, o), blk("b6", o), ALU.subtract)
-
-    def loser_p(t, o, n, bank):
-        lin(blk(bank, 8 + o, n), [("idf", blk("y%d" % t, o, n)), ("idg", blk("u", o, n))])
-
-    def loser(o, n, bank):
-        tt(blk("ls", o, n), blk("dnl", o, n), blk(bank, 8 + o, n), ALU.max)
-        cp(blk("l16", o, n), blk("ls", o, n))
-
-    def differ(o, early):
-        e = "e%d" % o
-        tt(A(e), X("pool", 0, V, "y16", 32 * (o - 1), 32 * o), big("xs", o), ALU.subtract)
-        ts(A("cmpa"), A(e), 0.0, ALU.is_lt)
-        if early:
-            moved_p(o - 1, True)
-        count("b0", "cmpa")
-
-    def moved_p(o, last):
-        x0, x1, x2, e1, e2 = big("xs", 0), big("xs", 1), big("xs", 2), A("e1"), A("e2")
-        d, l = (A("b2"), A("b3")) if o == 0 else (A("b1"), A("b4"))
-        if last:
-            mm(d, A("id2"), e2 if o else e1, False, True)
-            mm(l, A("idn"), e2 if o else e1, False, True)
-        elif o == 0:
-            lin(d, [("idn", x0), ("idn", A("mb")), ("id2", x1)], True, False)
-            lin(l, [("id1", x0), ("id1", A("mb")), ("idn", x1)], True, False)
+        y, u, nk = "y%d" % t, "u%d" % t, "nk%d" % t
+        signs = OPT["c12" if o else "cmp0"][t] == "s"
+        if o:
+            carry = pick(t, 2 + o, "y16", 32 * o - 32, 32 * o)
+            act(second(t, o), carry)
+            if signs:
+                signed("cmpa", "b3", [("id1", first(t, o)), ("idn", second(t, o))], -0.5)
+            else:
+                tt(A("cmpa"), carry, first(t, o), ALU.is_lt)
+        elif signs:
+            signed("cmpa", "b3", [("idi", A("z%d" % t)), ("idi", A("w%d" % t)), ("id1", first(t, 0))], -0.25)
         else:
-            lin(d, [("idm", x1), ("idn", e1), ("id2", x2)], True, False)
-            lin(l, [("id2", x1), ("id1", e1), ("idn", x2)], True, False)
-
-    def moved_s(o):
-        act(big("sg", o), A("b1" if o else "b2"), ACT.Sign)
-        act(big("lc", o), A("b4" if o else "b3"))
-
-    def both_p(by, bx):
-        lin(A(by), [("id1", big("xs", 2)), ("id1", A("e2")), ("idn", big("sg", 2))])
-        lin(A(bx), [("id1", big("xs", 2)), ("id1", big("sg", 2))])
-
-    def both_s(by, bx):
-        act(A("xyn", 0, 2 * H, 2), A(by))
-        act(A("xyn", 1, 2 * H, 2), A(bx))
-
-    def put(o, a=0, b=32):
-        dst = X("pool", 0, V + H, "l16", 32 * o + a, 32 * o + b)
-        if o < 2:
-            tt(dst, big("lc", o, 16 * a, 16 * b), big("sg", o, 16 * a, 16 * b), ALU.add)
-        else:
-            cp(dst, A("ln2", 16 * a, 16 * b))
-
-    def meld_start(t):
-        tt(A("cmpa"), big("xs", 0), A("b2"), ALU.is_gt)
-        count("b0", "cmpa")
-        carries(t)
+            lin(A("b3"), [("idh", A("z%d" % t)), ("idh", A("w%d" % t))])
+            tt(A("cmpa"), first(t, 0), A("b3"), ALU.is_gt)
+        c = count("b0", "cmpa", signs, blk("y16", o), blk("sm", o), blk(nk, o))
         if t == 0:
-            halve()
-        link(t, 0)
+            newroot(o + 1, A("b0", 0, 32), c)
+        now = [("id1", blk("xi", o - 1)), ("idf", blk(u, o - 1))] if o else [("idf", blk(y, 0))]
+        lin(blk("b7", 3), [("idn", blk("xi", o))] + now)
+        tt(blk(u, o), blk("sm", o), blk("b7", 3), ALU.mult)
+        if o == 2:
+            lin(blk("b7", 5), [("id1", blk("xi", o)), ("idf", blk(u, o))])
+        lin(blk("b7", 4), now + [("idg", blk(u, o))])
+        ts(blk("l16", 3 * t + o), blk("b7", 4), C, ALU.add)
+        if o == 2:
+            act(blk(y, 1), blk("b7", 5))
 
-    dma("y", [(T.pool[:, 0:V], T.rec[:])], [], [A("pool", 0, V)], "lrec")
-    dma("s", [(T.rti[:], T.rt[:])], [], [A("rti")], "lrt")
-    dma("s", [(T.sv[:], T.rec[:, 0:2])], [], [A("sv")], "lsv")
+    def newroot(o, place, c):
+        tt(A("rv"), place, blk("hi", o), ALU.min)
+        ts(blk("p16", o), A("rv"), pair(0, 3 + max(o - 1, 0))[1] - UB[0] + c, ALU.add)
+        act(root(1, o), kept(o, "p16", 32 * o, 32 * o + 32))
+
+    def numbers(t):
+        for o in range(4):
+            mm(blk("b7", 6 + o), A("idf"), blk("y%d" % t, 1))
+        tt(A("cc"), A("ic"), blk("b7", 6, 4), ALU.mult)
+        if t:
+            lin(blk("b7", 10, 4), [("id1", A("ao")), ("idj", A("er")), ("idj", A("er")), ("id1", A("cc"))])
+            act(A("r2"), blk("b7", 10, 4))
+        else:
+            lin(blk("b7", 10, 4), [("id1", A("ao")), ("id1", A("cc"))])
+            act(blk("ad", 3, 4), blk("b7", 10, 4))
+
+    def put(t, lst, c, fn, spare):
+        n = 32 // OPT["pieces"][4 * t + (1 + c // 32 % 3) * spare]
+        for a in range(0, 32, n):
+            fn(X("outp", 0, V + H * spare, lst, c + a, c + a + n), 16 * a, 16 * (a + n))
+
+    def put_half(t):
+        put(t, "m16", 32 * t, lambda dst, a, b: cp(dst, second(t, 0, a, b)), 0)
+
+    def put_lost(o):
+        put(0, "l16", 32 * o, lambda dst, a, b: cp(dst, A("lo%d" % o, a, b)), 1)
+
+    def moved(t, o):
+        x, y, w = first(t, o), second(t, o), second(t, o + 1) if o < 2 else A("y3")
+        if o == 2:
+            act(w, pick(t, 5, "y16", 64, 96))
+        lin(A("b4"), [("id1", x), ("id1", y), ("idm", w)])
+        act(big("sg", o % 2), A("b4"), ACT.Sign, None, -1.0)
+        if t == 0:
+            lin(A("b5"), [("id1", x), ("id1", y), ("idn", w), ("id1", big("sg", o % 2))])
+            act(A("lo%d" % o), A("b5"))
+            return put_lost(o)
+        lin(A("b5"), [("id1", x), ("id1", y), ("idn", w)])
+        act(big("lc", o), A("b5"))
+        put(t, "l16", 32 * (3 * t + o), lambda dst, a, b: tt(dst, A("lc", H * o + a, H * o + b), A("sg", H * o + a, H * o + b), ALU.add), 1)
+
+    def both(t):
+        x, y = first(t, 2), second(t, 2)
+        lin(A("b4"), [("idn", x), ("id1", y)])
+        act(A("dw", 1, 2 * H, 2), A("b4"), ACT.Sign)
+        lin(A("b5"), [("idn", x), ("id1", y), ("idn", A("dw", 1, 2 * H, 2))])
+        act(A("dw", 0, 2 * H, 2), A("b5"))
+
+    def chosen(t):
+        act(A("ln"), X("dw", 0, 2 * H, "y16", 64, 96))
+        put(t, "l16", 32 * (3 * t + 2), lambda dst, a, b: tt(dst, first(t, 2, a, b), A("ln", a, b), ALU.add), 1)
+
+    dma("y", [(T.pool[:, P0:P0 + V], T.rec[:])], [], [A("pool", P0, P0 + V)], "lrec", 4.2)
+    dma("s", [(T.rti[:], T.rt[:])], [], [A("rti")], "lrt", 1.5)
     iota(A("pc", 0, 1), [[0, 1]], 0, 1)
     iota(A("t1"), [[1, 144]], 0, 0)
-    iota(A("ali"), [[16, 128]], int(OFF), 0)
+    iota(A("ali", 32, 128), [[2 * H, 3], [32, 32]], 33, 0)
+    iota(A("ali", 0, 32), [[32, 32]], 32, 0)
     iota(A("blki"), [[1, 8], [0, 16]], 0, 0)
-    iota(A("dmi"), [[0, 3], [16, 32]], V, 0)
-    iota(A("h2i"), [[32, 32]], 0, 0)
-    iota(A("uci"), [[256, 4]], 0, 0)
+    iota(A("cvi"), [[16, 3], [0, 4]], 0, 0)
     iota(A("m2"), [[-16, 2], [32, 8], [1, 16]], 0, 0)
-    iota(A("chw", 2048, V), [[0, 1024]], 0, 0)
-    ms(A("chw", 0, 1024), 0)
+    iota(A("dmi"), [[0, 3], [16, 32]], int(V - C), 0)
+    iota(A("chw", 2560, V), [[0, 512]], 0, 0)
+    for a in range(0, 2560, 512):
+        ms(A("chw", a, a + 512), 0)
     ts(A("pc", 1, 2), A("pc", 0, 1), 15, ALU.bitwise_and)
     ts(A("pc", 2, 3), A("pc", 0, 1), 4, ALU.logical_shift_right)
     cp(A("pf", 0, 3), A("pc", 0, 3))
     ts(A("pf", 4, 5), A("pf", 2, 3), 16.0, ALU.mult, 15.0, ALU.add)
     ts(A("pf", 3, 4), A("pf", 2, 3), 32.0, ALU.mult, A("pf", 1, 2), ALU.add)
     ts(A("id1"), A("t1", 0, 128), A("pf", 0, 1), ALU.is_equal)
-    ts(A("bc"), A("t1"), A("pf", 4, 5), ALU.is_equal, 4096.0, ALU.mult)
+    ts(A("bc"), A("t1"), A("pf", 4, 5), ALU.is_equal, 1 / 32, ALU.mult)
+    ts(A("pf", 6, 7), A("pf", 1, 2), 2.0, ALU.mult)
+    if "s" in OPT["cmp0"] + OPT["c12"] + OPT["duel1"]:
+        ts(A("bd"), A("bc"), 0.5, ALU.mult)
     ts(A("blk"), A("blki"), A("pf", 2, 3), ALU.is_equal)
-    act(A("al"), A("ali"), ACT.Identity, A("pf", 1, 2))
-    act(A("pf", 5, 6), A("pf", 1, 2), ACT.Copy, None, 2.0)
-    act(A("pf", 6, 7), A("pf", 1, 2), ACT.Copy, None, 16.0)
-    for name, c in (("idf", 1.0), ("idg", -1.0), ("idh", 0.5), ("idn", -1.0), ("id2", 2.0), ("idm", -2.0), ("id4", 4.0),
-                    ("idk", -8192.0)):
+    ts(A("rz"), A("rti"), 0.0, ALU.is_gt, 16.0, ALU.mult)
+    tt(A("ri"), A("rz"), A("rti"), ALU.add)
+    cp(A("r16"), A("ri"))
+    cp(A("e16"), A("ri", 0, 128, 32))
+    ts(blk("ad", 3, 4), A("rti"), C, ALU.subtract)
+    ts(blk("ad", 0, 3), A("dmi"), A("pf", 1, 2), ALU.add)
+    ms(A("pool", P0 - 16, P0), 256.0)
+    act(A("al"), A("ali"), ACT.Identity, A("pf", 6, 7))
+    ts(A("j2"), blk("al", 0), 32.0, ALU.subtract)
+    for k, c in enumerate((15 / 64, 31 / 64, 63 / 128, 95 / 128)):
+        act(blk("th", k), blk("al", 0), ACT.Identity, 0.5 - c - 32)
+    act(A("jc"), blk("al", 0), ACT.Identity, -31.0)
+    for o, n in ((0, 2), (2, 1), (3, 1)):
+        ts(blk("wb", o, n), A("t1", 0, 32 * n), 0.0, ALU.mult, float(pair(0, 3 + max(o - 1, 0))[1] - UB[0]), ALU.add)
+    for name, c in EYE[1:] + EYF:
         act(A(name), A("id1"), ACT.Copy, None, c)
-    act(A("blkn"), A("blk"), ACT.Copy, None, -1.0)
-    act(A("dm"), A("dmi"), ACT.Identity, A("pf", 1, 2))
-    act(A("h2"), A("h2i"), ACT.Identity, A("pf", 5, 6))
-    act(A("uc", 0, 3), A("uci", 0, 3), ACT.Identity, A("pf", 6, 7))
-    act(A("uc", 3, 4), A("uci", 0, 1))
-    act(A("cb"), A("h2i"), ACT.Identity, 30720.0, 0.0)
-    ms(A("chw", 1024, 2048), 0)
-    cp(A("r16"), A("rti"))
-    cp(A("e16"), A("rti", 0, 128, 32))
-    cp(A("r0"), A("rti"))
-    dma("y", [(T.chw[16 * k:16 * k + 3, :], T.ch[k]) for k in range(8)], [], [A("chw")], "lch")
+    fill(A("one"), 1.0)
+    dma("y", [(T.chw[16 * k:16 * k + 3, :], T.ch[k]) for k in range(8)], [A("pool", P0, P0 + 16)], [A("chw")], "lch", 2.5)
     ts(A("rm", 0, 3), A("t1", 0, 3), A("pf", 1, 2), ALU.is_equal)
     for o in range(3):
         ts(A("bo", 144 * o, 144 * o + 144), A("t1"), A("pf", 4, 5), ALU.is_equal, A("rm", o, o + 1), ALU.mult)
-    tt(A("td"), blk("r0", 1), blk("r0", 0), ALU.subtract)
-    ms(A("pool", 0, 1), 256.0)
+        act(blk("lp", o), blk("al", 0), ACT.Identity, LOS[o] - P0 - 16 - MID[o], 0.5)
+    for o, n in ((0, 1), (1, 2)):
+        fill(blk("cm", o, n), MID[o] - C)
+    ts(A("c15"), A("cm"), C, ALU.add)
+    ts(A("cp5"), A("cm"), C + P0, ALU.add)
+    ts(A("pf", 5, 6), A("rm", 0, 1), MID[0] - MID[1], ALU.mult, MID[1], ALU.add)
+    act(A("xp"), blk("al", 0, 3), ACT.Identity, float(UB[0] - P0))
+    act(A("er"), A("ri"), ACT.Sign)
+    for a, b, c in ((0, 1, 0.0), (1, 2, 1.0), (2, 4, 3.0)):
+        fill(blk("cl", a, b - a), c)
+    fill(A("lui"), 3.0)
+    for a, b, st, c in ((0, 8, 1, 0.0), (16, 32, 2, 2.0), (32, 64, 8, 1.0), (33, 64, 8, 1.0), (36, 64, 8, 2.0), (38, 64, 8, 2.0)):
+        fill(A("lui", a, b, st), c)
+    ts(A("pf", 7, 8), A("pf", 1, 2), 3.0, ALU.min, 4.0, ALU.mult)
+    act(A("lut"), A("lui"), ACT.Identity, A("pf", 7, 8))
+    fill(A("lf", 16, 24), 2.0)
+    ts(A("idw"), A("id1"), 1023 / 2048, ALU.mult)
+    for none in (A("pool", UB[0], UB[0] + 32), A("pool", 0, 32)):
+        fill(none, 256.0)
+    ts(A("csh", 0, 12), A("cvi"), A("pf", 1, 2), ALU.add, 16.0, ALU.mult)
+    ts(A("csh", 12, 16), A("t1", 0, 4), 0.0, ALU.mult)
 
-    act(A("eo"), X("pool", 0, V, "e16", 0, 4))
+    act(A("eo"), given("e16", 0, 4))
+    early = len(ops) - 1
     send(0)
-    roots(0, "v", 0)
-    roots(0, "s", 1)
-    duel(1, "cmpa")
-    roots(2, "s")
-    roots(1, "s")
-    roots(3, "s")
-    ms(A("cq"), -0.25)
-    cp(A("id16"), A("id1"))
-    ts(A("c15"), A("t1", 0, 32), 0.0, ALU.mult, 1536.0, ALU.add)
-    crown(1)
-    duel(2, "cmpb")
-    follow(1)
-    crown(2)
-    duel(3, "cmpa")
-    follow(2)
-    crown(3)
-    cp(A("z0", 0, 256), X("rw", 0, 4 * H, "ml16", 0, 16))
-    act(A("z0", 256, H), X("rw", 0, 4 * H, "ml16", 16, 32))
-    send(1)
-    act(A("tx"), A("ei", 0, 64, 16), ACT.Identity, -0.5)
-    act(A("lt", 0, 3), A("ei", 16, 64, 16), ACT.Sign, A("tx", 0, 1), -1.0)
-    act(A("lt", 3, 5), A("ei", 32, 64, 16), ACT.Sign, A("tx", 1, 2), -1.0)
-    act(A("lt", 5, 6), A("ei", 48, 49), ACT.Sign, A("tx", 2, 3), -1.0)
-    follow(3)
-    cp(A("m16"), blk("y0", 0))
-    children()
-    for o in range(2):
-        tt(blk("ge", o), A("ml"), blk("al", o + 1), ALU.is_ge)
-    for o in range(1, 4):
-        tt(blk("ne", o), A("ml"), blk("al", o), ALU.not_equal)
-    tt(blk("a", 0), blk("r0", 0), blk("ge", 0), ALU.mult)
-    tt(blk("a", 1, 3), blk("r0", 1, 3), blk("ne", 1, 3), ALU.mult)
-    mm(A("b3", 0, 3), A("blk"), A("lt", 0, 3))
-    mm(A("b3", 3, 4), A("blk"), A("ei", 0, 1))
-    lin(A("b3", 4, 6), [("blk", A("lt", 3, 5)), ("blkn", A("lt", 1, 3))])
-    lin(A("b3", 6, 7), [("blk", A("ei", 16, 17)), ("blkn", A("ei", 0, 1))])
-    mm(A("b3", 7, 8), A("blk"), A("lt", 5, 6))
-    mm(A("b3", 8, 10), A("blk"), A("ei", 32, 64, 16))
-    halve_open(0)
-    wrap_children("b7")
-
-    def col(n, k):
-        return A(n, k, k + 1)
-
-    def wins(out, a):
-        act(col("tz", 15), a, ACT.Sign, -1.0)
-        act(out, col("tz", 15), ACT.Relu)
-
-    def choose(out, w, yes, no):
-        act(col("tz", 14), no, ACT.Identity, yes, -1.0)
-        act(out, col("tz", 14), ACT.Identity, no, w)
-
-    act(A("ty", 0, 10), A("b3", 0, 10))
-    wins(col("tz", 0), col("ty", 0))
-    for k in range(3):
-        act(col("tz", 1 + k), col("ty", 4 + k), ACT.Identity, col("ty", 1 + k), col("tz", 0))
-    wins(col("tz", 4), col("tz", 1))
-    choose(col("tz", 5), col("tz", 4), col("ty", 7), col("tz", 2))
-    wins(col("tz", 7), col("tz", 5))
-    choose(col("tz", 6), col("tz", 4), col("ty", 8), col("tz", 3))
-    choose(col("tz", 8), col("tz", 7), col("ty", 9), col("tz", 6))
-    act(A("ea"), A("a"), ACT.Sign)
-    tt(blk("kw", 0), blk("b4", 0), blk("ge", 0), ALU.mult)
-    shift_a(col("tz", 8))
-    shift_v((0,))
-    shift_p((0,), False)
-    shift_p((0,), True)
-    tt(blk("kw", 1, 2), blk("b7", 1, 2), blk("ge", 1, 2), ALU.mult)
-    shift_v((1, 2))
-    ts(blk("eb", 0), blk("b5", 0), 0.0, ALU.is_gt)
-    shift_p((1, 2), False)
-    tt(blk("tb", 0), blk("eb", 0), blk("b0", 0), ALU.mult)
-    tt(A("td"), blk("tb", 0), blk("a", 0), ALU.add)
-    cp(blk("x16", 0), A("td"))
-    act(big("xs", 0), X("pool", 0, V, "x16", 0, 32))
+    cp(root(0, 0, 0, 320), given("r16", 0, 20))
+    act(root(0, 0, 320, H), given("r16", 20, 32))
+    ops[-1][8].append(early)
+    for o in (1, 2, 3):
+        act(root(0, o), given("r16", 32 * o, 32 * o + 32))
+    duel(0, 1, "cmpa")
+    duel(0, 2, "cmpb")
+    third(0)
+    duel(0, 3, "cmpa")
+    sendz(0)
+    dma("y", [(T.outp[:, 0:V], T.rec[:])], [A("z0")], [A("outp", 0, V)], "lout", 5.0)
+    crowned(0)
+    shift(0)
     structure(0)
 
-    meld_start(0)
-    root(0, 0, 2)
-    cp(X("pool", 0, V + H, "m16", 0, 32), A("mb"))
-    moved_p(0, False)
-    roots(0, "s")
-    roots(1, "s")
-    differ(1, False)
-    gap(0, 1)
-    lin(A("b1"), [("id1", big("rw", 0)), ("idn", big("rw", 1))])
-    act(A("cmpb"), A("b1"), ACT.Sign, -0.5)
-    moved_p(0, True)
-    count("b7", "cmpb", True)
+    halve(0)
+    newroot(0, A("jc"), 0.0)
+    link(0, 0)
     link(0, 1)
-    root(0, 2)
-    roots(2, "s")
-    moved_s(0)
-    differ(2, False)
-    gap(0, 2)
-    crown(1)
-    moved_p(1, False)
-    duel(2, "cmpb")
+    duel(1, 1, "cmpb")
+    duel(1, 2, "cmpb")
     link(0, 2)
-    root(0, 3)
-    roots(3, "s", 1)
-    roots(3, "v", 0)
-    act(big("sg", 2), A("e2"), ACT.Sign)
-    moved_p(1, True)
-    moved_s(1)
-    loser_p(0, 0, 3, "b0")
-    lin(blk("b0", 11, 3), [("idf", blk("y0", 1, 3)), ("idk", blk("nl", 0, 3))])
-    crown(2)
-    duel(3, "cmpa")
-    lin(blk("b6", 6), [("idf", blk("r1", o)) for o in range(4)], True, False)
-    pick()
-    loser(0, 3, "b0")
-    act(A("wl"), blk("b0", 11, 3))
-    crown(3)
-    cp(A("fo"), X("rw", 0, 4 * H, "ml16", 0, 1))
+    cp(A("f16"), A("p16", 0, 128, 32))
+    (cp if OPT["fo"] == "v" else act)(A("fo"), kept(3, "f16", 0, 4))
     send(2)
-    act(A("z1"), X("rw", 0, 4 * H, "ml16", 0, 32))
-    send(3)
+    duel(1, 3, "cmpb")
+    sendz(1)
+    third(1)
+    numbers(0)
+    crowned(1)
+    put_half(0)
+    moved(0, 0)
+    moved(0, 1)
+    moved(0, 2)
 
-    for o in range(4):
-        mm(blk("b7", o), A("idf"), A("ml"))
-    both_p("b2", "b3")
-    both_s("b2", "b3")
-    act(A("ln2"), X("xyn", 0, 2 * H, "o16", 0, 32))
-    put(0, 0, 16)
-    tt(A("ne"), A("al"), blk("b7", 0, 4), ALU.not_equal)
-    tt(A("a"), A("r1"), A("ne"), ALU.mult)
-    lin(blk("b6", 6), [("idg", blk("a", o)) for o in range(4)], False, True)
-    tt(A("ge"), blk("al", 1, 3), blk("b7", 0, 3), ALU.is_le)
-    put(0, 16, 32)
-    cp(A("m16"), blk("b6", 6))
-    children()
-    for o in range(3):
-        tt(blk("fx", o), blk("wl", o), blk("b6", 6), ALU.is_equal)
-    act(blk("y1", 0), blk("b6", 6))
-    wrap_children("b4")
-    put(1)
-    tt(A("ta"), blk("b4", 0, 3), A("ge"), ALU.mult)
-    lin(blk("b7", 0, 3), [("idf", A("ls")), ("idg", A("ta"))])
-    mm(A("b0", 0, 1), A("blk"), A("fi", 0, 1))
-    shift_a(A("b0", 0, 1))
-    tt(A("tb"), A("fx"), blk("b7", 0, 3), ALU.mult)
-    lin(blk("b7", 0, 3), [("idf", A("ta")), ("idf", A("tb"))])
-    act(A("kw"), blk("b7", 0, 3))
-    act(A("ea"), A("a"), ACT.Sign)
-    halve_open(1)
-    put(2, 0, 16)
-    shift_v((0, 1, 2))
-    shift_p((0, 1, 2), False)
-    shift_p((0, 1, 2), True)
-    put(2, 16, 32)
+    shift(1)
     structure(1)
-    meld_start(1)
-    loser_p(1, 0, 1, "b6")
-    cp(X("pool", 0, V + H, "m16", 0, 32), A("mb"))
-    moved_p(0, False)
-    differ(1, True)
-    moved_s(0)
-    moved_p(1, False)
-    gap(1, 1)
-    loser(0, 1, "b6")
-    kept()
+    halve(1)
+    put_half(1)
+    link(1, 0)
     link(1, 1)
-    loser_p(1, 1, 1, "b6")
-    differ(2, True)
-    act(A("pool", 0, 1), A("sv", 0, 1))
-    act(big("sg", 2), A("e2"), ACT.Sign)
-    both_p("b5", "b7")
-    moved_s(1)
-    both_s("b5", "b7")
-    gap(1, 2)
-    loser(1, 1, "b6")
-    put(0)
+    moved(1, 0)
     link(1, 2)
-    loser_p(1, 2, 1, "b6")
-    put(1)
-    loser(2, 1, "b6")
-    put(2)
-    dma("y", [(T.yrec[:], T.pool[:, 0:V])], [A("pool", 0, V)], [], "sto")
-    tt(blk("y1", 3), blk("u", 2), blk("b6", 5), ALU.add)
-    root(1, 0, 3)
-    root(1, 3)
-    dma("s", [(T.yrt[:], T.r2[:])], [A("r2")], [], "stp")
+    moved(1, 1)
+    both(1)
+    chosen(1)
+    dma("y", [(T.yrec[:], T.outp[:, 0:V])], [A("outp", 0, V)], [], "sto", 3.7)
+    numbers(1)
+    dma("s", [(T.yrt[:], T.r2[:])], [A("r2")], [], "stp", 1.5)
+    emit(g, T, Q, ops)
 
-    seen = {}
+
+def emit(g, T, Q, ops):
+    n, wake = len(ops), OPT["wake"]
+    psum = [sorted({x[0] for x in o[2] + o[3] if SCRATCH[x[0]][0] == "psum"}) for o in ops]
+    seen, dep, soft = {}, [], []
+    for k, o in enumerate(ops):
+        d, s = set(), set()
+        for regs, w in ((o[2], False), (o[3], True)):
+            for name, a, b, st in regs:
+                for a2, b2, st2, j, w2 in seen.get(name, []):
+                    apart = st == 2 and st2 == 2 and (a - a2) % 2
+                    if a < b2 and a2 < b and not apart and (w or w2) and not (o[0] == "p" and ops[j][0] == "p"):
+                        (s if w and not OPT["waw"] and o[0] == ops[j][0] and o[0] in "vs" and not ops[j][4] else d).add(j)
+        dep.append(d)
+        soft.append(s - d)
+        for regs, w in ((o[2], False), (o[3], True)):
+            for name, a, b, st in regs:
+                seen.setdefault(name, []).append((a, b, st, k, w))
+    before = [[(j, ops[j][7] + wake) for j in dep[k]] + [(j, max(ops[j][6], 0.01)) for j in list(soft[k]) + ops[k][8]] for k in range(n)]
+    behind = [[] for _ in range(n)]
+    for k in range(n):
+        for j, gap in before[k]:
+            behind[j].append((k, gap))
+
+    def lay(seq, back):
+        at, used = [0.0] * n, {}
+        for k in seq:
+            q, busy = ops[k][0], ops[k][6]
+            if back:
+                t = max([ops[k][7] - busy] + [at[j] + ops[j][6] + gap - busy for j, gap in behind[k]])
+            else:
+                t = max([0.0] + [at[j] + gap for j, gap in before[k]])
+            if q != "x":
+                spans = [(a, b) for a, b, _ in used.get(q, [])]
+                spans += [(a - wake, b + wake) for bank in psum[k] for a, b, q2 in used.get(bank, []) if q2 != q]
+                for a, b in sorted(spans):
+                    if a < t + busy and t < b:
+                        t = b
+                for r in [q] + psum[k]:
+                    used.setdefault(r, []).append((t, t + busy, q))
+            at[k] = t
+        if back:
+            end = max(at[k] + ops[k][6] for k in range(n))
+            at = [end - at[k] - ops[k][6] for k in range(n)]
+        return at
+
+    if not ORDER:
+        fills = [False] * n
+        for k in range(n):
+            fills[k] = (ops[k][0] == "v" and ops[k][3][0][0] == "outp") or any(fills[j] for j, _ in before[k])
+        best, wait = None, [0.0] * n
+        for _ in range(OPT["rounds"]):
+            rest = [0.0] * n
+            for k in range(n - 1, -1, -1):
+                rest[k] = max([ops[k][7]] + [gap + wait[j] + rest[j] for j, gap in behind[k]])
+            start = lay(sorted(range(n), key=lambda k: (fills[k] and OPT["fill"], -rest[k], k)), False)
+            now = (max(start[k] + ops[k][7] for k in range(n)), start)
+            best = min(best or now, now)
+            for k in range(n):
+                wait[k] += OPT["damp"] * (start[k] - max([0.0] + [start[j] + gap for j, gap in before[k]]) - wait[k])
+        start = best[1]
+        for _ in range(OPT["turns"]):
+            late = lay(sorted(range(n), key=lambda k: (-start[k], -k)), True)
+            start = lay(sorted(range(n), key=lambda k: (late[k], k)), False)
+            best = min(best, (max(start[k] + ops[k][7] for k in range(n)), start))
+        ORDER.extend(sorted(range(n), key=lambda k: (best[1][k], k)))
+        ORDER.append((best, before, psum))
+    order = ORDER[:-1]
     clock = {q: {} for q in Q}
-    done, waits, need = [], [], set()
-    for k, (q, fn, rd, wr, sem, cnt) in enumerate(ops):
-        dep = {}
-        for regs, w in ((rd, False), (wr, True)):
-            for name, a, b in regs:
-                ps = SCRATCH[name][0] == "psum"
-                for a2, b2, j, w2 in seen.get(name, []):
-                    if ps:
-                        hit = ops[j][0] != q
-                    else:
-                        hit = a < b2 and a2 < b and (w or w2)
-                    if hit:
-                        key = ops[j][4] or ops[j][0]
-                        dep[key] = max(dep.get(key, -1), j)
-        wl = []
+    place = {k: i for i, k in enumerate(order)}
+    done, waits, need, held = {}, {}, set(), {}
+    for k in order:
+        q, sem = ops[k][0], ops[k][4]
+        want = {}
+        for j in list(dep[k]) + [j for bank in psum[k] for q2, j in held.get(bank, {}).items() if q2 != q]:
+            key = ops[j][4] or ops[j][0]
+            want[key] = max(want.get(key, -1), place[j])
+        waits[k] = []
         if q != "x":
-            for key, j in sorted(dep.items(), key=lambda e: -e[1]):
-                if clock[q].get(key, -1) < j:
-                    wl.append(j)
-                    need.add(j)
-                    for k2, j2 in done[j].items():
-                        clock[q][k2] = max(clock[q].get(k2, -1), j2)
-        waits.append(wl)
-        d = dict(clock[q]) if q != "x" else {}
-        d[sem or q] = k
-        done.append(d)
-        for name, a, b in rd:
-            seen.setdefault(name, []).append((a, b, k, False))
-        for name, a, b in wr:
-            seen.setdefault(name, []).append((a, b, k, True))
-    tick, n = {}, {}
-    for k, (q, fn, rd, wr, sem, cnt) in enumerate(ops):
+            for key, i in sorted(want.items(), key=lambda e: -e[1]):
+                if clock[q].get(key, -1) < i:
+                    waits[k].append(order[i])
+                    need.add(order[i])
+                    for k2, i2 in done[order[i]].items():
+                        clock[q][k2] = max(clock[q].get(k2, -1), i2)
+        done[k] = dict(clock[q]) if q != "x" else {}
+        done[k][sem or q] = place[k]
+        for bank in psum[k]:
+            held.setdefault(bank, {})[q] = k
+    tick, cnt = {}, {}
+    for k in order:
+        q, sem = ops[k][0], ops[k][4]
         if sem is not None:
-            tick[k] = (sem, cnt)
+            tick[k] = (sem, ops[k][5])
         elif k in need:
-            n[q] = n.get(q, 0) + 1
-            tick[k] = ("c" + q, n[q])
-    for k, (q, fn, rd, wr, sem, cnt) in enumerate(ops):
+            cnt[q] = cnt.get(q, 0) + 1
+            tick[k] = ("c" + q, cnt[q])
+    for k in order:
+        q, fn, sem = ops[k][0], ops[k][1], ops[k][4]
         for j in waits[k]:
             Q[q].wait_ge(T.sem[tick[j][0]], tick[j][1])
         if fn is not None:
             ins = fn()
             if sem is None and k in need:
                 ins.then_inc(T.sem["c" + q], 1)
-    for k, (q, fn, rd, wr, sem, cnt) in enumerate(ops):
-        if sem is not None and k not in need:
-            g.wait_ge(T.sem[sem], cnt)
+    for k in order:
+        if ops[k][4] is not None and k not in need:
+            g.wait_ge(T.sem[ops[k][4]], ops[k][5])

@@ -1,3 +1,4 @@
+import numpy as np
 from concourse.bass import DstId, RemoteDMATransfer
 from concourse.mybir import AluOpType as ALU, ActivationFunctionType as ACT
 
@@ -10,15 +11,22 @@ C = 2048.0
 K = 16384.0
 MAGIC = 12582912.0
 F, B, I, U, HF = "float32", "bfloat16", "int32", "uint16", "float16"
-OPT = {"cmp0": "vv", "c12": "vv", "duel1": "vv", "pieces": (4, 2, 2, 2, 2, 2, 2, 1), "sc": 3.0, "ga": 1.4, "lat": (7.3, 5.7, 4.8, 5.5),
+OPT = {"cmp": "vvvvvs", "duel1": "vv", "pieces": (4, 4, 2, 2, 2, 2, 2, 1),
        "zs": (16, 16), "lt": "vs", "fo": "s", "cut": (((0, 1), (1, 2)), ((0, 1), (1, 2))),
-       "wake": 0.11, "turns": 2, "rounds": 8, "damp": 0.3, "fill": False, "xs": (16, 0), "cy": 0.92, "waw": True,
-       "wb": (("b6", "b4", "b5"), ("b6", "b1", "b3"))}
+       "xs": (16, 0, 0, 0, 0, 0), "rs": (0, 0, 0, 0), "mb": "vv", "other": "pp",
+       "mv": (("b4", "b5"), ("b3", "b2"), ("b4", "b5"), ("b4", "b5"), ("b4", "b5")),
+       "wb": (("b6", "b4", "b5"), ("b6", "b1", "b0")), "seed": 1, "moves": 7000, "warm": 0.006, "aim": 0.3, "late": (0, 0, 0, 0)}
+CYCLE = np.array([0.92, 0.83, 1.0, 1.16, 0.91, 1.0])
+SCATTER = np.array([3.0, 2.5, 3.5, 6.4, 1.65, 3.0])
+GATHER = np.array([1.4, 1.25, 1.56, 2.3, 1.0, 1.5])
+WAKE = (0.11, 0.12, 0.07, 0.1, 0.15, 0.18)
+HOPS = np.array([6.5, 6.6, 5.0, 5.2, 7.6, 9.0])
+SHARE = (0.0, 2 / 52, 1 / 55, 1 / 77, 1 / 56, 1 / 64)
 ORDER = []
 
 
-EYE = (("id1", 1.0), ("idn", -1.0), ("idh", 0.5), ("idi", -0.5), ("idm", -2.0), ("idq", -4.0), ("idk", K / 2), ("idb", 33 / 128),
-       ("idl", -K), ("idj", C / 2), ("idu", -C / 2))
+EYE = (("id1", 1.0), ("idn", -1.0), ("idh", 0.5), ("idi", -0.5), ("idk", K / 2), ("idm", -2.0), ("idq", -4.0), ("idb", 33 / 128),
+       ("idl", -K), ("idx", K), ("idj", C / 2), ("idu", -C / 2))
 EYF = (("idf", 1.0), ("idg", -1.0))
 ALIAS = {"z0": ("pool", LOS[1], H), "cmpb": ("pool", LOS[2], H)}
 ALIAS.update({"lo%d" % o: ("pool", LOS[o], H) for o in range(3)})
@@ -32,7 +40,7 @@ def _sb(n, d):
 
 SCRATCH = {
     "pool": _sb(UB[0] + 32 + 12 * H, B), "outp": _sb(V + H, B), "v1": _sb(6 * H, B), "chw": _sb(V, I), "rti": _sb(128, I),
-    "y3": _sb(H, B), "kx": _sb(96, F), "gx": _sb(144, HF), "alp": _sb(96, F), "lp": _sb(96, F), "cm": _sb(96, B), "cp5": _sb(96, HF),
+    "mf": _sb(H, F), "y3": _sb(H, B), "kx": _sb(96, F), "gx": _sb(144, HF), "alp": _sb(96, F), "lp": _sb(96, F), "cm": _sb(96, B), "cp5": _sb(96, HF),
     "cf": _sb(96, B), "qs": _sb(64, B), "vq": _sb(64, HF), "dmi": _sb(96, F), "ri": _sb(128, F), "te": _sb(96, B),
     "uq": _sb(32, B), "er": _sb(128, B),
     "cmpa": _sb(H, B), "sg": _sb(2 * H, B), "lc": _sb(2 * H, B),
@@ -50,9 +58,9 @@ SCRATCH = {
     "sd": _sb(96, B), "sm": _sb(96, B), "ng": _sb(96, B), "nh": _sb(32, B), "ce": _sb(96, HF), "u3": _sb(32, F),
     "ad": _sb(224, F), "ea": _sb(128, B), "eb": _sb(96, B), "bz": _sb(96, F), "nk0": _sb(128, B), "nk1": _sb(128, B),
     "mm": _sb(192, HF), "ic": _sb(128, B), "fp": _sb(128, F), "xi": _sb(96, HF), "ao": _sb(128, HF),
-    "y0": _sb(64, F), "y1": _sb(64, F), "u0": _sb(96, F), "u1": _sb(96, F), "cc": _sb(128, HF),
-    "xt": _sb(96, F), "x16": _sb(96, U), "y16": _sb(96, U), "rv": _sb(32, F),
-    "p16": _sb(128, U), "l16": _sb(192, U), "fx": _sb(96, B), "alt": _sb(96, F),
+    "y0": _sb(32, F), "y1": _sb(32, F), "yc": _sb(32, HF), "ls": _sb(96, F), "ct": _sb(96, B), "u0": _sb(96, F), "u1": _sb(96, F), "cc": _sb(128, HF),
+    "xt": _sb(96, F), "x16": _sb(96, U), "y16": _sb(96, U), "rv": _sb(128, F),
+    "p16": _sb(128, U), "l16": _sb(192, U), "o16": _sb(64, U), "fx": _sb(96, B), "alt": _sb(96, F),
     "kw": _sb(96, F), "g16": _sb(144, HF), "sa": _sb(16, F), "s16": _sb(16, U), "si": _sb(16, I), "sj": _sb(16, I),
     "lt": _sb(8, B), "lu": _sb(8, B), "lf": _sb(24, F), "t16": _sb(2, U), "q16": _sb(16, U),
 }
@@ -121,7 +129,7 @@ def rank_program(g, core, T, topo):
         for o in wr:
             w += o[1]
             r += o[3] or []
-        ops.append((q, fn, r, w, sem, cnt, busy, busy if done is None else done, list(after)))
+        ops.append((q, fn, r, w, sem, cnt, busy + 0 * CYCLE, (busy if done is None else done) + 0 * CYCLE, list(after)))
 
     def val(o):
         return o[0] if isinstance(o, tuple) else o
@@ -132,14 +140,14 @@ def rank_program(g, core, T, topo):
     def lasts(out, a, b=None, fix=0.03):
         n = out[2]
         if out[3]:
-            return 0.05 + OPT["sc"] * n / 1000
+            return 0.05 + SCATTER * n / 1000
         if a is not None and a[3]:
-            return 0.06 + OPT["ga"] * n / 1000
+            return 0.06 + GATHER * n / 1000
         if b is not None:
             n *= 2 if kind(a)[0] == kind(b)[0] else 1
         elif fix < 0.05 and WIDTH[kind(out)[2]] == 2 and (a is None or WIDTH[kind(a)[2]] == 2):
             n /= 2
-        return fix + max(64, n) * OPT["cy"] / 1000
+        return fix + max(64, n) * CYCLE / 1000
 
     def tt(out, a, b, alu):
         op("v", lambda: g.vector.tensor_tensor(out[0], a[0], b[0], alu), [a, b], [out], lasts(out, a, b))
@@ -169,7 +177,7 @@ def rank_program(g, core, T, topo):
 
     def run(calls):
         bank = calls[0][0][1][0][0]
-        t = sum(max(64, c[2][2]) * (4 if kind(c[1])[2] == F else 1) * OPT["cy"] / 2000 for c in calls)
+        t = sum(max(64, c[2][2]) * (4 if kind(c[1])[2] == F else 1) for c in calls) * CYCLE / 2000
 
         def fn():
             return [g.tensor.matmul(o[0], l[0], r[0], st, sp) for o, l, r, st, sp in calls][-1]
@@ -208,13 +216,13 @@ def rank_program(g, core, T, topo):
         tr, tot = [], 0
         for j, c in enumerate(hs):
             e = topo.engines(core, c)
-            e = e[j * len(e) // 2:(j + 1) * len(e) // 2]
+            e = e[j::2]
             rid, pid = topo.addr(c, core)
             tr.append(RemoteDMATransfer(dst_ids=[DstId(rid=rid, pnc=pid)], dma_engine_mask=bits(e), remote_sem=T.sem["a" + tag],
                                         src=A(src, j * wd, (j + 1) * wd)[0], dst=T[mid][:]))
             tot += len(e)
         op("g", lambda: g.remote_dma_fused(tr, local_sem=T.sem["l" + tag]), [A(src)], [], 0.3, "l" + tag, tot, 2.0)
-        op("x", None, [], [A(MSG[k][3])], 0.0, "a" + tag, sum(n_arr), OPT["lat"][k], [len(ops) - 1])
+        op("x", None, [], [A(MSG[k][3])], 0.0, "a" + tag, sum(n_arr), HOPS + (1.8, 0.0, -0.9, 0.1)[k] + OPT["late"][k] * (np.array(SHARE) == 0), [len(ops) - 1])
 
     def blk(name, o, n=1):
         return A(name, 32 * o, 32 * (o + n))
@@ -244,8 +252,8 @@ def rank_program(g, core, T, topo):
     def given(off, c, d):
         return X("pool", P0 - 16, P0 + V, off, c, d)
 
-    def count(bank, cmp, signs, out16, flag, nk=None):
-        out, c = A(bank, 0, 32), (15 / 64 if nk is None else 63 / 128) + signs / 4
+    def count(out, cmp, signs, out16, flag, nk=None):
+        c = (15 / 64 if nk is None else 63 / 128) + signs / 4
         lin(out, [("id1", A("j2"))] + ([] if nk is None else [("idb", nk)]), True, False)
         wrap(out, "bd" if signs else "bc", 0, cmp)
         ts(out16, out, c, ALU.add)
@@ -265,7 +273,7 @@ def rank_program(g, core, T, topo):
         else:
             act(pair(t, o - 1, 0), pick(t, o - 2, "ml16", 32 * o - 64, 32 * o - 32))
             tt(A(cmp), pick(t, o - 2, "ml16", 32 * o - 64, 32 * o - 32), root(t, o), ALU.is_gt)
-        count("b1", cmp, signs, blk("ml16", o - 1), blk("sd", o - 1))
+        count(blk("b1", (15, 8, 0)[o - 1]), cmp, signs, blk("ml16", o - 1), blk("sd", o - 1))
 
     def third(t):
         (r, at), s1, s2, one = (("ad", 3), ("ao", 0))[t], blk("sd", 0), blk("sd", 1), blk("one", 0)
@@ -285,32 +293,32 @@ def rank_program(g, core, T, topo):
                 tt(blk("vq", k), blk("qs", k), blk("b7", 5), ALU.mult)
                 late[k] = [("id1", blk("vq", k))]
         lin(blk("b6", 13), [(("idf", "id1")[t], blk(r, at + 3))] + [("idn", blk("ce", o)) for o in range(3)] + late[0])
-        lin(blk("b2", 0), [("id1", blk("ce", o)) for o in range(3)] + late[1], True, False)
+        lin(blk("b0", 0), [("id1", blk("ce", o)) for o in range(3)] + late[1], True, False)
         if t:
-            for o in range(3):
-                lin(blk("b3", 10 + o), [("id1", blk("qs", 1)), ("idi", blk("nk0", o))] + [[("idm", one), ("idn", one)], [("idm", one)], [("idn", one)]][o]
-                    + [("id1", blk("sm", p)) for p in range(o + 1, 3)])
-            act(A("te"), blk("b3", 10, 3))
+            lin(blk("b6", 10, 3), [("id1", A("ct")), ("idi", blk("nk0", 0, 3))], True, False)
+            run([(blk("b6", 10, 3 - p), A("id1"), blk("sm", p, 3 - p), False, False) for p in (1, 2)]
+                + [(blk("b6", 10 + o), A("id1"), blk("qs", 1), False, o == 2) for o in range(3)])
+            act(A("te"), blk("b6", 10, 3))
 
     def crowned(t):
         one = blk("one", 0)
         tt(A("u3"), blk("sd", 2), blk("b6", 13), ALU.mult)
-        mm(blk("b2", 0), A("idf"), A("u3"), False, True)
-        ts(blk("m16", t), blk("b2", 0), C, ALU.add)
+        mm(blk("b0", 0), A("idf"), A("u3"), False, True)
+        ts(blk("m16", t), blk("b0", 0), C, ALU.add)
         ts(A("kg"), X("chw", 0, V, "m16", 32 * t, 32 * t + 32), A("pf", 5, 6), ALU.subtract)
-        act(blk("y%d" % t, 0), blk("b2", 0))
-        for o in range(3):
-            lin(blk("b1", 1 + o), [("idn", blk("sd", j)) for j in range(o, 3)])
+        act(blk("y%d" % t, 0), blk("b0", 0))
+        run([(blk("b1", 1, 3 - j), A("idn"), blk("sd", j, 3 - j), j == 0, j == 2) for j in range(3)])
         act(A("ng"), blk("b1", 1, 3), ACT.Sign, 0.5)
         if t:
             tt(A("uq"), blk("sd", 2), blk("b6", 14), ALU.mult)
-            for o in range(3):
-                lin(blk("b1", 12 + o), [("idk" if o else "idl", x) for x in (blk("te", o), A("uq")) * (1 + (o > 0))])
+            lin(blk("b1", 12), [("idl", blk("te", 0)), ("idl", A("uq"))])
+            run([(blk("b1", 13, 2), A("idx"), blk("te", 1, 2), True, False)] + [(blk("b1", 12 + o), A("idx"), A("uq"), False, o == 2) for o in (1, 2)])
             tt(blk("alp", 0), blk("b1", 12), blk("lp", 0), ALU.max)
             tt(blk("alp", 1, 2), blk("b1", 13, 2), blk("lp", 1, 2), ALU.min)
-        lin(blk("b1", 4), [("idi", one), ("idi", blk("ng", 0)), ("id1", blk("er", 0))])
-        lin(blk("b1", 5, 2), [("idh", blk("ng", 0, 2)), ("idi", blk("ng", 1, 2)), ("id1", blk("er", 1, 2))])
-        lin(blk("b1", 7), [("idi", one), ("idh", blk("ng", 2)), ("id1", blk("er", 3))])
+            act(blk("fx", 0), blk("b1", 12), ACT.Relu, 0.5, -1 / K)
+            act(blk("fx", 1, 2), blk("b1", 13, 2), ACT.Relu, 0.5, 1 / K)
+        run([(blk("b1", 4, 4), A("id1"), A("er"), True, False), (blk("b1", 4, 3), A("idi"), A("ng"), False, False),
+             (blk("b1", 5, 3), A("idh"), A("ng"), False, False), (blk("b1", 4), A("idi"), one, False, False), (blk("b1", 7), A("idi"), one, False, True)])
         act(A("ea"), blk("b1", 4, 4), ACT.Relu)
         for o in range(3):
             out, w = blk(OPT["wb"][t][o], 8 + o), ("idk", "idl")[t]
@@ -321,19 +329,15 @@ def rank_program(g, core, T, topo):
             else:
                 act(blk("kw", o), out)
         if t:
-            for o in range(3):
-                lin(blk("b1", 1 + o), [("id1", blk("te", o)), ("id1", A("uq")), ("idh", one)])
-            act(A("fx"), blk("b1", 1, 3), ACT.Relu)
-            lin(blk("b1", 4, 3), [("idg", A("u0")), ("idg", A("lp")), ("idn", A("cm"))], True, False)
-            run([(blk("b1", 4), A("idf"), blk("y0", 0), False, False), (blk("b1", 5, 2), A("idf"), blk("u0", 0, 2), False, False),
-                 (blk("b1", 5, 2), A("id1"), blk("xi", 0, 2), False, True)])
-            tt(A("alt"), A("fx"), blk("b1", 4, 3), ALU.mult)
+            lin(blk("b1", 1, 3), [("idg", A("lp")), ("idn", A("cm")), ("idf", A("ls"))])
+            tt(A("alt"), A("fx"), blk("b1", 1, 3), ALU.mult)
             lin(blk("b1", 12, 3), [("idf", A("kw")), ("idf", A("alt"))])
             act(A("kx"), blk("b1", 12, 3))
 
     def sendz(t):
         n = OPT["zs"][t]
-        cp(A("z%d" % t, 0, 16 * n), pick(t, 2, "ml16", 64, 64 + n))
+        if n:
+            cp(A("z%d" % t, 0, 16 * n), pick(t, 2, "ml16", 64, 64 + n))
         act(A("z%d" % t, 16 * n, H), pick(t, 2, "ml16", 64 + n, 96))
         send(1 + 2 * t)
 
@@ -376,7 +380,7 @@ def rank_program(g, core, T, topo):
             cp(blk("x16", o, n), blk("xt", o, n))
         for o in range(3):
             lo, hi = (0, P0 + V + H * o) if t else (P0, pair(0, 1)[2])
-            n = OPT["xs"][t] if o == 0 else 0
+            n = OPT["xs"][3 * t + o]
             if n:
                 cp(first(t, o, 0, 16 * n), X("pool", lo, hi, "x16", 32 * o, 32 * o + n))
             act(first(t, o, 16 * n, H), X("pool", lo, hi, "x16", 32 * o + n, 32 * o + 32))
@@ -397,9 +401,12 @@ def rank_program(g, core, T, topo):
         lin(blk(bk, 9, 2), [("idh", blk(nk, 1, 2)), ("idi", blk(nk, 0, 2))])
         lin(blk(bk, 11), [("idh", blk("one", 0)), ("idi", blk(nk, 3))])
         act(A("ic"), blk(bk, 8, 4))
-        lin(blk(bk, 12, 3), [("idh", blk(nk, 0, 3)), ("idh", A("eb")), ("id1", blk("ea", 0, 3))])
-        mm(blk(bk, 15), A("id1"), blk("ea", 3))
-        if t == 0:
+        if t:
+            run([(blk(bk, 12, 4), A("idx"), A("ea"), True, False), (blk(bk, 12, 3), A("idk"), blk(nk, 0, 3), False, False),
+                 (blk(bk, 12, 3), A("idk"), A("eb"), False, False), (blk(bk, 12, 4), A("idf"), blk("ad", 3, 4), False, True)])
+        else:
+            lin(blk(bk, 12, 3), [("idh", blk(nk, 0, 3)), ("idh", A("eb")), ("id1", blk("ea", 0, 3))])
+            mm(blk(bk, 15), A("id1"), blk("ea", 3))
             tt(A("fp"), A("al"), blk(bk, 12, 4), ALU.mult)
             lin(blk(bk, 8, 4), [("idk", A("ic")), ("idn", A("wb"))])
             tt(A("hi"), A("fp"), blk(bk, 8, 4), ALU.add)
@@ -410,6 +417,9 @@ def rank_program(g, core, T, topo):
         lin(blk("b7", 0, 3), [(("idg", "idf")[t], A("bz")), (w, one), (w, A("eb"))], True, False)
         lin(blk("b7", 0, 3), [("id1", blk("mm", 0, 3)), ("id1", blk("mm", 3, 3))], False, True)
         cp(A("xi"), blk("b7", 0, 3))
+        if t:
+            act(A("fp"), blk(bk, 12, 4), ACT.Relu, C - K)
+            return
         tt(A("ao"), blk("ad", 3, 4), blk(bk, 12, 4), ALU.mult)
         lin(blk(bk, 8, 3), [("idh", blk(nk, 0, 3)), ("idh", A("eb")), ("id1", blk("ea", 0, 3)), ("id1", blk("ic", 0, 3))])
         lin(blk(bk, 11), [("id1", blk("ea", 3)), ("id1", blk("ic", 3))])
@@ -418,16 +428,22 @@ def rank_program(g, core, T, topo):
     def halve(t):
         z, w = A("z%d" % t), A("w%d" % t)
         lin(A("b2"), [("idw", z), ("idw", w)])
-        ts(second(t, 0), A("b2"), MAGIC, ALU.add, MAGIC, ALU.subtract)
+        if OPT["mb"][t] == "v":
+            ts(second(t, 0), A("b2"), MAGIC, ALU.add, MAGIC, ALU.subtract)
+        else:
+            act(A("mf"), A("b2"), ACT.Identity, MAGIC)
+            act(second(t, 0), A("mf"), ACT.Identity, -MAGIC)
 
     def link(t, o):
         y, u, nk = "y%d" % t, "u%d" % t, "nk%d" % t
-        signs = OPT["c12" if o else "cmp0"][t] == "s"
+        signs = OPT["cmp"][3 * t + o] == "s"
         if o:
             carry = pick(t, 2 + o, "y16", 32 * o - 32, 32 * o)
             act(second(t, o), carry)
             if signs:
                 signed("cmpa", "b3", [("id1", first(t, o)), ("idn", second(t, o))], -0.5)
+                if o == 2:
+                    act(A("dw", 1, 2 * H, 2), A("b3"), ACT.Sign, None, -1.0)
             else:
                 tt(A("cmpa"), carry, first(t, o), ALU.is_lt)
         elif signs:
@@ -435,9 +451,9 @@ def rank_program(g, core, T, topo):
         else:
             lin(A("b3"), [("idh", A("z%d" % t)), ("idh", A("w%d" % t))])
             tt(A("cmpa"), first(t, 0), A("b3"), ALU.is_gt)
-        c = count("b0", "cmpa", signs, blk("y16", o), blk("sm", o), blk(nk, o))
+        c = count(blk("b0", 5 + o), "cmpa", signs, blk("y16", o), blk("sm", o), blk(nk, o))
         if t == 0:
-            newroot(o + 1, A("b0", 0, 32), c)
+            newroot(o + 1, blk("b0", 5 + o), c)
         now = [("id1", blk("xi", o - 1)), ("idf", blk(u, o - 1))] if o else [("idf", blk(y, 0))]
         lin(blk("b7", 3), [("idn", blk("xi", o))] + now)
         tt(blk(u, o), blk("sm", o), blk("b7", 3), ALU.mult)
@@ -445,22 +461,29 @@ def rank_program(g, core, T, topo):
             lin(blk("b7", 5), [("id1", blk("xi", o)), ("idf", blk(u, o))])
         lin(blk("b7", 4), now + [("idg", blk(u, o))])
         ts(blk("l16", 3 * t + o), blk("b7", 4), C, ALU.add)
+        if t == 0:
+            act(blk("ls", o), blk("b7", 4))
         if o == 2:
-            act(blk(y, 1), blk("b7", 5))
+            (act if t else cp)(A(("yc", "u3")[t]), blk("b7", 5))
 
     def newroot(o, place, c):
-        tt(A("rv"), place, blk("hi", o), ALU.min)
-        ts(blk("p16", o), A("rv"), pair(0, 3 + max(o - 1, 0))[1] - UB[0] + c, ALU.add)
-        act(root(1, o), kept(o, "p16", 32 * o, 32 * o + 32))
+        tt(blk("rv", o), place, blk("hi", o), ALU.min)
+        ts(blk("p16", o), blk("rv", o), pair(0, 3 + max(o - 1, 0))[1] - UB[0] + c, ALU.add)
+        n = OPT["rs"][o]
+        if n:
+            cp(root(1, o, 0, 16 * n), kept(o, "p16", 32 * o, 32 * o + n))
+        act(root(1, o, 16 * n, H), kept(o, "p16", 32 * o + n, 32 * o + 32))
 
     def numbers(t):
-        for o in range(4):
-            mm(blk("b7", 6 + o), A("idf"), blk("y%d" % t, 1))
-        tt(A("cc"), A("ic"), blk("b7", 6, 4), ALU.mult)
         if t:
-            lin(blk("b7", 10, 4), [("id1", A("ao")), ("idj", A("er")), ("idj", A("er")), ("id1", A("cc"))])
-            act(A("r2"), blk("b7", 10, 4))
+            lin(blk("b1", 0, 4), [("idx", A("ic"))], True, False)
+            run([(blk("b1", o), A("idf"), A("u3"), False, o == 3) for o in range(4)])
+            act(A("hi"), blk("b1", 0, 4), ACT.Relu, C - K)
+            lin(blk("b1", 4, 4), [("idf", A("fp")), ("idf", A("hi"))])
+            act(A("r2"), blk("b1", 4, 4))
         else:
+            run([(blk("b7", 6 + o), A("id1"), A("yc"), True, True) for o in range(4)])
+            tt(A("cc"), A("ic"), blk("b7", 6, 4), ALU.mult)
             lin(blk("b7", 10, 4), [("id1", A("ao")), ("id1", A("cc"))])
             act(blk("ad", 3, 4), blk("b7", 10, 4))
 
@@ -479,20 +502,29 @@ def rank_program(g, core, T, topo):
         x, y, w = first(t, o), second(t, o), second(t, o + 1) if o < 2 else A("y3")
         if o == 2:
             act(w, pick(t, 5, "y16", 64, 96))
-        lin(A("b4"), [("id1", x), ("id1", y), ("idm", w)])
-        act(big("sg", o % 2), A("b4"), ACT.Sign, None, -1.0)
-        if t == 0:
-            lin(A("b5"), [("id1", x), ("id1", y), ("idn", w), ("id1", big("sg", o % 2))])
-            act(A("lo%d" % o), A("b5"))
-            return put_lost(o)
-        lin(A("b5"), [("id1", x), ("id1", y), ("idn", w)])
-        act(big("lc", o), A("b5"))
+        if t and OPT["other"][o] == "g":
+            lin(blk("b7", 14 + o), [("id1", A("j2")), ("id1", blk("one", 0)), ("idn", blk("sm", o))])
+            cp(blk("o16", o), blk("b7", 14 + o))
+            act(big("lc", o), pick(t, 3 + o, "o16", 32 * o, 32 * o + 32))
+            lin(A("b4"), [("id1", w), ("idn", big("lc", o))])
+            act(big("sg", o), A("b4"), ACT.Sign)
+        else:
+            bd, bl = [A(b) for b in OPT["mv"][3 * t + o]]
+            lin(bd, [("id1", x), ("id1", y), ("idm", w)])
+            act(big("sg", o % 2), bd, ACT.Sign, None, -1.0)
+            if t == 0:
+                lin(bl, [("id1", x), ("id1", y), ("idn", w), ("id1", big("sg", o % 2))])
+                act(A("lo%d" % o), bl)
+                return put_lost(o)
+            lin(bl, [("id1", x), ("id1", y), ("idn", w)])
+            act(big("lc", o), bl)
         put(t, "l16", 32 * (3 * t + o), lambda dst, a, b: tt(dst, A("lc", H * o + a, H * o + b), A("sg", H * o + a, H * o + b), ALU.add), 1)
 
     def both(t):
         x, y = first(t, 2), second(t, 2)
-        lin(A("b4"), [("idn", x), ("id1", y)])
-        act(A("dw", 1, 2 * H, 2), A("b4"), ACT.Sign)
+        if OPT["cmp"][5] == "v":
+            lin(A("b4"), [("idn", x), ("id1", y)])
+            act(A("dw", 1, 2 * H, 2), A("b4"), ACT.Sign)
         lin(A("b5"), [("idn", x), ("id1", y), ("idn", A("dw", 1, 2 * H, 2))])
         act(A("dw", 0, 2 * H, 2), A("b5"))
 
@@ -511,8 +543,8 @@ def rank_program(g, core, T, topo):
     iota(A("m2"), [[-16, 2], [32, 8], [1, 16]], 0, 0)
     iota(A("dmi"), [[0, 3], [16, 32]], int(V - C), 0)
     iota(A("chw", 2560, V), [[0, 512]], 0, 0)
-    for a in range(0, 2560, 512):
-        ms(A("chw", a, a + 512), 0)
+    for a in range(0, 1280, 640):
+        ms(A("chw", a, a + 640), 0)
     ts(A("pc", 1, 2), A("pc", 0, 1), 15, ALU.bitwise_and)
     ts(A("pc", 2, 3), A("pc", 0, 1), 4, ALU.logical_shift_right)
     cp(A("pf", 0, 3), A("pc", 0, 3))
@@ -521,55 +553,45 @@ def rank_program(g, core, T, topo):
     ts(A("id1"), A("t1", 0, 128), A("pf", 0, 1), ALU.is_equal)
     ts(A("bc"), A("t1"), A("pf", 4, 5), ALU.is_equal, 1 / 32, ALU.mult)
     ts(A("pf", 6, 7), A("pf", 1, 2), 2.0, ALU.mult)
-    if "s" in OPT["cmp0"] + OPT["c12"] + OPT["duel1"]:
-        ts(A("bd"), A("bc"), 0.5, ALU.mult)
     ts(A("blk"), A("blki"), A("pf", 2, 3), ALU.is_equal)
     ts(A("rz"), A("rti"), 0.0, ALU.is_gt, 16.0, ALU.mult)
     tt(A("ri"), A("rz"), A("rti"), ALU.add)
     cp(A("r16"), A("ri"))
     cp(A("e16"), A("ri", 0, 128, 32))
     ts(blk("ad", 3, 4), A("rti"), C, ALU.subtract)
-    ts(blk("ad", 0, 3), A("dmi"), A("pf", 1, 2), ALU.add)
     ms(A("pool", P0 - 16, P0), 256.0)
     act(A("al"), A("ali"), ACT.Identity, A("pf", 6, 7))
     ts(A("j2"), blk("al", 0), 32.0, ALU.subtract)
-    for k, c in enumerate((15 / 64, 31 / 64, 63 / 128, 95 / 128)):
-        act(blk("th", k), blk("al", 0), ACT.Identity, 0.5 - c - 32)
-    act(A("jc"), blk("al", 0), ACT.Identity, -31.0)
-    for o, n in ((0, 2), (2, 1), (3, 1)):
-        ts(blk("wb", o, n), A("t1", 0, 32 * n), 0.0, ALU.mult, float(pair(0, 3 + max(o - 1, 0))[1] - UB[0]), ALU.add)
-    for name, c in EYE[1:] + EYF:
+    act(blk("th", 0), blk("al", 0), ACT.Identity, 0.5 - 15 / 64 - 32)
+    for name, c in EYE[1:4] + EYF:
         act(A(name), A("id1"), ACT.Copy, None, c)
     fill(A("one"), 1.0)
-    dma("y", [(T.chw[16 * k:16 * k + 3, :], T.ch[k]) for k in range(8)], [A("pool", P0, P0 + 16)], [A("chw")], "lch", 2.5)
     ts(A("rm", 0, 3), A("t1", 0, 3), A("pf", 1, 2), ALU.is_equal)
     for o in range(3):
         ts(A("bo", 144 * o, 144 * o + 144), A("t1"), A("pf", 4, 5), ALU.is_equal, A("rm", o, o + 1), ALU.mult)
-        act(blk("lp", o), blk("al", 0), ACT.Identity, LOS[o] - P0 - 16 - MID[o], 0.5)
-    for o, n in ((0, 1), (1, 2)):
-        fill(blk("cm", o, n), MID[o] - C)
-    ts(A("c15"), A("cm"), C, ALU.add)
-    ts(A("cp5"), A("cm"), C + P0, ALU.add)
     ts(A("pf", 5, 6), A("rm", 0, 1), MID[0] - MID[1], ALU.mult, MID[1], ALU.add)
-    act(A("xp"), blk("al", 0, 3), ACT.Identity, float(UB[0] - P0))
     act(A("er"), A("ri"), ACT.Sign)
-    for a, b, c in ((0, 1, 0.0), (1, 2, 1.0), (2, 4, 3.0)):
-        fill(blk("cl", a, b - a), c)
+    for out, c in ((A("lf", 16, 24), 2), (blk("cm", 0), MID[0] - C), (blk("cm", 1, 2), MID[1] - C), (blk("cl", 0), 0), (blk("cl", 1), 1),
+                   (blk("cl", 2, 2), 3), (A("pool", UB[0], UB[0] + 32), 256), (A("pool", 0, 32), 256)):
+        fill(out, float(c))
     fill(A("lui"), 3.0)
     for a, b, st, c in ((0, 8, 1, 0.0), (16, 32, 2, 2.0), (32, 64, 8, 1.0), (33, 64, 8, 1.0), (36, 64, 8, 2.0), (38, 64, 8, 2.0)):
         fill(A("lui", a, b, st), c)
     ts(A("pf", 7, 8), A("pf", 1, 2), 3.0, ALU.min, 4.0, ALU.mult)
     act(A("lut"), A("lui"), ACT.Identity, A("pf", 7, 8))
-    fill(A("lf", 16, 24), 2.0)
     ts(A("idw"), A("id1"), 1023 / 2048, ALU.mult)
-    for none in (A("pool", UB[0], UB[0] + 32), A("pool", 0, 32)):
-        fill(none, 256.0)
     ts(A("csh", 0, 12), A("cvi"), A("pf", 1, 2), ALU.add, 16.0, ALU.mult)
     ts(A("csh", 12, 16), A("t1", 0, 4), 0.0, ALU.mult)
 
     act(A("eo"), given("e16", 0, 4))
     early = len(ops) - 1
     send(0)
+    sent = len(ops) - 2
+    iota(A("chw", 1280, 2560), [[0, 1280]], 0, 0)
+    ops[-1][8].append(sent)
+    iota(A("ct"), [[1, 3], [0, 32]], -3, 0)
+    ops[-1][8].append(len(ops) - 2)
+    dma("y", [(T.chw[16 * k:16 * k + 3, :], T.ch[k]) for k in range(8)], [], [A("chw")], "lch", 2.5)
     cp(root(0, 0, 0, 320), given("r16", 0, 20))
     act(root(0, 0, 320, H), given("r16", 20, 32))
     ops[-1][8].append(early)
@@ -580,7 +602,26 @@ def rank_program(g, core, T, topo):
     third(0)
     duel(0, 3, "cmpa")
     sendz(0)
-    dma("y", [(T.outp[:, 0:V], T.rec[:])], [A("z0")], [A("outp", 0, V)], "lout", 5.0)
+    ops[-2][3].append(("outp", 0, V, None))
+    dma("y", [(T.outp[:, 0:V], T.rec[:])], [], [A("outp", 0, V)], "lout", 4.2)
+    gate = len(ops) - 4
+    for name, c in EYE[4:]:
+        act(A(name), A("id1"), ACT.Copy, None, c)
+    for k, c in ((1, 31 / 64), (2, 63 / 128), (3, 95 / 128)):
+        act(blk("th", k), blk("al", 0), ACT.Identity, 0.5 - c - 32)
+    act(A("jc"), blk("al", 0), ACT.Identity, -31.0)
+    act(A("xp"), blk("al", 0, 3), ACT.Identity, float(UB[0] - P0))
+    act(blk("ad", 0, 3), A("dmi"), ACT.Identity, A("pf", 1, 2))
+    for o in range(3):
+        act(blk("lp", o), blk("al", 0), ACT.Identity, LOS[o] - P0 - 16 - MID[o], 0.5)
+    for o, n in ((0, 2), (2, 1), (3, 1)):
+        ts(blk("wb", o, n), A("t1", 0, 32 * n), 0.0, ALU.mult, float(pair(0, 3 + max(o - 1, 0))[1] - UB[0]), ALU.add)
+    ts(A("c15"), A("cm"), C, ALU.add)
+    ts(A("cp5"), A("cm"), C + P0, ALU.add)
+    if "s" in OPT["cmp"] + OPT["duel1"]:
+        ts(A("bd"), A("bc"), 0.5, ALU.mult)
+    for o in ops[gate + 4:]:
+        o[8].append(gate)
     crowned(0)
     shift(0)
     structure(0)
@@ -616,79 +657,130 @@ def rank_program(g, core, T, topo):
     moved(1, 1)
     both(1)
     chosen(1)
-    dma("y", [(T.yrec[:], T.outp[:, 0:V])], [A("outp", 0, V)], [], "sto", 3.7)
     numbers(1)
-    dma("s", [(T.yrt[:], T.r2[:])], [A("r2")], [], "stp", 1.5)
+    dma("y", [(T.yrt[:], T.r2[:])], [A("r2")], [], "stp", 1.5)
+    dma("y", [(T.yrec[:], T.outp[:, 0:V])], [A("outp", 0, V)], [], "sto", 3.7)
+    ops[-1][8].append(len(ops) - 2)
     emit(g, T, Q, ops)
 
 
+def arrange(ops, dep, psum):
+    n, qs, speeds = len(ops), [o[0] for o in ops], range(len(WAKE))
+    busy = [[float(o[6][m]) for o in ops] for m in speeds]
+    done = [[float(o[7][m]) for o in ops] for m in speeds]
+    before = [[[(j, done[m][j] + WAKE[m]) for j in sorted(dep[k])] + [(j, max(busy[m][j], 0.01)) for j in ops[k][8]]
+               for k in range(n)] for m in speeds]
+
+    ends = [k for k in range(n) if ops[k][4]]
+
+    def lay(rank):
+        for k in range(n):
+            for j, _ in before[0][k]:
+                if rank[j] >= rank[k]:
+                    rank[k] = rank[j] + 1e-6
+        at, used, wake = [0.0] * n, {}, WAKE[0]
+        for k in sorted(range(n), key=lambda k: rank[k]):
+            q, t = qs[k], 0.0
+            for j, gap in before[0][k]:
+                if at[j] + gap > t:
+                    t = at[j] + gap
+            if q != "x":
+                spans = [x for x in used.get(q, [])[-40:] if x[1] > t]
+                for bank in psum[k]:
+                    spans += [(a - wake, b + wake, q2) for a, b, q2 in used.get(bank, [])[-20:] if q2 != q and b + wake > t]
+                for a, b, _ in sorted(spans):
+                    if a >= t + busy[0][k]:
+                        break
+                    t = max(t, b)
+                for r in [q] + psum[k]:
+                    used.setdefault(r, []).append((t, t + busy[0][k], q))
+            at[k] = t
+        return at
+
+    def length(at, was=None):
+        order, held, edges, parts = sorted(range(n), key=lambda k: (at[k], k)), {}, [None] * n, []
+        for k in order:
+            edges[k] = (held.get(qs[k]), [j for bank in psum[k] for q, j in held.setdefault(bank, {}).items() if q != qs[k]])
+            if qs[k] != "x":
+                held[qs[k]] = k
+            for bank in psum[k]:
+                held[bank][qs[k]] = k
+        for m in speeds[1:]:
+            now, bm, wake = [0.0] * n, busy[m], WAKE[m]
+            for k in order:
+                j, banks = edges[k]
+                t = 0.0 if j is None else now[j] + bm[j]
+                for j, gap in before[m][k]:
+                    if now[j] + gap > t:
+                        t = now[j] + gap
+                for j in banks:
+                    if now[j] + bm[j] + wake > t:
+                        t = now[j] + bm[j] + wake
+                now[k] = t
+            parts.append(max(now[k] + done[m][k] for k in ends) * SHARE[m])
+            if was and sum(parts) > sum(was[:m]) + 0.015:
+                return None
+            k = max(ends, key=lambda k: now[k] + done[m][k])
+            while now[k] > 4:
+                j = max(before[m][k], key=lambda e: now[e[0]] + e[1], default=None)
+                if j is None or now[j[0]] + j[1] < now[k] - 1e-9:
+                    j = (max([i for i in [edges[k][0]] + edges[k][1] if i is not None], key=lambda i: now[i] + bm[i]),)
+                    held.setdefault("late", []).append((k, j[0]))
+                k = j[0]
+        return parts + [held.get("late", [])]
+
+    best, wait = None, [0.0] * n
+    for _ in range(8):
+        rest = list(done[0])
+        for k in range(n - 1, -1, -1):
+            for j, gap in before[0][k]:
+                rest[j] = max(rest[j], gap + wait[k] + rest[k])
+        at = lay([-r for r in rest])
+        parts = length(at)
+        best = min(best or (1e9,), (sum(parts[:-1]), at, parts))
+        for k in range(n):
+            wait[k] += 0.3 * (at[k] - max([0.0] + [at[j] + gap for j, gap in before[0][k]]) - wait[k])
+    draw, (now, at, was) = np.random.RandomState(OPT["seed"]), best
+    for i in range(OPT["moves"]):
+        rank = list(at)
+        for _ in range(2):
+            k, by = int(draw.randint(n)), float(draw.uniform(-1.5, 1.5))
+            if draw.rand() < OPT["aim"]:
+                k, j = was[-1][draw.randint(len(was[-1]))]
+                by = at[j] - at[k] - 0.01 - float(draw.exponential(0.3))
+                if draw.rand() < 0.5:
+                    k, by = j, -by
+            rank[k] += by
+            while before[0][k] and by < 0 and draw.rand() < 0.6:
+                k = max(before[0][k], key=lambda e: at[e[0]] + e[1])[0]
+                rank[k] += by
+        new = lay(rank)
+        parts = length(new, was)
+        if parts and sum(parts[:-1]) <= now + OPT["warm"] * (1 - i / OPT["moves"]) * draw.rand():
+            now, at, was = sum(parts[:-1]), new, parts
+            best = min(best, (now, at, was))
+    return sorted(range(n), key=lambda k: (best[1][k], k)) + [[round(p / s, 2) for p, s in zip(best[2], SHARE[1:])]]
+
+
 def emit(g, T, Q, ops):
-    n, wake = len(ops), OPT["wake"]
+    n = len(ops)
     psum = [sorted({x[0] for x in o[2] + o[3] if SCRATCH[x[0]][0] == "psum"}) for o in ops]
-    seen, dep, soft = {}, [], []
+    seen, dep = {}, []
     for k, o in enumerate(ops):
-        d, s = set(), set()
+        d = set()
         for regs, w in ((o[2], False), (o[3], True)):
             for name, a, b, st in regs:
                 for a2, b2, st2, j, w2 in seen.get(name, []):
                     apart = st == 2 and st2 == 2 and (a - a2) % 2
                     if a < b2 and a2 < b and not apart and (w or w2) and not (o[0] == "p" and ops[j][0] == "p"):
-                        (s if w and not OPT["waw"] and o[0] == ops[j][0] and o[0] in "vs" and not ops[j][4] else d).add(j)
+                        d.add(j)
         dep.append(d)
-        soft.append(s - d)
         for regs, w in ((o[2], False), (o[3], True)):
             for name, a, b, st in regs:
                 seen.setdefault(name, []).append((a, b, st, k, w))
-    before = [[(j, ops[j][7] + wake) for j in dep[k]] + [(j, max(ops[j][6], 0.01)) for j in list(soft[k]) + ops[k][8]] for k in range(n)]
-    behind = [[] for _ in range(n)]
-    for k in range(n):
-        for j, gap in before[k]:
-            behind[j].append((k, gap))
-
-    def lay(seq, back):
-        at, used = [0.0] * n, {}
-        for k in seq:
-            q, busy = ops[k][0], ops[k][6]
-            if back:
-                t = max([ops[k][7] - busy] + [at[j] + ops[j][6] + gap - busy for j, gap in behind[k]])
-            else:
-                t = max([0.0] + [at[j] + gap for j, gap in before[k]])
-            if q != "x":
-                spans = [(a, b) for a, b, _ in used.get(q, [])]
-                spans += [(a - wake, b + wake) for bank in psum[k] for a, b, q2 in used.get(bank, []) if q2 != q]
-                for a, b in sorted(spans):
-                    if a < t + busy and t < b:
-                        t = b
-                for r in [q] + psum[k]:
-                    used.setdefault(r, []).append((t, t + busy, q))
-            at[k] = t
-        if back:
-            end = max(at[k] + ops[k][6] for k in range(n))
-            at = [end - at[k] - ops[k][6] for k in range(n)]
-        return at
-
     if not ORDER:
-        fills = [False] * n
-        for k in range(n):
-            fills[k] = (ops[k][0] == "v" and ops[k][3][0][0] == "outp") or any(fills[j] for j, _ in before[k])
-        best, wait = None, [0.0] * n
-        for _ in range(OPT["rounds"]):
-            rest = [0.0] * n
-            for k in range(n - 1, -1, -1):
-                rest[k] = max([ops[k][7]] + [gap + wait[j] + rest[j] for j, gap in behind[k]])
-            start = lay(sorted(range(n), key=lambda k: (fills[k] and OPT["fill"], -rest[k], k)), False)
-            now = (max(start[k] + ops[k][7] for k in range(n)), start)
-            best = min(best or now, now)
-            for k in range(n):
-                wait[k] += OPT["damp"] * (start[k] - max([0.0] + [start[j] + gap for j, gap in before[k]]) - wait[k])
-        start = best[1]
-        for _ in range(OPT["turns"]):
-            late = lay(sorted(range(n), key=lambda k: (-start[k], -k)), True)
-            start = lay(sorted(range(n), key=lambda k: (late[k], k)), False)
-            best = min(best, (max(start[k] + ops[k][7] for k in range(n)), start))
-        ORDER.extend(sorted(range(n), key=lambda k: (best[1][k], k)))
-        ORDER.append((best, before, psum))
-    order = ORDER[:-1]
+        ORDER.extend(arrange(ops, dep, psum))
+    order = ORDER[:n]
     clock = {q: {} for q in Q}
     place = {k: i for i, k in enumerate(order)}
     done, waits, need, held = {}, {}, set(), {}

import numpy as np
from concourse.bass import DstId, RemoteDMATransfer
from concourse.mybir import AluOpType as ALU, ActivationFunctionType as ACT

V, H = 3072, 512
P0 = 32 + 7 * H + 16
UB = (P0 + V + 2 * H, 0)
LOS = (P0 - 16 - H, P0 + V, P0 + V + H)
MID = (1520.0, 2048.0, 2048.0)
C = 2048.0
K = 16384.0
MAGIC = 12582912.0
F, B, I, U, HF = "float32", "bfloat16", "int32", "uint16", "float16"
OPT = {"cmp": "vvvvvs", "duel1": "vv", "pieces": (4, 4, 2, 2, 2, 2, 2, 1),
       "zs": (16, 16), "lt": "vs", "fo": "s", "cut": (((0, 1), (1, 2)), ((0, 1), (1, 2))),
       "xs": (16, 0, 0, 0, 0, 0), "rs": (0, 0, 0, 0), "mb": "vv", "other": "pp",
       "mv": (("b4", "b5"), ("b3", "b2"), ("b4", "b5"), ("b4", "b5"), ("b4", "b5")),
       "wb": (("b6", "b4", "b5"), ("b6", "b1", "b0")), "seed": 1, "moves": 7000, "warm": 0.006, "aim": 0.3, "late": (0, 0, 0, 0)}
CYCLE = np.array([0.92, 0.83, 1.0, 1.16, 0.91, 1.0])
SCATTER = np.array([3.0, 2.5, 3.5, 6.4, 1.65, 3.0])
GATHER = np.array([1.4, 1.25, 1.56, 2.3, 1.0, 1.5])
WAKE = (0.11, 0.12, 0.07, 0.1, 0.15, 0.18)
HOPS = np.array([6.5, 6.6, 5.0, 5.2, 7.6, 9.0])
SHARE = (0.0, 2 / 52, 1 / 55, 1 / 77, 1 / 56, 1 / 64)
ORDER = []


EYE = (("id1", 1.0), ("idn", -1.0), ("idh", 0.5), ("idi", -0.5), ("idk", K / 2), ("idm", -2.0), ("idq", -4.0), ("idb", 33 / 128),
       ("idl", -K), ("idx", K), ("idj", C / 2), ("idu", -C / 2))
EYF = (("idf", 1.0), ("idg", -1.0))
ALIAS = {"z0": ("pool", LOS[1], H), "cmpb": ("pool", LOS[2], H)}
ALIAS.update({"lo%d" % o: ("pool", LOS[o], H) for o in range(3)})
ALIAS.update({e[0]: ("eye", 128 * k, 128) for k, e in enumerate(EYE)})
ALIAS.update({e[0]: ("eyf", 128 * k, 128) for k, e in enumerate(EYF)})


def _sb(n, d):
    return ("sbuf", [128, n], d)


SCRATCH = {
    "pool": _sb(UB[0] + 32 + 12 * H, B), "outp": _sb(V + H, B), "v1": _sb(6 * H, B), "chw": _sb(V, I), "rti": _sb(128, I),
    "mf": _sb(H, F), "y3": _sb(H, B), "kx": _sb(96, F), "gx": _sb(144, HF), "alp": _sb(96, F), "lp": _sb(96, F), "cm": _sb(96, B), "cp5": _sb(96, HF),
    "cf": _sb(96, B), "qs": _sb(64, B), "vq": _sb(64, HF), "dmi": _sb(96, F), "ri": _sb(128, F), "te": _sb(96, B),
    "uq": _sb(32, B), "er": _sb(128, B),
    "cmpa": _sb(H, B), "sg": _sb(2 * H, B), "lc": _sb(2 * H, B),
    "dw": _sb(2 * H, B), "ln": _sb(H, B), "kg": _sb(H, HF), "idw": _sb(128, HF),
    "z1": _sb(H, B), "w0": _sb(H, B), "w1": _sb(H, B),
    "eo": _sb(64, B), "ei": _sb(64, B), "fo": _sb(64, B), "fi": _sb(64, B),
    "he": _sb(32, B), "hf": _sb(32, B), "h0": _sb(H // 2, B), "h1": _sb(H // 2, B),
    "pc": _sb(4, I), "pf": _sb(8, F), "t1": _sb(144, F), "bc": _sb(144, B), "bd": _sb(144, B), "bo": _sb(3 * 144, HF),
    "rm": _sb(4, F), "eye": _sb(128 * len(EYE), B), "eyf": _sb(128 * len(EYF), F),
    "th": _sb(128, F), "wb": _sb(128, HF), "jc": _sb(32, F), "hi": _sb(128, F), "f16": _sb(4, U),
    "cl": _sb(128, B), "one": _sb(96, B), "c15": _sb(96, HF), "j2": _sb(32, HF), "csh": _sb(16, HF),
    "blk": _sb(128, B), "blki": _sb(128, B), "m2": _sb(256, B), "pp": _sb(256, HF),
    "ali": _sb(128, F), "al": _sb(128, F), "xp": _sb(96, F), "cvi": _sb(12, F), "lui": _sb(64, F), "lut": _sb(64, F),
    "r2": _sb(128, F), "rz": _sb(128, F), "r16": _sb(128, U), "e16": _sb(4, U), "ml16": _sb(96, U), "m16": _sb(64, U),
    "sd": _sb(96, B), "sm": _sb(96, B), "ng": _sb(96, B), "nh": _sb(32, B), "ce": _sb(96, HF), "u3": _sb(32, F),
    "ad": _sb(224, F), "ea": _sb(128, B), "eb": _sb(96, B), "bz": _sb(96, F), "nk0": _sb(128, B), "nk1": _sb(128, B),
    "mm": _sb(192, HF), "ic": _sb(128, B), "fp": _sb(128, F), "xi": _sb(96, HF), "ao": _sb(128, HF),
    "y0": _sb(32, F), "y1": _sb(32, F), "yc": _sb(32, HF), "ls": _sb(96, F), "ct": _sb(96, B), "u0": _sb(96, F), "u1": _sb(96, F), "cc": _sb(128, HF),
    "xt": _sb(96, F), "x16": _sb(96, U), "y16": _sb(96, U), "rv": _sb(128, F),
    "p16": _sb(128, U), "l16": _sb(192, U), "o16": _sb(64, U), "fx": _sb(96, B), "alt": _sb(96, F),
    "kw": _sb(96, F), "g16": _sb(144, HF), "sa": _sb(16, F), "s16": _sb(16, U), "si": _sb(16, I), "sj": _sb(16, I),
    "lt": _sb(8, B), "lu": _sb(8, B), "lf": _sb(24, F), "t16": _sb(2, U), "q16": _sb(16, U),
}
for _k in range(8):
    SCRATCH["b%d" % _k] = ("psum", [128, 512], F)
SEMAPHORES = ["cv", "cs", "cp", "cg", "lrec", "lrt", "lch", "lout", "sto", "stp", "ae", "a0", "af", "a1", "le", "l0", "lf", "l1"]
MSG = (("e", "eo", "he", "ei", 32), ("0", "z0", "h0", "w0", H // 2), ("f", "fo", "hf", "fi", 32), ("1", "z1", "h1", "w1", H // 2))
WIDTH = {F: 4, I: 4, B: 2, U: 2, HF: 2}


def helpers(src, dst, topo):
    ok = [c for c in topo.cores_of(src) if c != src and topo.may_write(c, dst)]
    near = [c for c in ok if topo.die(c) == topo.die(src)]
    far = [c for c in ok if topo.die(c) != topo.die(src)]
    return [near[0], far[0]]


def bits(engs):
    return sum(1 << e for e in engs)


def hand_on(g, core, T, topo, src, dst, k):
    rid, pid = topo.addr(dst, core)
    n_in = len(topo.engines(src, core)) // 2
    engs = topo.engines(core, dst)
    for tag, _, mid, land, wd in MSG:
        g.wait_ge(T.sem["a" + tag], n_in)
        g.remote_dma(T[land][:, k * wd:(k + 1) * wd], T[mid][:], T.sem["a" + tag], T.sem["l" + tag], pid, rid, bits(engs))
    for tag, _, mid, land, wd in MSG:
        g.wait_ge(T.sem["l" + tag], len(engs))


def rank_program(g, core, T, topo):
    cores = list(T.cores)
    nr = len(cores)
    rank = T.rank_of(core)
    if rank is None:
        for r in range(nr):
            hs = helpers(cores[r], cores[(r + 1) % nr], topo)
            if core in hs:
                hand_on(g, core, T, topo, cores[r], cores[(r + 1) % nr], hs.index(core))
        return
    nxt, prv = cores[(rank + 1) % nr], cores[(rank - 1) % nr]
    hs = helpers(core, nxt, topo)
    n_arr = [len(topo.engines(c, core)) for c in helpers(prv, core, topo)]
    Q = {"v": g.vector, "s": g.scalar, "p": g.tensor, "g": g, "y": g.sync}
    ops = []
    last = {}

    def A(name, a=0, b=None, step=None):
        if name in ALIAS:
            name, a, b = ALIAS[name][0], ALIAS[name][1] + a, ALIAS[name][1] + (ALIAS[name][2] if b is None else b)
        if b is None:
            b = SCRATCH[name][1][1]
        ap = T[name][:, a:b] if step is None else T[name][:, a:b:step]
        return (ap, [(name, a, b, step)], len(range(a, b, step or 1)), None)

    def X(name, a, b, off, c, d):
        return (T[name][:, a:b].indirect(T[off][:, c:d]), [(name, a, b, None)], 16 * (d - c), [(off, c, d, None)])

    def op(q, fn, rd, wr, busy, sem=None, cnt=0, done=None, after=()):
        r, w = [], []
        for o in rd:
            if isinstance(o, tuple):
                r += o[1] + (o[3] or [])
        for o in wr:
            w += o[1]
            r += o[3] or []
        ops.append((q, fn, r, w, sem, cnt, busy + 0 * CYCLE, (busy if done is None else done) + 0 * CYCLE, list(after)))

    def val(o):
        return o[0] if isinstance(o, tuple) else o

    def kind(o):
        return SCRATCH[o[1][0][0]]

    def lasts(out, a, b=None, fix=0.03):
        n = out[2]
        if out[3]:
            return 0.05 + SCATTER * n / 1000
        if a is not None and a[3]:
            return 0.06 + GATHER * n / 1000
        if b is not None:
            n *= 2 if kind(a)[0] == kind(b)[0] else 1
        elif fix < 0.05 and WIDTH[kind(out)[2]] == 2 and (a is None or WIDTH[kind(a)[2]] == 2):
            n /= 2
        return fix + max(64, n) * CYCLE / 1000

    def tt(out, a, b, alu):
        op("v", lambda: g.vector.tensor_tensor(out[0], a[0], b[0], alu), [a, b], [out], lasts(out, a, b))

    def ts(out, a, s1, o1, s2=None, o2=None):
        if o2 is None:
            op("v", lambda: g.vector.tensor_scalar(out[0], a[0], val(s1), None, o1), [a, s1], [out], lasts(out, a))
        else:
            op("v", lambda: g.vector.tensor_scalar(out[0], a[0], val(s1), val(s2), o1, o2), [a, s1, s2], [out], lasts(out, a))

    def cp(out, a):
        op("v", lambda: g.vector.tensor_copy(out[0], a[0]), [a], [out], lasts(out, a))

    def ms(out, c):
        op("v", lambda: g.vector.memset(out[0], c), [], [out], lasts(out, None))

    def act(out, a, f=ACT.Copy, bias=None, scale=None):
        kw = {}
        if bias is not None:
            kw["bias"] = val(bias)
        if scale is not None:
            kw["scale"] = val(scale)
        op("s", lambda: g.scalar.activation(out[0], a[0], f, **kw), [a, bias, scale], [out], lasts(out, a, None, 0.05))

    def fill(out, c):
        act(out, A("t1", 0, out[2]), ACT.Identity, c, 0.0)

    def run(calls):
        bank = calls[0][0][1][0][0]
        t = sum(max(64, c[2][2]) * (4 if kind(c[1])[2] == F else 1) for c in calls) * CYCLE / 2000

        def fn():
            return [g.tensor.matmul(o[0], l[0], r[0], st, sp) for o, l, r, st, sp in calls][-1]
        op("p", fn, [c[1] for c in calls] + [c[2] for c in calls], [c[0] for c in calls], t, after=[last[bank]] if bank in last else [])
        last[bank] = len(ops) - 1

    def mm(out, l, r, st=True, sp=True):
        run([(out, l, r, st, sp)])

    def lin(out, terms, st=True, sp=True):
        calls = [(out, A(l), r, st and k == 0, sp and k == len(terms) - 1) for k, (l, r) in enumerate(terms)]
        if out[2] < H:
            run(calls)
        else:
            for c in calls:
                run([c])

    def wrap(out, name, step, src):
        run([(out, A(name, step + 15 - i, step + 143 - i), A(src, i, H, 16), False, i == 15) for i in range(16)])

    def iota(out, pat, base, cm):
        t = 0.13 + out[2] / 500
        if kind(out)[2] == I:
            op("g", lambda: g.iota(out[0], pat, base, cm), [], [out], t)
        else:
            op("g", lambda: g.iota(out[0], pat, base, cm, allow_small_or_imprecise_dtypes=True), [], [out], t)

    def dma(q, pairs, rd, wr, sem, t):
        def fn():
            for o, i in pairs:
                Q[q].dma_start(o, i).then_inc(T.sem[sem], 16)
        op(q, fn, rd, wr, 0.05 * len(pairs), sem, 16 * len(pairs), t)

    def send(k):
        tag, src, mid, _, wd = MSG[k]
        tr, tot = [], 0
        for j, c in enumerate(hs):
            e = topo.engines(core, c)
            e = e[j::2]
            rid, pid = topo.addr(c, core)
            tr.append(RemoteDMATransfer(dst_ids=[DstId(rid=rid, pnc=pid)], dma_engine_mask=bits(e), remote_sem=T.sem["a" + tag],
                                        src=A(src, j * wd, (j + 1) * wd)[0], dst=T[mid][:]))
            tot += len(e)
        op("g", lambda: g.remote_dma_fused(tr, local_sem=T.sem["l" + tag]), [A(src)], [], 0.3, "l" + tag, tot, 2.0)
        op("x", None, [], [A(MSG[k][3])], 0.0, "a" + tag, sum(n_arr), HOPS + (1.8, 0.0, -0.9, 0.1)[k] + OPT["late"][k] * (np.array(SHARE) == 0), [len(ops) - 1])

    def blk(name, o, n=1):
        return A(name, 32 * o, 32 * (o + n))

    def big(name, o):
        return A(name, H * o, H * o + H)

    def pair(t, k, side=None, a=0, b=H):
        name, at = ("v1", 2 * H * (k - 3)) if t and k > 2 else ("pool", UB[t] + 32 + 2 * H * k)
        return (name, at, at + 2 * H) if side is None else A(name, at + side + 2 * a, at + 2 * b, 2)

    def root(t, o, a=0, b=H):
        return pair(t, max(o - 1, 0), min(o, 1), a, b)

    def first(t, o, a=0, b=H):
        return pair(t, 3 + o, 0, a, b)

    def second(t, o, a=0, b=H):
        return pair(t, 3 + o, 1, a, b)

    def pick(t, k, off, c, d):
        return X(*pair(t, k), off, c, d)

    def kept(o, off, c, d):
        return X("pool", UB[0], pair(0, 3 + max(o - 1, 0))[2], off, c, d)

    def given(off, c, d):
        return X("pool", P0 - 16, P0 + V, off, c, d)

    def count(out, cmp, signs, out16, flag, nk=None):
        c = (15 / 64 if nk is None else 63 / 128) + signs / 4
        lin(out, [("id1", A("j2"))] + ([] if nk is None else [("idb", nk)]), True, False)
        wrap(out, "bd" if signs else "bc", 0, cmp)
        ts(out16, out, c, ALU.add)
        tt(flag, out, blk("th", 2 * (nk is not None) + signs), ALU.is_ge)
        return c

    def signed(cmp, bank, terms, bias):
        lin(A(bank), terms)
        act(A(cmp), A(bank), ACT.Sign, bias)

    def duel(t, o, cmp):
        signs = o == 1 and OPT["duel1"][t] == "s"
        if signs:
            signed(cmp, "b3", [("id1", root(t, 0)), ("idn", root(t, 1))], -0.5)
        elif o == 1:
            tt(A(cmp), given("r16", 32, 64) if t == 0 else kept(1, "p16", 32, 64), root(t, 0), ALU.is_lt)
        else:
            act(pair(t, o - 1, 0), pick(t, o - 2, "ml16", 32 * o - 64, 32 * o - 32))
            tt(A(cmp), pick(t, o - 2, "ml16", 32 * o - 64, 32 * o - 32), root(t, o), ALU.is_gt)
        count(blk("b1", (15, 8, 0)[o - 1]), cmp, signs, blk("ml16", o - 1), blk("sd", o - 1))

    def third(t):
        (r, at), s1, s2, one = (("ad", 3), ("ao", 0))[t], blk("sd", 0), blk("sd", 1), blk("one", 0)
        lin(blk("b6", 0), [("idn", s1), ("idn", s2)])
        act(A("nh"), blk("b6", 0), ACT.Sign, 0.5)
        lin(blk("b6", 10), [("idh", one), ("idh", A("nh"))])
        lin(blk("b6", 11), [("idh", one), ("idn", s2), ("idi", A("nh"))])
        mm(blk("b6", 12), A("id1"), s2)
        tt(A("ce"), blk(r, at, 3), blk("b6", 10, 3), ALU.mult)
        late = [[], []]
        if t:
            tt(A("cf"), blk("ic", 0, 3), blk("b6", 10, 3), ALU.mult)
            lin(blk("b6", 14), [("id1", blk("ic", 3))] + [("idn", blk("cf", o)) for o in range(3)])
            lin(blk("b6", 15), [("id1", blk("cf", o)) for o in range(3)])
            act(A("qs"), blk("b6", 14, 2))
            for k in range(2):
                tt(blk("vq", k), blk("qs", k), blk("b7", 5), ALU.mult)
                late[k] = [("id1", blk("vq", k))]
        lin(blk("b6", 13), [(("idf", "id1")[t], blk(r, at + 3))] + [("idn", blk("ce", o)) for o in range(3)] + late[0])
        lin(blk("b0", 0), [("id1", blk("ce", o)) for o in range(3)] + late[1], True, False)
        if t:
            lin(blk("b6", 10, 3), [("id1", A("ct")), ("idi", blk("nk0", 0, 3))], True, False)
            run([(blk("b6", 10, 3 - p), A("id1"), blk("sm", p, 3 - p), False, False) for p in (1, 2)]
                + [(blk("b6", 10 + o), A("id1"), blk("qs", 1), False, o == 2) for o in range(3)])
            act(A("te"), blk("b6", 10, 3))

    def crowned(t):
        one = blk("one", 0)
        tt(A("u3"), blk("sd", 2), blk("b6", 13), ALU.mult)
        mm(blk("b0", 0), A("idf"), A("u3"), False, True)
        ts(blk("m16", t), blk("b0", 0), C, ALU.add)
        ts(A("kg"), X("chw", 0, V, "m16", 32 * t, 32 * t + 32), A("pf", 5, 6), ALU.subtract)
        act(blk("y%d" % t, 0), blk("b0", 0))
        run([(blk("b1", 1, 3 - j), A("idn"), blk("sd", j, 3 - j), j == 0, j == 2) for j in range(3)])
        act(A("ng"), blk("b1", 1, 3), ACT.Sign, 0.5)
        if t:
            tt(A("uq"), blk("sd", 2), blk("b6", 14), ALU.mult)
            lin(blk("b1", 12), [("idl", blk("te", 0)), ("idl", A("uq"))])
            run([(blk("b1", 13, 2), A("idx"), blk("te", 1, 2), True, False)] + [(blk("b1", 12 + o), A("idx"), A("uq"), False, o == 2) for o in (1, 2)])
            tt(blk("alp", 0), blk("b1", 12), blk("lp", 0), ALU.max)
            tt(blk("alp", 1, 2), blk("b1", 13, 2), blk("lp", 1, 2), ALU.min)
            act(blk("fx", 0), blk("b1", 12), ACT.Relu, 0.5, -1 / K)
            act(blk("fx", 1, 2), blk("b1", 13, 2), ACT.Relu, 0.5, 1 / K)
        run([(blk("b1", 4, 4), A("id1"), A("er"), True, False), (blk("b1", 4, 3), A("idi"), A("ng"), False, False),
             (blk("b1", 5, 3), A("idh"), A("ng"), False, False), (blk("b1", 4), A("idi"), one, False, False), (blk("b1", 7), A("idi"), one, False, True)])
        act(A("ea"), blk("b1", 4, 4), ACT.Relu)
        for o in range(3):
            out, w = blk(OPT["wb"][t][o], 8 + o), ("idk", "idl")[t]
            lin(out, [(w, one), (w, blk("ng", o))], True, False)
            wrap(out, "bo", 144 * o, "kg")
            if t:
                tt(blk("kw", o), out, blk("alp", o), ALU.max if o else ALU.min)
            else:
                act(blk("kw", o), out)
        if t:
            lin(blk("b1", 1, 3), [("idg", A("lp")), ("idn", A("cm")), ("idf", A("ls"))])
            tt(A("alt"), A("fx"), blk("b1", 1, 3), ALU.mult)
            lin(blk("b1", 12, 3), [("idf", A("kw")), ("idf", A("alt"))])
            act(A("kx"), blk("b1", 12, 3))

    def sendz(t):
        n = OPT["zs"][t]
        if n:
            cp(A("z%d" % t, 0, 16 * n), pick(t, 2, "ml16", 64, 64 + n))
        act(A("z%d" % t, 16 * n, H), pick(t, 2, "ml16", 64 + n, 96))
        send(1 + 2 * t)

    def shift(t):
        ei = ("ei", "fi")[t]
        for p, a in ((0, 0), (1, 3), (2, 5)):
            if OPT["lt"][t] == "v":
                ts(A("lt", a, a + 3 - p), A(ei, 16 * p + 16, 64, 16), A(ei, 16 * p, 16 * p + 1), ALU.is_lt)
            else:
                act(A("lu", a, a + 3 - p), A(ei, 16 * p + 16, 64, 16), ACT.Sign, A(ei, 16 * p, 16 * p + 1), -1.0)
        if OPT["lt"][t] == "s":
            act(A("lt", 0, 6), A("lu", 0, 6), ACT.Relu)
        mm(A("b3", 16, 32), A("id1"), A("csh"), True, False)
        run([(A("b3", 16 + 4 * k, 20 + 4 * k), A("blk"), A(ei, 0, 64, 16), False, k == 3) for k in range(4)])
        mm(A("b3", 0, 6), A("blk"), A("lt", 0, 6))
        ts(A("lf", 0, 6), A("b3", 0, 6), 8.5, ALU.is_ge)
        op("v", lambda: g.vector.tensor_tensor_scan(T.lf[:, 8:14], T.lf[:, 16:22], T.lf[:, 0:6], 0.0, ALU.mult, ALU.add),
           [A("lf", 16, 24), A("lf", 0, 6)], [A("lf", 8, 14)], 0.1)
        cp(A("t16", 0, 1), A("lf", 13, 14))
        cp(A("q16"), X("lut", 0, 64, "t16", 0, 1))
        cp(A("si"), A("b3", 16, 32))
        ts(A("sj", 0, 12), A("si", 0, 12), 4, ALU.logical_shift_right, 31, ALU.bitwise_and)
        ts(A("sj", 12, 16), A("si", 12, 16), 15, ALU.bitwise_and)
        cp(A("s16"), X("sj", 0, 16, "q16", 0, 1))
        cp(A("sa"), X("sj", 0, 16, "q16", 0, 1))
        ts(A("pp"), A("m2"), A("sa", 3, 4), ALU.add, A("pf", 3, 4), ALU.is_equal)
        for kw, g16, c, at in ((("kw", "g16", "cp5", 1), ("kx", "gx", "c15", 4)) if t else (("kw", "g16", "c15", 4),)):
            for o in range(3):
                cp(A(g16, 48 * o, 48 * o + 48), X(kw, 32 * o, 32 * o + 32, "s16", 0, 3))
                run([(blk("b6", at + o), A("id1"), blk(c, o), True, False)]
                    + [(blk("b6", at + o), A("pp", 128 * k, 128 * k + 128), A(g16, 48 * o + k, 48 * o + k + 32), False, k == 1) for k in range(2)])

    def structure(t):
        nk, one = "nk%d" % t, A("one")
        for o, n in OPT["cut"][t]:
            if t:
                tt(blk("xt", o, n), blk("b6", 1 + o, n), blk("al", o, n), ALU.max)
            else:
                tt(blk("xt", o, n), blk("b6", 4 + o, n), blk("xp", o, n), ALU.min)
            cp(blk("x16", o, n), blk("xt", o, n))
        for o in range(3):
            lo, hi = (0, P0 + V + H * o) if t else (P0, pair(0, 1)[2])
            n = OPT["xs"][3 * t + o]
            if n:
                cp(first(t, o, 0, 16 * n), X("pool", lo, hi, "x16", 32 * o, 32 * o + n))
            act(first(t, o, 16 * n, H), X("pool", lo, hi, "x16", 32 * o + n, 32 * o + 32))
        if t:
            act(A("eb"), blk("b6", 1, 3), ACT.Sign)
            act(A("bz"), blk("b6", 4, 3), ACT.Relu)
        else:
            act(A("eb"), blk("b6", 4, 3), ACT.Sign, K / 4, -1.0)
            act(A("bz"), blk("b6", 4, 3), ACT.Relu, K / 4, -1.0)
        mm(blk("b0", 1, 4), A("id1"), A("cl"), True, False)
        mm(blk("b0", 4), A("idk"), blk("ea", 3), False, False)
        for e, w in (("ea", ("idn", "idm", "idq")), ("eb", ("idi", "idn", "idm"))):
            run([(blk("b0", 1 + o), A(w[j]), blk(e, j), False, e == "eb" and o == 3 and j == 2)
                 for o in range(4) for j in range(min(o, 2) + 1)])
        act(A(nk), blk("b0", 1, 4), ACT.Sign)
        bk = ("b6", "b1")[t]
        lin(blk(bk, 8), [("idh", blk("one", 0)), ("idh", blk(nk, 0))])
        lin(blk(bk, 9, 2), [("idh", blk(nk, 1, 2)), ("idi", blk(nk, 0, 2))])
        lin(blk(bk, 11), [("idh", blk("one", 0)), ("idi", blk(nk, 3))])
        act(A("ic"), blk(bk, 8, 4))
        if t:
            run([(blk(bk, 12, 4), A("idx"), A("ea"), True, False), (blk(bk, 12, 3), A("idk"), blk(nk, 0, 3), False, False),
                 (blk(bk, 12, 3), A("idk"), A("eb"), False, False), (blk(bk, 12, 4), A("idf"), blk("ad", 3, 4), False, True)])
        else:
            lin(blk(bk, 12, 3), [("idh", blk(nk, 0, 3)), ("idh", A("eb")), ("id1", blk("ea", 0, 3))])
            mm(blk(bk, 15), A("id1"), blk("ea", 3))
            tt(A("fp"), A("al"), blk(bk, 12, 4), ALU.mult)
            lin(blk(bk, 8, 4), [("idk", A("ic")), ("idn", A("wb"))])
            tt(A("hi"), A("fp"), blk(bk, 8, 4), ALU.add)
        lin(blk("b7", 0, 3), [("idh", one), ("idh", blk(nk, 0, 3))])
        lin(blk("b7", 3, 3), [("idi", blk(nk, 0, 3)), ("idi", A("eb"))])
        tt(A("mm"), blk("ad", 0, 6), blk("b7", 0, 6), ALU.mult)
        w = ("idj", "idu")[t]
        lin(blk("b7", 0, 3), [(("idg", "idf")[t], A("bz")), (w, one), (w, A("eb"))], True, False)
        lin(blk("b7", 0, 3), [("id1", blk("mm", 0, 3)), ("id1", blk("mm", 3, 3))], False, True)
        cp(A("xi"), blk("b7", 0, 3))
        if t:
            act(A("fp"), blk(bk, 12, 4), ACT.Relu, C - K)
            return
        tt(A("ao"), blk("ad", 3, 4), blk(bk, 12, 4), ALU.mult)
        lin(blk(bk, 8, 3), [("idh", blk(nk, 0, 3)), ("idh", A("eb")), ("id1", blk("ea", 0, 3)), ("id1", blk("ic", 0, 3))])
        lin(blk(bk, 11), [("id1", blk("ea", 3)), ("id1", blk("ic", 3))])
        act(A("er"), blk(bk, 8, 4))

    def halve(t):
        z, w = A("z%d" % t), A("w%d" % t)
        lin(A("b2"), [("idw", z), ("idw", w)])
        if OPT["mb"][t] == "v":
            ts(second(t, 0), A("b2"), MAGIC, ALU.add, MAGIC, ALU.subtract)
        else:
            act(A("mf"), A("b2"), ACT.Identity, MAGIC)
            act(second(t, 0), A("mf"), ACT.Identity, -MAGIC)

    def link(t, o):
        y, u, nk = "y%d" % t, "u%d" % t, "nk%d" % t
        signs = OPT["cmp"][3 * t + o] == "s"
        if o:
            carry = pick(t, 2 + o, "y16", 32 * o - 32, 32 * o)
            act(second(t, o), carry)
            if signs:
                signed("cmpa", "b3", [("id1", first(t, o)), ("idn", second(t, o))], -0.5)
                if o == 2:
                    act(A("dw", 1, 2 * H, 2), A("b3"), ACT.Sign, None, -1.0)
            else:
                tt(A("cmpa"), carry, first(t, o), ALU.is_lt)
        elif signs:
            signed("cmpa", "b3", [("idi", A("z%d" % t)), ("idi", A("w%d" % t)), ("id1", first(t, 0))], -0.25)
        else:
            lin(A("b3"), [("idh", A("z%d" % t)), ("idh", A("w%d" % t))])
            tt(A("cmpa"), first(t, 0), A("b3"), ALU.is_gt)
        c = count(blk("b0", 5 + o), "cmpa", signs, blk("y16", o), blk("sm", o), blk(nk, o))
        if t == 0:
            newroot(o + 1, blk("b0", 5 + o), c)
        now = [("id1", blk("xi", o - 1)), ("idf", blk(u, o - 1))] if o else [("idf", blk(y, 0))]
        lin(blk("b7", 3), [("idn", blk("xi", o))] + now)
        tt(blk(u, o), blk("sm", o), blk("b7", 3), ALU.mult)
        if o == 2:
            lin(blk("b7", 5), [("id1", blk("xi", o)), ("idf", blk(u, o))])
        lin(blk("b7", 4), now + [("idg", blk(u, o))])
        ts(blk("l16", 3 * t + o), blk("b7", 4), C, ALU.add)
        if t == 0:
            act(blk("ls", o), blk("b7", 4))
        if o == 2:
            (act if t else cp)(A(("yc", "u3")[t]), blk("b7", 5))

    def newroot(o, place, c):
        tt(blk("rv", o), place, blk("hi", o), ALU.min)
        ts(blk("p16", o), blk("rv", o), pair(0, 3 + max(o - 1, 0))[1] - UB[0] + c, ALU.add)
        n = OPT["rs"][o]
        if n:
            cp(root(1, o, 0, 16 * n), kept(o, "p16", 32 * o, 32 * o + n))
        act(root(1, o, 16 * n, H), kept(o, "p16", 32 * o + n, 32 * o + 32))

    def numbers(t):
        if t:
            lin(blk("b1", 0, 4), [("idx", A("ic"))], True, False)
            run([(blk("b1", o), A("idf"), A("u3"), False, o == 3) for o in range(4)])
            act(A("hi"), blk("b1", 0, 4), ACT.Relu, C - K)
            lin(blk("b1", 4, 4), [("idf", A("fp")), ("idf", A("hi"))])
            act(A("r2"), blk("b1", 4, 4))
        else:
            run([(blk("b7", 6 + o), A("id1"), A("yc"), True, True) for o in range(4)])
            tt(A("cc"), A("ic"), blk("b7", 6, 4), ALU.mult)
            lin(blk("b7", 10, 4), [("id1", A("ao")), ("id1", A("cc"))])
            act(blk("ad", 3, 4), blk("b7", 10, 4))

    def put(t, lst, c, fn, spare):
        n = 32 // OPT["pieces"][4 * t + (1 + c // 32 % 3) * spare]
        for a in range(0, 32, n):
            fn(X("outp", 0, V + H * spare, lst, c + a, c + a + n), 16 * a, 16 * (a + n))

    def put_half(t):
        put(t, "m16", 32 * t, lambda dst, a, b: cp(dst, second(t, 0, a, b)), 0)

    def put_lost(o):
        put(0, "l16", 32 * o, lambda dst, a, b: cp(dst, A("lo%d" % o, a, b)), 1)

    def moved(t, o):
        x, y, w = first(t, o), second(t, o), second(t, o + 1) if o < 2 else A("y3")
        if o == 2:
            act(w, pick(t, 5, "y16", 64, 96))
        if t and OPT["other"][o] == "g":
            lin(blk("b7", 14 + o), [("id1", A("j2")), ("id1", blk("one", 0)), ("idn", blk("sm", o))])
            cp(blk("o16", o), blk("b7", 14 + o))
            act(big("lc", o), pick(t, 3 + o, "o16", 32 * o, 32 * o + 32))
            lin(A("b4"), [("id1", w), ("idn", big("lc", o))])
            act(big("sg", o), A("b4"), ACT.Sign)
        else:
            bd, bl = [A(b) for b in OPT["mv"][3 * t + o]]
            lin(bd, [("id1", x), ("id1", y), ("idm", w)])
            act(big("sg", o % 2), bd, ACT.Sign, None, -1.0)
            if t == 0:
                lin(bl, [("id1", x), ("id1", y), ("idn", w), ("id1", big("sg", o % 2))])
                act(A("lo%d" % o), bl)
                return put_lost(o)
            lin(bl, [("id1", x), ("id1", y), ("idn", w)])
            act(big("lc", o), bl)
        put(t, "l16", 32 * (3 * t + o), lambda dst, a, b: tt(dst, A("lc", H * o + a, H * o + b), A("sg", H * o + a, H * o + b), ALU.add), 1)

    def both(t):
        x, y = first(t, 2), second(t, 2)
        if OPT["cmp"][5] == "v":
            lin(A("b4"), [("idn", x), ("id1", y)])
            act(A("dw", 1, 2 * H, 2), A("b4"), ACT.Sign)
        lin(A("b5"), [("idn", x), ("id1", y), ("idn", A("dw", 1, 2 * H, 2))])
        act(A("dw", 0, 2 * H, 2), A("b5"))

    def chosen(t):
        act(A("ln"), X("dw", 0, 2 * H, "y16", 64, 96))
        put(t, "l16", 32 * (3 * t + 2), lambda dst, a, b: tt(dst, first(t, 2, a, b), A("ln", a, b), ALU.add), 1)

    dma("y", [(T.pool[:, P0:P0 + V], T.rec[:])], [], [A("pool", P0, P0 + V)], "lrec", 4.2)
    dma("s", [(T.rti[:], T.rt[:])], [], [A("rti")], "lrt", 1.5)
    iota(A("pc", 0, 1), [[0, 1]], 0, 1)
    iota(A("t1"), [[1, 144]], 0, 0)
    iota(A("ali", 32, 128), [[2 * H, 3], [32, 32]], 33, 0)
    iota(A("ali", 0, 32), [[32, 32]], 32, 0)
    iota(A("blki"), [[1, 8], [0, 16]], 0, 0)
    iota(A("cvi"), [[16, 3], [0, 4]], 0, 0)
    iota(A("m2"), [[-16, 2], [32, 8], [1, 16]], 0, 0)
    iota(A("dmi"), [[0, 3], [16, 32]], int(V - C), 0)
    iota(A("chw", 2560, V), [[0, 512]], 0, 0)
    for a in range(0, 1280, 640):
        ms(A("chw", a, a + 640), 0)
    ts(A("pc", 1, 2), A("pc", 0, 1), 15, ALU.bitwise_and)
    ts(A("pc", 2, 3), A("pc", 0, 1), 4, ALU.logical_shift_right)
    cp(A("pf", 0, 3), A("pc", 0, 3))
    ts(A("pf", 4, 5), A("pf", 2, 3), 16.0, ALU.mult, 15.0, ALU.add)
    ts(A("pf", 3, 4), A("pf", 2, 3), 32.0, ALU.mult, A("pf", 1, 2), ALU.add)
    ts(A("id1"), A("t1", 0, 128), A("pf", 0, 1), ALU.is_equal)
    ts(A("bc"), A("t1"), A("pf", 4, 5), ALU.is_equal, 1 / 32, ALU.mult)
    ts(A("pf", 6, 7), A("pf", 1, 2), 2.0, ALU.mult)
    ts(A("blk"), A("blki"), A("pf", 2, 3), ALU.is_equal)
    ts(A("rz"), A("rti"), 0.0, ALU.is_gt, 16.0, ALU.mult)
    tt(A("ri"), A("rz"), A("rti"), ALU.add)
    cp(A("r16"), A("ri"))
    cp(A("e16"), A("ri", 0, 128, 32))
    ts(blk("ad", 3, 4), A("rti"), C, ALU.subtract)
    ms(A("pool", P0 - 16, P0), 256.0)
    act(A("al"), A("ali"), ACT.Identity, A("pf", 6, 7))
    ts(A("j2"), blk("al", 0), 32.0, ALU.subtract)
    act(blk("th", 0), blk("al", 0), ACT.Identity, 0.5 - 15 / 64 - 32)
    for name, c in EYE[1:4] + EYF:
        act(A(name), A("id1"), ACT.Copy, None, c)
    fill(A("one"), 1.0)
    ts(A("rm", 0, 3), A("t1", 0, 3), A("pf", 1, 2), ALU.is_equal)
    for o in range(3):
        ts(A("bo", 144 * o, 144 * o + 144), A("t1"), A("pf", 4, 5), ALU.is_equal, A("rm", o, o + 1), ALU.mult)
    ts(A("pf", 5, 6), A("rm", 0, 1), MID[0] - MID[1], ALU.mult, MID[1], ALU.add)
    act(A("er"), A("ri"), ACT.Sign)
    for out, c in ((A("lf", 16, 24), 2), (blk("cm", 0), MID[0] - C), (blk("cm", 1, 2), MID[1] - C), (blk("cl", 0), 0), (blk("cl", 1), 1),
                   (blk("cl", 2, 2), 3), (A("pool", UB[0], UB[0] + 32), 256), (A("pool", 0, 32), 256)):
        fill(out, float(c))
    fill(A("lui"), 3.0)
    for a, b, st, c in ((0, 8, 1, 0.0), (16, 32, 2, 2.0), (32, 64, 8, 1.0), (33, 64, 8, 1.0), (36, 64, 8, 2.0), (38, 64, 8, 2.0)):
        fill(A("lui", a, b, st), c)
    ts(A("pf", 7, 8), A("pf", 1, 2), 3.0, ALU.min, 4.0, ALU.mult)
    act(A("lut"), A("lui"), ACT.Identity, A("pf", 7, 8))
    ts(A("idw"), A("id1"), 1023 / 2048, ALU.mult)
    ts(A("csh", 0, 12), A("cvi"), A("pf", 1, 2), ALU.add, 16.0, ALU.mult)
    ts(A("csh", 12, 16), A("t1", 0, 4), 0.0, ALU.mult)

    act(A("eo"), given("e16", 0, 4))
    early = len(ops) - 1
    send(0)
    sent = len(ops) - 2
    iota(A("chw", 1280, 2560), [[0, 1280]], 0, 0)
    ops[-1][8].append(sent)
    iota(A("ct"), [[1, 3], [0, 32]], -3, 0)
    ops[-1][8].append(len(ops) - 2)
    dma("y", [(T.chw[16 * k:16 * k + 3, :], T.ch[k]) for k in range(8)], [], [A("chw")], "lch", 2.5)
    cp(root(0, 0, 0, 320), given("r16", 0, 20))
    act(root(0, 0, 320, H), given("r16", 20, 32))
    ops[-1][8].append(early)
    for o in (1, 2, 3):
        act(root(0, o), given("r16", 32 * o, 32 * o + 32))
    duel(0, 1, "cmpa")
    duel(0, 2, "cmpb")
    third(0)
    duel(0, 3, "cmpa")
    sendz(0)
    ops[-2][3].append(("outp", 0, V, None))
    dma("y", [(T.outp[:, 0:V], T.rec[:])], [], [A("outp", 0, V)], "lout", 4.2)
    gate = len(ops) - 4
    for name, c in EYE[4:]:
        act(A(name), A("id1"), ACT.Copy, None, c)
    for k, c in ((1, 31 / 64), (2, 63 / 128), (3, 95 / 128)):
        act(blk("th", k), blk("al", 0), ACT.Identity, 0.5 - c - 32)
    act(A("jc"), blk("al", 0), ACT.Identity, -31.0)
    act(A("xp"), blk("al", 0, 3), ACT.Identity, float(UB[0] - P0))
    act(blk("ad", 0, 3), A("dmi"), ACT.Identity, A("pf", 1, 2))
    for o in range(3):
        act(blk("lp", o), blk("al", 0), ACT.Identity, LOS[o] - P0 - 16 - MID[o], 0.5)
    for o, n in ((0, 2), (2, 1), (3, 1)):
        ts(blk("wb", o, n), A("t1", 0, 32 * n), 0.0, ALU.mult, float(pair(0, 3 + max(o - 1, 0))[1] - UB[0]), ALU.add)
    ts(A("c15"), A("cm"), C, ALU.add)
    ts(A("cp5"), A("cm"), C + P0, ALU.add)
    if "s" in OPT["cmp"] + OPT["duel1"]:
        ts(A("bd"), A("bc"), 0.5, ALU.mult)
    for o in ops[gate + 4:]:
        o[8].append(gate)
    crowned(0)
    shift(0)
    structure(0)

    halve(0)
    newroot(0, A("jc"), 0.0)
    link(0, 0)
    link(0, 1)
    duel(1, 1, "cmpb")
    duel(1, 2, "cmpb")
    link(0, 2)
    cp(A("f16"), A("p16", 0, 128, 32))
    (cp if OPT["fo"] == "v" else act)(A("fo"), kept(3, "f16", 0, 4))
    send(2)
    duel(1, 3, "cmpb")
    sendz(1)
    third(1)
    numbers(0)
    crowned(1)
    put_half(0)
    moved(0, 0)
    moved(0, 1)
    moved(0, 2)

    shift(1)
    structure(1)
    halve(1)
    put_half(1)
    link(1, 0)
    link(1, 1)
    moved(1, 0)
    link(1, 2)
    moved(1, 1)
    both(1)
    chosen(1)
    numbers(1)
    dma("y", [(T.yrt[:], T.r2[:])], [A("r2")], [], "stp", 1.5)
    dma("y", [(T.yrec[:], T.outp[:, 0:V])], [A("outp", 0, V)], [], "sto", 3.7)
    ops[-1][8].append(len(ops) - 2)
    emit(g, T, Q, ops)


def arrange(ops, dep, psum):
    n, qs, speeds = len(ops), [o[0] for o in ops], range(len(WAKE))
    busy = [[float(o[6][m]) for o in ops] for m in speeds]
    done = [[float(o[7][m]) for o in ops] for m in speeds]
    before = [[[(j, done[m][j] + WAKE[m]) for j in sorted(dep[k])] + [(j, max(busy[m][j], 0.01)) for j in ops[k][8]]
               for k in range(n)] for m in speeds]

    ends = [k for k in range(n) if ops[k][4]]

    def lay(rank):
        for k in range(n):
            for j, _ in before[0][k]:
                if rank[j] >= rank[k]:
                    rank[k] = rank[j] + 1e-6
        at, used, wake = [0.0] * n, {}, WAKE[0]
        for k in sorted(range(n), key=lambda k: rank[k]):
            q, t = qs[k], 0.0
            for j, gap in before[0][k]:
                if at[j] + gap > t:
                    t = at[j] + gap
            if q != "x":
                spans = [x for x in used.get(q, [])[-40:] if x[1] > t]
                for bank in psum[k]:
                    spans += [(a - wake, b + wake, q2) for a, b, q2 in used.get(bank, [])[-20:] if q2 != q and b + wake > t]
                for a, b, _ in sorted(spans):
                    if a >= t + busy[0][k]:
                        break
                    t = max(t, b)
                for r in [q] + psum[k]:
                    used.setdefault(r, []).append((t, t + busy[0][k], q))
            at[k] = t
        return at

    def length(at, was=None):
        order, held, edges, parts = sorted(range(n), key=lambda k: (at[k], k)), {}, [None] * n, []
        for k in order:
            edges[k] = (held.get(qs[k]), [j for bank in psum[k] for q, j in held.setdefault(bank, {}).items() if q != qs[k]])
            if qs[k] != "x":
                held[qs[k]] = k
            for bank in psum[k]:
                held[bank][qs[k]] = k
        for m in speeds[1:]:
            now, bm, wake = [0.0] * n, busy[m], WAKE[m]
            for k in order:
                j, banks = edges[k]
                t = 0.0 if j is None else now[j] + bm[j]
                for j, gap in before[m][k]:
                    if now[j] + gap > t:
                        t = now[j] + gap
                for j in banks:
                    if now[j] + bm[j] + wake > t:
                        t = now[j] + bm[j] + wake
                now[k] = t
            parts.append(max(now[k] + done[m][k] for k in ends) * SHARE[m])
            if was and sum(parts) > sum(was[:m]) + 0.015:
                return None
            k = max(ends, key=lambda k: now[k] + done[m][k])
            while now[k] > 4:
                j = max(before[m][k], key=lambda e: now[e[0]] + e[1], default=None)
                if j is None or now[j[0]] + j[1] < now[k] - 1e-9:
                    j = (max([i for i in [edges[k][0]] + edges[k][1] if i is not None], key=lambda i: now[i] + bm[i]),)
                    held.setdefault("late", []).append((k, j[0]))
                k = j[0]
        return parts + [held.get("late", [])]

    best, wait = None, [0.0] * n
    for _ in range(8):
        rest = list(done[0])
        for k in range(n - 1, -1, -1):
            for j, gap in before[0][k]:
                rest[j] = max(rest[j], gap + wait[k] + rest[k])
        at = lay([-r for r in rest])
        parts = length(at)
        best = min(best or (1e9,), (sum(parts[:-1]), at, parts))
        for k in range(n):
            wait[k] += 0.3 * (at[k] - max([0.0] + [at[j] + gap for j, gap in before[0][k]]) - wait[k])
    draw, (now, at, was) = np.random.RandomState(OPT["seed"]), best
    for i in range(OPT["moves"]):
        rank = list(at)
        for _ in range(2):
            k, by = int(draw.randint(n)), float(draw.uniform(-1.5, 1.5))
            if draw.rand() < OPT["aim"]:
                k, j = was[-1][draw.randint(len(was[-1]))]
                by = at[j] - at[k] - 0.01 - float(draw.exponential(0.3))
                if draw.rand() < 0.5:
                    k, by = j, -by
            rank[k] += by
            while before[0][k] and by < 0 and draw.rand() < 0.6:
                k = max(before[0][k], key=lambda e: at[e[0]] + e[1])[0]
                rank[k] += by
        new = lay(rank)
        parts = length(new, was)
        if parts and sum(parts[:-1]) <= now + OPT["warm"] * (1 - i / OPT["moves"]) * draw.rand():
            now, at, was = sum(parts[:-1]), new, parts
            best = min(best, (now, at, was))
    return sorted(range(n), key=lambda k: (best[1][k], k)) + [[round(p / s, 2) for p, s in zip(best[2], SHARE[1:])]]


def emit(g, T, Q, ops):
    n = len(ops)
    psum = [sorted({x[0] for x in o[2] + o[3] if SCRATCH[x[0]][0] == "psum"}) for o in ops]
    seen, dep = {}, []
    for k, o in enumerate(ops):
        d = set()
        for regs, w in ((o[2], False), (o[3], True)):
            for name, a, b, st in regs:
                for a2, b2, st2, j, w2 in seen.get(name, []):
                    apart = st == 2 and st2 == 2 and (a - a2) % 2
                    if a < b2 and a2 < b and not apart and (w or w2) and not (o[0] == "p" and ops[j][0] == "p"):
                        d.add(j)
        dep.append(d)
        for regs, w in ((o[2], False), (o[3], True)):
            for name, a, b, st in regs:
                seen.setdefault(name, []).append((a, b, st, k, w))
    if not ORDER:
        ORDER.extend(arrange(ops, dep, psum))
    order = ORDER[:n]
    clock = {q: {} for q in Q}
    place = {k: i for i, k in enumerate(order)}
    done, waits, need, held = {}, {}, set(), {}
    for k in order:
        q, sem = ops[k][0], ops[k][4]
        want = {}
        for j in list(dep[k]) + [j for bank in psum[k] for q2, j in held.get(bank, {}).items() if q2 != q]:
            key = ops[j][4] or ops[j][0]
            want[key] = max(want.get(key, -1), place[j])
        waits[k] = []
        if q != "x":
            for key, i in sorted(want.items(), key=lambda e: -e[1]):
                if clock[q].get(key, -1) < i:
                    waits[k].append(order[i])
                    need.add(order[i])
                    for k2, i2 in done[order[i]].items():
                        clock[q][k2] = max(clock[q].get(k2, -1), i2)
        done[k] = dict(clock[q]) if q != "x" else {}
        done[k][sem or q] = place[k]
        for bank in psum[k]:
            held.setdefault(bank, {})[q] = k
    tick, cnt = {}, {}
    for k in order:
        q, sem = ops[k][0], ops[k][4]
        if sem is not None:
            tick[k] = (sem, ops[k][5])
        elif k in need:
            cnt[q] = cnt.get(q, 0) + 1
            tick[k] = ("c" + q, cnt[q])
    for k in order:
        q, fn, sem = ops[k][0], ops[k][1], ops[k][4]
        for j in waits[k]:
            Q[q].wait_ge(T.sem[tick[j][0]], tick[j][1])
        if fn is not None:
            ins = fn()
            if sem is None and k in need:
                ins.then_inc(T.sem["c" + q], 1)
    for k in order:
        if ops[k][4] is not None and k not in need:
            g.wait_ge(T.sem[ops[k][4]], ops[k][5])
